import numpy as np
import ml_dtypes


def mxq(x, axis, fmt="e4m3"):
    dtype, down = {"e4m3": (ml_dtypes.float8_e4m3fn, 7), "e5m2": (ml_dtypes.float8_e5m2, 14)}[fmt]
    v = np.moveaxis(np.asarray(x, np.float32).astype(ml_dtypes.bfloat16).astype(np.float64), axis, -1)
    blocks = v.reshape(v.shape[:-1] + (-1, 32))
    amax = np.abs(blocks).max(-1, keepdims=True)
    byte = np.maximum(np.where(amax > 0, np.frexp(amax)[1] - 1 + 127, 0) - down, 1)
    scale = np.exp2(byte - 127.0)
    codes = (blocks / scale).astype(np.float32).astype(dtype).astype(np.float64)
    return np.moveaxis((codes * scale).reshape(v.shape), -1, axis)


WIDE = False


def mx_kscale(k):
    if not WIDE:
        return np.ones(k)
    levels = np.array([10, -10, 5, -5, 0])
    if k % 512:
        return np.exp2(np.random.permutation(np.resize(levels, k // 32))).repeat(32)
    a = np.empty((k // 512, 16))
    for p in range(k // 512):
        a[p, :8] = np.random.permutation(np.resize(levels, 8))
        for g in range(8):
            far = levels[np.abs(levels - a[p, g]) >= 10]
            a[p, g + 8] = far[np.random.randint(len(far))]
    return np.exp2(a.ravel()).repeat(32)


BF16 = ml_dtypes.bfloat16


def bf(x):
    return np.asarray(x, np.float32).astype(BF16)


def f64(x):
    return np.asarray(x).astype(np.float64)


E2M1 = np.array([0.0, 0.5, 1.0, 1.5, 2.0, 3.0, 4.0, 6.0, -0.0, -0.5, -1.0, -1.5, -2.0, -3.0, -4.0, -6.0])


def pack_weight(w, fmt):
    k, n = w.shape
    w = f64(bf(w)).reshape(k // 32, 32, n)
    amax = np.abs(w).max(1)
    if fmt == "e4m3":
        byte = np.frexp(amax)[1] - 1 + 127 - 7
    else:
        mant, ex = np.frexp(amax / 6.0)
        byte = np.where(mant > 0.5, ex, ex - 1) + 127
    byte = np.clip(np.where(amax > 0, byte, 1), 1, 254)
    scaled = (w * np.exp2(127.0 - byte)[:, None, :]).reshape(k, n).astype(np.float32)
    by_word = np.ascontiguousarray(scaled.reshape(k // 512, 128, 4, n).transpose(0, 1, 3, 2))
    if fmt == "e4m3":
        words = by_word.astype(ml_dtypes.float8_e4m3fn).view(np.uint8)
    else:
        c = by_word.astype(ml_dtypes.float4_e2m1fn).view(np.uint8) & 0xF
        words = c[..., 0::2] | (c[..., 1::2] << 4)
    return np.ascontiguousarray(words), np.ascontiguousarray(byte.astype(np.uint8).reshape(k // 512, 16, n))


def unpack_weight(words, scales, fmt):
    g, p, n, _ = words.shape
    if fmt == "e4m3":
        vals = np.ascontiguousarray(words).view(ml_dtypes.float8_e4m3fn).astype(np.float64)
    else:
        nib = np.empty((g, p, n, 4), np.uint8)
        nib[..., 0::2] = words & 0xF
        nib[..., 1::2] = words >> 4
        vals = E2M1[nib]
    vals = vals * np.repeat(np.exp2(scales.astype(np.float64) - 127.0), 8, axis=1)[..., None]
    return vals.transpose(0, 1, 3, 2).reshape(g * 512, n)
def pack4(w):
    words, scales = pack_weight(w, "e2m1")
    return words.reshape(words.shape[0], 128, -1), scales


def unpack4(words, scales):
    return unpack_weight(words.reshape(words.shape[0], 128, -1, 2), scales, "e2m1")


M, K, F, R, J = 1024, 1024, 1536, 1024, 512


def setup_inputs():
    s = mx_kscale(K)
    t = mx_kscale(F)
    u = mx_kscale(J)
    boot = np.random.standard_normal((K, M)) * s[:, None]
    dev = np.random.standard_normal((K, F)) / np.sqrt(K) / s[:, None] * t
    boot_words, boot_scales = pack4(boot)
    dev_words, dev_scales = pack4(dev)
    return {"boot_words": boot_words, "boot_scales": boot_scales,
            "dev_words": dev_words, "dev_scales": dev_scales,
            "base": bf(0.5 * np.random.standard_normal(F) * t),
            "expo": bf(np.random.standard_normal((R, J)) * u),
            "sig": bf(np.random.standard_normal((J, F)) / np.sqrt(J) / u[:, None] / t),
            "rlen": bf((1 + 0.1 * np.random.standard_normal(M)) / np.sqrt(F))}


def reference(boot_words, boot_scales, dev_words, dev_scales, base, expo, sig, rlen):
    d = unpack4(boot_words, boot_scales).T @ unpack4(dev_words, dev_scales)
    c = np.maximum(d + f64(base), 0.0)
    p = mxq(f64(expo), 1, "e4m3") @ mxq(f64(sig), 0, "e4m3")
    y = mxq(c, 1, "e4m3") @ mxq(p, 1, "e4m3").T
    return y * f64(rlen)[:, None]

@@ -1,0 +1,315 @@
+from contextlib import ExitStack
+
+import concourse.mybir as mybir
+from concourse.masks import make_identity
+
+M, K, F, R, J = 1024, 1024, 1536, 1024, 512
+FLOPS = 2 * M * K * F + 2 * R * J * F + 2 * M * R * F
+
+F32 = mybir.dt.float32
+BF16 = mybir.dt.bfloat16
+I32 = mybir.dt.int32
+U32 = mybir.dt.uint32
+U8 = mybir.dt.uint8
+FP8X4 = mybir.dt.float8_e4m3fn_x4
+FP4X4 = mybir.dt.float4_e2m1fn_x4
+ACT = mybir.ActivationFunctionType
+ALU = mybir.AluOpType
+
+P = 128
+PACK = 4
+PASS = P * PACK
+BANK = 512
+KG = K // PASS
+FG = F // PASS
+RUN = 4
+
+
+def tile_bootstrap_signature_cosine_s12_kernel(
+    tc, boot_words, boot_scales, dev_words, dev_scales, base, expo, sig, rlen, out
+):
+    nc = tc.nc
+    with ExitStack() as ctx:
+        keep = ctx.enter_context(tc.tile_pool(name="keep", bufs=1))
+        ring = ctx.enter_context(tc.tile_pool(name="ring", bufs=2))
+        psum = ctx.enter_context(tc.psum_pool(name="psum", bufs=8))
+        ctx.enter_context(tc.manual_schedule())
+
+        dev_w_raw = keep.tile([P, KG, 2 * F], U8, name="dev_w_raw", align_bytes=64)
+        dev_s_raw = keep.tile([P, KG, F], U8, name="dev_s_raw", align_bytes=64)
+        dev_w = keep.tile([P, KG, 2 * F], U8, name="dev_w", align_bytes=64)
+        dev_s = keep.tile([P, KG, F], U8, name="dev_s", align_bytes=64)
+        boot_w = keep.tile([P, KG, 2 * M], U8, name="boot_w", align_bytes=64)
+        boot_s = keep.tile([P, KG, M], U8, name="boot_s", align_bytes=64)
+        base_raw = keep.tile([FG, PASS], BF16, name="base_raw", align_bytes=64)
+        base_rows = keep.tile([P, PACK, P], BF16, name="base_rows", align_bytes=64)
+        base_cols = keep.tile([P, PACK, FG], F32, name="base_cols", align_bytes=64)
+        rlen_rows = keep.tile([P, P], BF16, name="rlen_rows", align_bytes=64)
+        rlen_cols = keep.tile([P, M // P], F32, name="rlen_cols", align_bytes=64)
+        ident_bf = keep.tile([P, P], BF16, name="ident_bf", align_bytes=64)
+        ident_f32 = keep.tile([P, P], F32, name="ident_f32", align_bytes=64)
+        warm = keep.tile([P, 8], F32, name="warm", align_bytes=64)
+        sig_raw = keep.tile([P, FG, PACK, PASS], BF16, name="sig_raw", align_bytes=64)
+        sig_c = keep.tile([P, F], U32, name="sig_c", align_bytes=64)
+        sig_s = keep.tile([P, F], U8, name="sig_s", align_bytes=64)
+        expo_raw = keep.tile([P, R // P, J], BF16, name="expo_raw", align_bytes=64)
+        expo_t = keep.tile([P, R * PACK], BF16, name="expo_t", align_bytes=64)
+        expo_c = keep.tile([P, R], U32, name="expo_c", align_bytes=64)
+        expo_s = keep.tile([P, R], U8, name="expo_s", align_bytes=64)
+        cat_rows = keep.tile([P, 2, FG, PACK, BANK], BF16, name="cat_rows", align_bytes=64)
+        cat_c = keep.tile([P, FG, M], U32, name="cat_c", align_bytes=64)
+        cat_s = keep.tile([P, FG, M], U8, name="cat_s", align_bytes=64)
+        mix_in = keep.tile([P, FG, R * PACK], BF16, name="mix_in", align_bytes=64)
+        mix_c = keep.tile([P, FG, R], U32, name="mix_c", align_bytes=64)
+        mix_s = keep.tile([P, FG, R], U8, name="mix_s", align_bytes=64)
+
+        nc.gpsimd.memset(warm[:], 0.0)
+        nc.scalar.activation(out=warm[:, 4:5], in_=warm[:, 0:1], func=ACT.Relu)
+        nc.vector.memset(dev_s_raw[:].rearrange("p g n -> p (g n)").bitcast(I32), 0)
+        nc.vector.memset(boot_s[:].rearrange("p g n -> p (g n)").bitcast(I32), 0)
+        nc.vector.memset(base_rows[:], 0.0)
+        nc.vector.memset(rlen_rows[:], 0.0)
+
+        def load_words(eng, dst, src, lo, hi):
+            eng.dma_start(
+                out=dst[:, :, lo:hi].bitcast(I32),
+                in_=src.rearrange("g p n -> p g n")[:, :, lo:hi].bitcast(I32),
+            )
+
+        def load_scales(eng, dst, src):
+            by_row = src.rearrange("g (q r) n -> r q g n", r=4)
+            for r in range(4):
+                eng.dma_start(out=dst[r:P:32, :, :].bitcast(I32), in_=by_row[r].bitcast(I32))
+
+        load_words(nc.gpsimd, boot_w, boot_words, 0, 2 * BANK)
+        make_identity(nc, ident_bf[:])
+        make_identity(nc, ident_f32[:])
+        nc.sync.dma_start(out=base_raw[:], in_=base.rearrange("(g f) -> g f", f=PASS))
+        load_words(nc.sync, dev_w_raw, dev_words, 0, 2 * PASS)
+        load_scales(nc.sync, dev_s_raw, dev_scales)
+        load_scales(nc.sync, boot_s, boot_scales)
+        load_words(nc.sync, dev_w_raw, dev_words, 2 * PASS, 2 * F)
+        sig_view = sig.rearrange("(p j) (g f) -> p g j f", j=PACK, f=PASS)
+        expo_view = expo.rearrange("(i p) j -> p i j", p=P)
+        nc.sync.dma_start(out=sig_raw[:, 0], in_=sig_view[:, 0])
+        nc.sync.dma_start(out=sig_raw[:, 1], in_=sig_view[:, 1])
+        nc.sync.dma_start(out=expo_raw[:, 0:4], in_=expo_view[:, 0:4])
+        nc.sync.dma_start(out=sig_raw[:, 2], in_=sig_view[:, 2])
+        nc.sync.dma_start(out=rlen_rows[0 : M // P, :], in_=rlen.rearrange("(i p) -> i p", p=P))
+        nc.sync.dma_start(out=expo_raw[:, 4:8], in_=expo_view[:, 4:8])
+        load_words(nc.sync, boot_w, boot_words, 2 * BANK, 4 * BANK)
+
+        def order_dev(g):
+            w_cols = slice(g * 2 * PASS, (g + 1) * 2 * PASS)
+            s_cols = slice(g * PASS, (g + 1) * PASS)
+            nc.vector.tensor_copy(
+                out=dev_w[:, :, w_cols].bitcast(I32).rearrange("p k (t a w) -> p k t a w", t=PACK, w=2),
+                in_=dev_w_raw[:, :, w_cols].bitcast(I32).rearrange("p k (a t w) -> p k t a w", t=PACK, w=2),
+            )
+            nc.vector.tensor_copy(
+                out=dev_s[:, :, s_cols].bitcast(I32).rearrange("p k (t a) -> p k t a", t=PACK),
+                in_=dev_s_raw[:, :, s_cols].bitcast(I32).rearrange("p k (a t) -> p k t a", t=PACK),
+            )
+
+        def turn_base():
+            nc.vector.tensor_copy(
+                out=base_rows[0:FG].rearrange("g t (a i) -> g t a i", i=RUN),
+                in_=base_raw[:].rearrange("g (a t i) -> g t a i", t=PACK, i=RUN),
+            )
+            bank = psum.tile([P, PACK, P], BF16, name="base_bank", tag="bank")
+            for t in range(PACK):
+                nc.tensor.transpose(bank[:, t, :], base_rows[:, t, :], ident_bf[:])
+            nc.vector.tensor_copy(out=base_cols[:], in_=bank[:, :, 0:FG])
+
+        def turn_rlen():
+            bank = psum.tile([P, P], BF16, name="rlen_bank", tag="bank")
+            nc.tensor.transpose(bank[:], rlen_rows[:], ident_bf[:])
+            nc.vector.tensor_copy(out=rlen_cols[:], in_=bank[:, 0 : M // P])
+
+        def cat_bank(h, g, t, eng):
+            bank = psum.tile([P, BANK], F32, name="cat_bank", tag="bank")
+            col = g * PASS + t * P
+            for k in range(KG):
+                nc.tensor.matmul_mx(
+                    out=bank[:],
+                    lhsT=dev_w[:, k, 2 * col : 2 * (col + P)].bitcast(FP4X4),
+                    lhsT_scale=dev_s[:, k, col : col + P],
+                    rhs=boot_w[:, k, 2 * h * BANK : 2 * (h + 1) * BANK].bitcast(FP4X4),
+                    rhs_scale=boot_s[:, k, h * BANK : (h + 1) * BANK],
+                    start=(k == 0),
+                    stop=(k == KG - 1),
+                )
+            bias = base_cols[:, t, g : g + 1]
+            if eng == "S":
+                nc.scalar.activation(out=cat_rows[:, h, g, t, :], in_=bank[:], func=ACT.Relu, bias=bias)
+            else:
+                nc.vector.tensor_scalar(
+                    out=cat_rows[:, h, g, t, :], in0=bank[:], scalar1=bias, scalar2=0.0, op0=ALU.add, op1=ALU.max
+                )
+
+        staged = {}
+
+        def cat_weave(h, g):
+            woven = ring.tile([P, BANK * PACK], BF16, name="woven", tag="woven", bufs=3, align_bytes=64)
+            nc.vector.tensor_copy(
+                out=woven[:].rearrange("p (c i t) -> p c t i", i=RUN, t=PACK),
+                in_=cat_rows[:, h, g].rearrange("p t (c i) -> p c t i", i=RUN),
+            )
+            staged[("cat", h, g)] = woven
+
+        def cat_quant(h, g):
+            n = slice(h * BANK, (h + 1) * BANK)
+            nc.vector.quantize_mx(out=cat_c[:, g, n].bitcast(FP8X4), scales=cat_s[:, g, n], in_=staged[("cat", h, g)][:])
+
+        def sig_weave(g):
+            woven = ring.tile([P, BANK * PACK], BF16, name="woven", tag="woven", bufs=3, align_bytes=64)
+            nc.vector.tensor_copy(
+                out=woven[:].rearrange("p (t a i j) -> p t a j i", t=PACK, i=RUN, j=PACK),
+                in_=sig_raw[:, g].rearrange("p j (a t i) -> p t a j i", t=PACK, i=RUN),
+            )
+            staged[("sig", g)] = woven
+
+        def sig_quant(g):
+            n = slice(g * PASS, (g + 1) * PASS)
+            nc.vector.quantize_mx(out=sig_c[:, n].bitcast(FP8X4), scales=sig_s[:, n], in_=staged[("sig", g)][:])
+
+        def expo_bank(b, eng):
+            bank = psum.tile([P, 2, 2, P], F32, name="expo_bank", tag="bank")
+            for i in range(2):
+                words = expo_raw[:, 2 * b + i, :].bitcast(F32)
+                for u in range(2):
+                    nc.tensor.transpose(bank[:, i, u, :], words[:, u : J // 2 : 2], ident_f32[:])
+            dst = expo_t[:, b * 2 * PASS : (b + 1) * 2 * PASS].bitcast(F32).rearrange("p (i r u) -> p i r u", i=2, u=2)
+            src = bank[:].rearrange("p i u r -> p i r u")
+            if eng == "S":
+                nc.scalar.copy(out=dst, in_=src)
+            else:
+                nc.vector.tensor_copy(out=dst, in_=src)
+
+        def expo_quant(h):
+            n = slice(h * BANK, (h + 1) * BANK)
+            nc.vector.quantize_mx(
+                out=expo_c[:, n].bitcast(FP8X4), scales=expo_s[:, n], in_=expo_t[:, h * BANK * PACK : (h + 1) * BANK * PACK]
+            )
+
+        def mix_bank(g, i, eng):
+            bank = psum.tile([P, PACK, P], F32, name="mix_bank", tag="bank")
+            n = slice(i * P, (i + 1) * P)
+            for t in range(PACK):
+                c = slice(g * PASS + t * P, g * PASS + (t + 1) * P)
+                nc.tensor.matmul_mx(
+                    out=bank[:, t, :],
+                    lhsT=sig_c[:, c].bitcast(FP8X4),
+                    lhsT_scale=sig_s[:, c],
+                    rhs=expo_c[:, n].bitcast(FP8X4),
+                    rhs_scale=expo_s[:, n],
+                    start=True,
+                    stop=True,
+                )
+            dst = mix_in[:, g, i * PASS : (i + 1) * PASS].rearrange("p (r t) -> p r t", t=PACK)
+            src = bank[:].rearrange("p t r -> p r t")
+            if eng == "S":
+                nc.scalar.copy(out=dst, in_=src)
+            else:
+                nc.vector.tensor_copy(out=dst, in_=src)
+
+        def mix_quant(g, h):
+            n = slice(h * BANK, (h + 1) * BANK)
+            nc.vector.quantize_mx(
+                out=mix_c[:, g, n].bitcast(FP8X4),
+                scales=mix_s[:, g, n],
+                in_=mix_in[:, g, h * BANK * PACK : (h + 1) * BANK * PACK],
+            )
+
+        def out_bank(i, h, eng):
+            bank = psum.tile([P, BANK], F32, name="out_bank", tag="bank")
+            m = slice(i * P, (i + 1) * P)
+            n = slice(h * BANK, (h + 1) * BANK)
+            for g in range(FG):
+                nc.tensor.matmul_mx(
+                    out=bank[:],
+                    lhsT=cat_c[:, g, m].bitcast(FP8X4),
+                    lhsT_scale=cat_s[:, g, m],
+                    rhs=mix_c[:, g, n].bitcast(FP8X4),
+                    rhs_scale=mix_s[:, g, n],
+                    start=(g == 0),
+                    stop=(g == FG - 1),
+                )
+            result = ring.tile([P, BANK], F32, name="result", tag="result", bufs=8)
+            factor = rlen_cols[:, i : i + 1]
+            if eng == "S":
+                nc.scalar.activation(out=result[:], in_=bank[:], func=ACT.Copy, scale=factor)
+            else:
+                nc.vector.tensor_scalar(out=result[:], in0=bank[:], scalar1=factor, scalar2=None, op0=ALU.mult)
+            nc.sync.dma_start(out=out[m, n], in_=result[:])
+
+        turn_base()
+        order_dev(0)
+        order_dev(1)
+        order_dev(2)
+        for g in range(FG):
+            for t in range(PACK):
+                cat_bank(0, g, t, "S")
+        sig_weave(0)
+        sig_weave(1)
+        sig_quant(0)
+        cat_weave(0, 0)
+        sig_quant(1)
+        sig_weave(2)
+        cat_quant(0, 0)
+        turn_rlen()
+        expo_bank(0, "S")
+        expo_bank(1, "S")
+        cat_weave(0, 1)
+        sig_quant(2)
+        expo_bank(2, "V")
+        expo_bank(3, "S")
+        expo_quant(0)
+        cat_weave(0, 2)
+        cat_quant(0, 1)
+        for t in range(PACK):
+            cat_bank(1, 0, t, "S")
+        for i in range(4):
+            mix_bank(0, i, "V")
+            if i == 0:
+                cat_quant(0, 2)
+        for t in range(PACK):
+            cat_bank(1, 1, t, "S")
+        for i in range(4):
+            mix_bank(1, i, "V")
+            if i == 0:
+                mix_quant(0, 0)
+        expo_quant(1)
+        for t in range(PACK):
+            cat_bank(1, 2, t, "S")
+        for i in range(4):
+            mix_bank(2, i, "VSVS"[i])
+            if i == 0:
+                mix_quant(1, 0)
+        mix_bank(0, 4, "S")
+        mix_quant(2, 0)
+        for i in range(1, 4):
+            mix_bank(0, 4 + i, "S")
+        cat_weave(1, 0)
+        for i in range(4):
+            mix_bank(1, 4 + i, "S")
+        out_bank(0, 0, "S")
+        cat_weave(1, 1)
+        cat_quant(1, 0)
+        out_bank(1, 0, "S")
+        cat_weave(1, 2)
+        cat_quant(1, 1)
+        out_bank(2, 0, "S")
+        cat_quant(1, 2)
+        mix_quant(0, 1)
+        out_bank(3, 0, "V")
+        for i in range(4):
+            mix_bank(2, 4 + i, "SV"[i % 2])
+            if i == 1:
+                mix_quant(1, 1)
+        out_bank(4, 0, "S")
+        mix_quant(2, 1)
+        for i in range(5, 8):
+            out_bank(i, 0, "VS"[i % 2])
+        for i in range(8):
+            out_bank(i, 1, "VS"[i % 2])

@@ -35,11 +35,11 @@ def tile_bootstrap_signature_cosine_s12_kernel(
         psum = ctx.enter_context(tc.psum_pool(name="psum", bufs=8))
         ctx.enter_context(tc.manual_schedule())
 
-        dev_w_raw = keep.tile([P, KG, 2 * F], U8, name="dev_w_raw", align_bytes=64)
+        dev_w_raw = keep.tile([P, FG, KG, 2 * PASS], U8, name="dev_w_raw", align_bytes=64)
         dev_s_raw = keep.tile([P, KG, F], U8, name="dev_s_raw", align_bytes=64)
-        dev_w = keep.tile([P, KG, 2 * F], U8, name="dev_w", align_bytes=64)
-        dev_s = keep.tile([P, KG, F], U8, name="dev_s", align_bytes=64)
-        boot_w = keep.tile([P, KG, 2 * M], U8, name="boot_w", align_bytes=64)
+        dev_w = keep.tile([P, FG, KG, 2 * PASS], U8, name="dev_w", align_bytes=64)
+        dev_s = keep.tile([P, FG, KG, PASS], U8, name="dev_s", align_bytes=64)
+        boot_w = keep.tile([P, 2, KG, 2 * BANK], U8, name="boot_w", align_bytes=64)
         boot_s = keep.tile([P, KG, M], U8, name="boot_s", align_bytes=64)
         base_raw = keep.tile([FG, PASS], BF16, name="base_raw", align_bytes=64)
         base_rows = keep.tile([P, PACK, P], BF16, name="base_rows", align_bytes=64)
@@ -63,52 +63,54 @@ def tile_bootstrap_signature_cosine_s12_kernel(
         mix_c = keep.tile([P, FG, R], U32, name="mix_c", align_bytes=64)
         mix_s = keep.tile([P, FG, R], U8, name="mix_s", align_bytes=64)
 
-        nc.gpsimd.memset(warm[:], 0.0)
-        nc.scalar.activation(out=warm[:, 4:5], in_=warm[:, 0:1], func=ACT.Relu)
-        nc.vector.memset(dev_s_raw[:].rearrange("p g n -> p (g n)").bitcast(I32), 0)
-        nc.vector.memset(boot_s[:].rearrange("p g n -> p (g n)").bitcast(I32), 0)
-        nc.vector.memset(base_rows[:], 0.0)
-        nc.vector.memset(rlen_rows[:], 0.0)
+        staged = {}
 
-        def load_words(eng, dst, src, lo, hi):
-            eng.dma_start(
-                out=dst[:, :, lo:hi].bitcast(I32),
-                in_=src.rearrange("g p n -> p g n")[:, :, lo:hi].bitcast(I32),
+        def load_words(dst, src, part):
+            nc.sync.dma_start(
+                out=dst[:, part].bitcast(I32),
+                in_=src.rearrange("k p (c n) -> p c k n", n=2 * BANK)[:, part].bitcast(I32),
             )
 
-        def load_scales(eng, dst, src):
-            by_row = src.rearrange("g (q r) n -> r q g n", r=4)
-            for r in range(4):
-                eng.dma_start(out=dst[r:P:32, :, :].bitcast(I32), in_=by_row[r].bitcast(I32))
+        def load_scales(dst, src):
+            by_quadrant = src.rearrange("g (q r) n -> q r g n", r=4)
+            for q in range(4):
+                nc.sync.dma_start(out=dst[32 * q : 32 * q + 4, :, :].bitcast(I32), in_=by_quadrant[q].bitcast(I32))
 
-        load_words(nc.gpsimd, boot_w, boot_words, 0, 2 * BANK)
+        nc.gpsimd.memset(dev_s_raw[:].rearrange("p g n -> p (g n)").bitcast(I32), 0)
+        nc.vector.memset(boot_s[:].rearrange("p g n -> p (g n)").bitcast(I32), 0)
+        nc.vector.memset(warm[:], 0.0)
+        nc.scalar.dma_start(out=base_raw[:], in_=base.rearrange("(g f) -> g f", f=PASS))
+        nc.scalar.activation(out=warm[:, 4:5], in_=warm[:, 0:1], func=ACT.Relu)
+        nc.vector.memset(base_rows[:], 0.0)
+        nc.vector.memset(rlen_rows[:], 0.0)
         make_identity(nc, ident_bf[:])
         make_identity(nc, ident_f32[:])
-        nc.sync.dma_start(out=base_raw[:], in_=base.rearrange("(g f) -> g f", f=PASS))
-        load_words(nc.sync, dev_w_raw, dev_words, 0, 2 * PASS)
-        load_scales(nc.sync, dev_s_raw, dev_scales)
-        load_scales(nc.sync, boot_s, boot_scales)
-        load_words(nc.sync, dev_w_raw, dev_words, 2 * PASS, 2 * F)
+        load_words(dev_w_raw, dev_words, 0)
+        load_scales(dev_s_raw, dev_scales)
+        load_words(boot_w, boot_words, 0)
+        load_scales(boot_s, boot_scales)
+        load_words(dev_w_raw, dev_words, 1)
         sig_view = sig.rearrange("(p j) (g f) -> p g j f", j=PACK, f=PASS)
         expo_view = expo.rearrange("(i p) j -> p i j", p=P)
         nc.sync.dma_start(out=sig_raw[:, 0], in_=sig_view[:, 0])
+        load_words(dev_w_raw, dev_words, 2)
         nc.sync.dma_start(out=sig_raw[:, 1], in_=sig_view[:, 1])
         nc.sync.dma_start(out=expo_raw[:, 0:4], in_=expo_view[:, 0:4])
         nc.sync.dma_start(out=sig_raw[:, 2], in_=sig_view[:, 2])
-        nc.sync.dma_start(out=rlen_rows[0 : M // P, :], in_=rlen.rearrange("(i p) -> i p", p=P))
         nc.sync.dma_start(out=expo_raw[:, 4:8], in_=expo_view[:, 4:8])
-        load_words(nc.sync, boot_w, boot_words, 2 * BANK, 4 * BANK)
+        nc.sync.dma_start(out=rlen_rows[0 : M // P, :], in_=rlen.rearrange("(i p) -> i p", p=P))
+        load_words(boot_w, boot_words, 1)
 
         def order_dev(g):
-            w_cols = slice(g * 2 * PASS, (g + 1) * 2 * PASS)
-            s_cols = slice(g * PASS, (g + 1) * PASS)
             nc.vector.tensor_copy(
-                out=dev_w[:, :, w_cols].bitcast(I32).rearrange("p k (t a w) -> p k t a w", t=PACK, w=2),
-                in_=dev_w_raw[:, :, w_cols].bitcast(I32).rearrange("p k (a t w) -> p k t a w", t=PACK, w=2),
+                out=dev_w[:, g].bitcast(I32).rearrange("p k (t a w) -> p k t a w", t=PACK, w=2),
+                in_=dev_w_raw[:, g].bitcast(I32).rearrange("p k (a t w) -> p k t a w", t=PACK, w=2),
             )
+
+        def order_dev_scales():
             nc.vector.tensor_copy(
-                out=dev_s[:, :, s_cols].bitcast(I32).rearrange("p k (t a) -> p k t a", t=PACK),
-                in_=dev_s_raw[:, :, s_cols].bitcast(I32).rearrange("p k (a t) -> p k t a", t=PACK),
+                out=dev_s[:].bitcast(I32).rearrange("p g k (t a) -> p g k t a", t=PACK),
+                in_=dev_s_raw[:].bitcast(I32).rearrange("p k (g a t) -> p g k t a", g=FG, t=PACK),
             )
 
         def turn_base():
@@ -119,7 +121,23 @@ def tile_bootstrap_signature_cosine_s12_kernel(
             bank = psum.tile([P, PACK, P], BF16, name="base_bank", tag="bank")
             for t in range(PACK):
                 nc.tensor.transpose(bank[:, t, :], base_rows[:, t, :], ident_bf[:])
-            nc.vector.tensor_copy(out=base_cols[:], in_=bank[:, :, 0:FG])
+            staged["base"] = bank
+
+        def fetch_base():
+            nc.vector.tensor_copy(out=base_cols[:], in_=staged["base"][:, :, 0:FG])
+
+        def warm_up(passes):
+            bank = psum.tile([P, BANK], F32, name="warm_bank", tag="bank")
+            for i in range(passes):
+                nc.tensor.matmul_mx(
+                    out=bank[:],
+                    lhsT=dev_w_raw[:, 0, 0, 0 : 2 * P].bitcast(FP4X4),
+                    lhsT_scale=dev_s_raw[:, 0, 0:P],
+                    rhs=dev_w_raw[:, 0, 0, :].bitcast(FP4X4),
+                    rhs_scale=dev_s_raw[:, 0, 0:BANK],
+                    start=True,
+                    stop=True,
+                )
 
         def turn_rlen():
             bank = psum.tile([P, P], BF16, name="rlen_bank", tag="bank")
@@ -128,13 +146,13 @@ def tile_bootstrap_signature_cosine_s12_kernel(
 
         def cat_bank(h, g, t, eng):
             bank = psum.tile([P, BANK], F32, name="cat_bank", tag="bank")
-            col = g * PASS + t * P
+            col = t * P
             for k in range(KG):
                 nc.tensor.matmul_mx(
                     out=bank[:],
-                    lhsT=dev_w[:, k, 2 * col : 2 * (col + P)].bitcast(FP4X4),
-                    lhsT_scale=dev_s[:, k, col : col + P],
-                    rhs=boot_w[:, k, 2 * h * BANK : 2 * (h + 1) * BANK].bitcast(FP4X4),
+                    lhsT=dev_w[:, g, k, 2 * col : 2 * (col + P)].bitcast(FP4X4),
+                    lhsT_scale=dev_s[:, g, k, col : col + P],
+                    rhs=boot_w[:, h, k, :].bitcast(FP4X4),
                     rhs_scale=boot_s[:, k, h * BANK : (h + 1) * BANK],
                     start=(k == 0),
                     stop=(k == KG - 1),
@@ -146,8 +164,6 @@ def tile_bootstrap_signature_cosine_s12_kernel(
                 nc.vector.tensor_scalar(
                     out=cat_rows[:, h, g, t, :], in0=bank[:], scalar1=bias, scalar2=0.0, op0=ALU.add, op1=ALU.max
                 )
-
-        staged = {}
 
         def cat_weave(h, g):
             woven = ring.tile([P, BANK * PACK], BF16, name="woven", tag="woven", bufs=3, align_bytes=64)
@@ -221,10 +237,10 @@ def tile_bootstrap_signature_cosine_s12_kernel(
                 in_=mix_in[:, g, h * BANK * PACK : (h + 1) * BANK * PACK],
             )
 
-        def out_bank(i, h, eng):
-            bank = psum.tile([P, BANK], F32, name="out_bank", tag="bank")
+        def out_bank(i, h, eng, lo=0, width=BANK):
+            bank = psum.tile([P, width], F32, name="out_bank", tag="bank")
             m = slice(i * P, (i + 1) * P)
-            n = slice(h * BANK, (h + 1) * BANK)
+            n = slice(h * BANK + lo, h * BANK + lo + width)
             for g in range(FG):
                 nc.tensor.matmul_mx(
                     out=bank[:],
@@ -235,7 +251,7 @@ def tile_bootstrap_signature_cosine_s12_kernel(
                     start=(g == 0),
                     stop=(g == FG - 1),
                 )
-            result = ring.tile([P, BANK], F32, name="result", tag="result", bufs=8)
+            result = ring.tile([P, width], F32, name="result", tag="result", bufs=8)
             factor = rlen_cols[:, i : i + 1]
             if eng == "S":
                 nc.scalar.activation(out=result[:], in_=bank[:], func=ACT.Copy, scale=factor)
@@ -245,14 +261,17 @@ def tile_bootstrap_signature_cosine_s12_kernel(
 
         turn_base()
         order_dev(0)
+        order_dev_scales()
+        fetch_base()
+        warm_up(3)
         order_dev(1)
+        sig_weave(0)
         order_dev(2)
         for g in range(FG):
             for t in range(PACK):
                 cat_bank(0, g, t, "S")
-        sig_weave(0)
-        sig_weave(1)
         sig_quant(0)
+        sig_weave(1)
         cat_weave(0, 0)
         sig_quant(1)
         sig_weave(2)
@@ -270,13 +289,13 @@ def tile_bootstrap_signature_cosine_s12_kernel(
         for t in range(PACK):
             cat_bank(1, 0, t, "S")
         for i in range(4):
-            mix_bank(0, i, "V")
+            mix_bank(0, i, "VVVS"[i])
             if i == 0:
                 cat_quant(0, 2)
         for t in range(PACK):
             cat_bank(1, 1, t, "S")
         for i in range(4):
-            mix_bank(1, i, "V")
+            mix_bank(1, i, "VVVS"[i])
             if i == 0:
                 mix_quant(0, 0)
         expo_quant(1)
@@ -302,7 +321,7 @@ def tile_bootstrap_signature_cosine_s12_kernel(
         out_bank(2, 0, "S")
         cat_quant(1, 2)
         mix_quant(0, 1)
-        out_bank(3, 0, "V")
+        out_bank(3, 0, "S")
         for i in range(4):
             mix_bank(2, 4 + i, "SV"[i % 2])
             if i == 1:
@@ -311,5 +330,7 @@ def tile_bootstrap_signature_cosine_s12_kernel(
         mix_quant(2, 1)
         for i in range(5, 8):
             out_bank(i, 0, "VS"[i % 2])
-        for i in range(8):
+        for i in range(7):
             out_bank(i, 1, "VS"[i % 2])
+        out_bank(7, 1, "S", 0, 256)
+        out_bank(7, 1, "V", 256, 256)

@@ -35,7 +35,7 @@ def tile_bootstrap_signature_cosine_s12_kernel(
         psum = ctx.enter_context(tc.psum_pool(name="psum", bufs=8))
         ctx.enter_context(tc.manual_schedule())
 
-        dev_w_raw = keep.tile([P, FG, KG, 2 * PASS], U8, name="dev_w_raw", align_bytes=64)
+        dev_w_raw = keep.tile([P, KG, 2 * F], U8, name="dev_w_raw", align_bytes=64)
         dev_s_raw = keep.tile([P, KG, F], U8, name="dev_s_raw", align_bytes=64)
         dev_w = keep.tile([P, FG, KG, 2 * PASS], U8, name="dev_w", align_bytes=64)
         dev_s = keep.tile([P, FG, KG, PASS], U8, name="dev_s", align_bytes=64)
@@ -85,15 +85,13 @@ def tile_bootstrap_signature_cosine_s12_kernel(
         nc.vector.memset(rlen_rows[:], 0.0)
         make_identity(nc, ident_bf[:])
         make_identity(nc, ident_f32[:])
-        load_words(dev_w_raw, dev_words, 0)
-        load_scales(dev_s_raw, dev_scales)
         load_words(boot_w, boot_words, 0)
+        load_scales(dev_s_raw, dev_scales)
+        nc.sync.dma_start(out=dev_w_raw[:].bitcast(I32), in_=dev_words.rearrange("k p n -> p k n").bitcast(I32))
         load_scales(boot_s, boot_scales)
-        load_words(dev_w_raw, dev_words, 1)
         sig_view = sig.rearrange("(p j) (g f) -> p g j f", j=PACK, f=PASS)
         expo_view = expo.rearrange("(i p) j -> p i j", p=P)
         nc.sync.dma_start(out=sig_raw[:, 0], in_=sig_view[:, 0])
-        load_words(dev_w_raw, dev_words, 2)
         nc.sync.dma_start(out=sig_raw[:, 1], in_=sig_view[:, 1])
         nc.sync.dma_start(out=expo_raw[:, 0:4], in_=expo_view[:, 0:4])
         nc.sync.dma_start(out=sig_raw[:, 2], in_=sig_view[:, 2])
@@ -104,7 +102,7 @@ def tile_bootstrap_signature_cosine_s12_kernel(
         def order_dev(g):
             nc.vector.tensor_copy(
                 out=dev_w[:, g].bitcast(I32).rearrange("p k (t a w) -> p k t a w", t=PACK, w=2),
-                in_=dev_w_raw[:, g].bitcast(I32).rearrange("p k (a t w) -> p k t a w", t=PACK, w=2),
+                in_=dev_w_raw[:, :, g * 2 * PASS : (g + 1) * 2 * PASS].bitcast(I32).rearrange("p k (a t w) -> p k t a w", t=PACK, w=2),
             )
 
         def order_dev_scales():
@@ -131,9 +129,9 @@ def tile_bootstrap_signature_cosine_s12_kernel(
             for i in range(passes):
                 nc.tensor.matmul_mx(
                     out=bank[:],
-                    lhsT=dev_w_raw[:, 0, 0, 0 : 2 * P].bitcast(FP4X4),
+                    lhsT=boot_w[:, 0, 0, 0 : 2 * P].bitcast(FP4X4),
                     lhsT_scale=dev_s_raw[:, 0, 0:P],
-                    rhs=dev_w_raw[:, 0, 0, :].bitcast(FP4X4),
+                    rhs=boot_w[:, 0, 0, :].bitcast(FP4X4),
                     rhs_scale=dev_s_raw[:, 0, 0:BANK],
                     start=True,
                     stop=True,
@@ -202,10 +200,10 @@ def tile_bootstrap_signature_cosine_s12_kernel(
             else:
                 nc.vector.tensor_copy(out=dst, in_=src)
 
-        def expo_quant(h):
-            n = slice(h * BANK, (h + 1) * BANK)
+        def expo_quant(b):
+            n = slice(b * 2 * P, (b + 1) * 2 * P)
             nc.vector.quantize_mx(
-                out=expo_c[:, n].bitcast(FP8X4), scales=expo_s[:, n], in_=expo_t[:, h * BANK * PACK : (h + 1) * BANK * PACK]
+                out=expo_c[:, n].bitcast(FP8X4), scales=expo_s[:, n], in_=expo_t[:, b * 2 * PASS : (b + 1) * 2 * PASS]
             )
 
         def mix_bank(g, i, eng):
@@ -229,18 +227,18 @@ def tile_bootstrap_signature_cosine_s12_kernel(
             else:
                 nc.vector.tensor_copy(out=dst, in_=src)
 
-        def mix_quant(g, h):
-            n = slice(h * BANK, (h + 1) * BANK)
+        def mix_quant(g, lo, width):
+            n = slice(lo, lo + width)
             nc.vector.quantize_mx(
                 out=mix_c[:, g, n].bitcast(FP8X4),
                 scales=mix_s[:, g, n],
-                in_=mix_in[:, g, h * BANK * PACK : (h + 1) * BANK * PACK],
+                in_=mix_in[:, g, lo * PACK : (lo + width) * PACK],
             )
 
-        def out_bank(i, h, eng, lo=0, width=BANK):
+        def out_bank(i, lo, width, eng):
             bank = psum.tile([P, width], F32, name="out_bank", tag="bank")
             m = slice(i * P, (i + 1) * P)
-            n = slice(h * BANK + lo, h * BANK + lo + width)
+            n = slice(lo, lo + width)
             for g in range(FG):
                 nc.tensor.matmul_mx(
                     out=bank[:],
@@ -251,7 +249,7 @@ def tile_bootstrap_signature_cosine_s12_kernel(
                     start=(g == 0),
                     stop=(g == FG - 1),
                 )
-            result = ring.tile([P, width], F32, name="result", tag="result", bufs=8)
+            result = ring.tile([P, width], F32, name="result", tag="result", bufs=10)
             factor = rlen_cols[:, i : i + 1]
             if eng == "S":
                 nc.scalar.activation(out=result[:], in_=bank[:], func=ACT.Copy, scale=factor)
@@ -260,77 +258,117 @@ def tile_bootstrap_signature_cosine_s12_kernel(
             nc.sync.dma_start(out=out[m, n], in_=result[:])
 
         turn_base()
-        order_dev(0)
         order_dev_scales()
         fetch_base()
+        order_dev(0)
         warm_up(3)
         order_dev(1)
-        sig_weave(0)
         order_dev(2)
-        for g in range(FG):
-            for t in range(PACK):
-                cat_bank(0, g, t, "S")
-        sig_quant(0)
+        sig_weave(0)
         sig_weave(1)
+        sig_quant(0)
+        cat_bank(0, 0, 0, "S")
+        cat_bank(0, 0, 1, "S")
+        cat_bank(0, 0, 2, "S")
+        cat_bank(0, 0, 3, "S")
         cat_weave(0, 0)
         sig_quant(1)
         sig_weave(2)
         cat_quant(0, 0)
+        cat_bank(0, 1, 0, "S")
+        cat_bank(0, 1, 1, "S")
+        cat_bank(0, 1, 2, "S")
+        cat_bank(0, 1, 3, "S")
+        cat_bank(0, 2, 0, "S")
+        cat_bank(0, 2, 1, "S")
+        cat_bank(0, 2, 2, "S")
+        cat_bank(0, 2, 3, "S")
         turn_rlen()
-        expo_bank(0, "S")
-        expo_bank(1, "S")
         cat_weave(0, 1)
         sig_quant(2)
-        expo_bank(2, "V")
-        expo_bank(3, "S")
+        expo_bank(0, "S")
         expo_quant(0)
-        cat_weave(0, 2)
-        cat_quant(0, 1)
-        for t in range(PACK):
-            cat_bank(1, 0, t, "S")
-        for i in range(4):
-            mix_bank(0, i, "VVVS"[i])
-            if i == 0:
-                cat_quant(0, 2)
-        for t in range(PACK):
-            cat_bank(1, 1, t, "S")
-        for i in range(4):
-            mix_bank(1, i, "VVVS"[i])
-            if i == 0:
-                mix_quant(0, 0)
+        expo_bank(1, "S")
         expo_quant(1)
-        for t in range(PACK):
-            cat_bank(1, 2, t, "S")
-        for i in range(4):
-            mix_bank(2, i, "VSVS"[i])
-            if i == 0:
-                mix_quant(1, 0)
-        mix_bank(0, 4, "S")
-        mix_quant(2, 0)
-        for i in range(1, 4):
-            mix_bank(0, 4 + i, "S")
+        expo_bank(2, "S")
+        expo_bank(3, "S")
+        cat_quant(0, 1)
+        cat_weave(0, 2)
+        cat_bank(1, 0, 0, "S")
+        cat_bank(1, 0, 1, "S")
+        cat_bank(1, 0, 2, "S")
+        cat_bank(1, 0, 3, "S")
+        mix_bank(0, 0, "S")
+        mix_bank(0, 1, "V")
+        mix_bank(0, 2, "S")
+        mix_bank(0, 3, "V")
+        cat_quant(0, 2)
+        expo_quant(2)
+        mix_bank(1, 0, "S")
+        mix_bank(1, 1, "V")
+        mix_bank(1, 2, "S")
+        mix_bank(1, 3, "V")
+        mix_quant(0, 0, 512)
+        mix_bank(2, 0, "S")
+        mix_bank(2, 1, "V")
+        mix_bank(2, 2, "S")
+        mix_bank(2, 3, "V")
+        mix_quant(1, 0, 512)
+        cat_bank(1, 1, 0, "S")
+        cat_bank(1, 1, 1, "S")
+        cat_bank(1, 1, 2, "S")
+        cat_bank(1, 1, 3, "V")
+        mix_quant(2, 0, 512)
         cat_weave(1, 0)
-        for i in range(4):
-            mix_bank(1, 4 + i, "S")
-        out_bank(0, 0, "S")
-        cat_weave(1, 1)
+        mix_bank(0, 4, "S")
+        mix_bank(0, 5, "S")
+        mix_bank(1, 4, "S")
+        mix_bank(1, 5, "S")
+        mix_quant(0, 512, 256)
         cat_quant(1, 0)
-        out_bank(1, 0, "S")
-        cat_weave(1, 2)
+        mix_bank(2, 4, "S")
+        mix_bank(2, 5, "S")
+        mix_quant(1, 512, 256)
+        cat_weave(1, 1)
+        cat_bank(1, 2, 0, "S")
+        cat_bank(1, 2, 1, "S")
+        cat_bank(1, 2, 2, "S")
+        cat_bank(1, 2, 3, "S")
+        mix_quant(2, 512, 256)
+        expo_quant(3)
         cat_quant(1, 1)
-        out_bank(2, 0, "S")
+        cat_weave(1, 2)
+        out_bank(0, 0, 512, "S")
+        out_bank(1, 0, 512, "S")
+        out_bank(2, 0, 512, "S")
+        out_bank(3, 0, 512, "V")
         cat_quant(1, 2)
-        mix_quant(0, 1)
-        out_bank(3, 0, "S")
-        for i in range(4):
-            mix_bank(2, 4 + i, "SV"[i % 2])
-            if i == 1:
-                mix_quant(1, 1)
-        out_bank(4, 0, "S")
-        mix_quant(2, 1)
-        for i in range(5, 8):
-            out_bank(i, 0, "VS"[i % 2])
-        for i in range(7):
-            out_bank(i, 1, "VS"[i % 2])
-        out_bank(7, 1, "S", 0, 256)
-        out_bank(7, 1, "V", 256, 256)
+        mix_bank(0, 6, "S")
+        mix_bank(0, 7, "S")
+        out_bank(0, 512, 256, "V")
+        out_bank(1, 512, 256, "V")
+        mix_bank(1, 6, "S")
+        mix_bank(1, 7, "S")
+        mix_quant(0, 768, 256)
+        out_bank(2, 512, 256, "V")
+        out_bank(3, 512, 256, "V")
+        mix_bank(2, 6, "S")
+        mix_bank(2, 7, "V")
+        mix_quant(1, 768, 256)
+        out_bank(4, 0, 512, "S")
+        mix_quant(2, 768, 256)
+        out_bank(5, 0, 512, "V")
+        out_bank(6, 0, 512, "S")
+        out_bank(7, 0, 512, "V")
+        out_bank(4, 512, 256, "S")
+        out_bank(5, 512, 256, "V")
+        out_bank(6, 512, 256, "S")
+        out_bank(7, 512, 256, "V")
+        out_bank(0, 768, 256, "S")
+        out_bank(1, 768, 256, "V")
+        out_bank(2, 768, 256, "S")
+        out_bank(3, 768, 256, "V")
+        out_bank(4, 768, 256, "S")
+        out_bank(5, 768, 256, "V")
+        out_bank(6, 768, 256, "S")
+        out_bank(7, 768, 256, "V")

@@ -40,7 +40,7 @@ def tile_bootstrap_signature_cosine_s12_kernel(
         dev_w = keep.tile([P, FG, KG, 2 * PASS], U8, name="dev_w", align_bytes=64)
         dev_s = keep.tile([P, FG, KG, PASS], U8, name="dev_s", align_bytes=64)
         boot_w = keep.tile([P, 2, KG, 2 * BANK], U8, name="boot_w", align_bytes=64)
-        boot_s = keep.tile([P, KG, M], U8, name="boot_s", align_bytes=64)
+        boot_s = keep.tile([P, 2, KG, BANK], U8, name="boot_s", align_bytes=64)
         base_raw = keep.tile([FG, PASS], BF16, name="base_raw", align_bytes=64)
         base_rows = keep.tile([P, PACK, P], BF16, name="base_rows", align_bytes=64)
         base_cols = keep.tile([P, PACK, FG], F32, name="base_cols", align_bytes=64)
@@ -53,6 +53,7 @@ def tile_bootstrap_signature_cosine_s12_kernel(
         sig_c = keep.tile([P, F], U32, name="sig_c", align_bytes=64)
         sig_s = keep.tile([P, F], U8, name="sig_s", align_bytes=64)
         expo_raw = keep.tile([P, R // P, J], BF16, name="expo_raw", align_bytes=64)
+        expo_uw = keep.tile([P, R // P, 2, P], F32, name="expo_uw", align_bytes=64)
         expo_t = keep.tile([P, R * PACK], BF16, name="expo_t", align_bytes=64)
         expo_c = keep.tile([P, R], U32, name="expo_c", align_bytes=64)
         expo_s = keep.tile([P, R], U8, name="expo_s", align_bytes=64)
@@ -73,11 +74,11 @@ def tile_bootstrap_signature_cosine_s12_kernel(
 
         def load_scales(dst, src):
             by_quadrant = src.rearrange("g (q r) n -> q r g n", r=4)
-            for q in range(4):
-                nc.sync.dma_start(out=dst[32 * q : 32 * q + 4, :, :].bitcast(I32), in_=by_quadrant[q].bitcast(I32))
+            for q in (0, 2, 1, 3):
+                nc.sync.dma_start(out=dst[32 * q : 32 * q + 4].bitcast(I32), in_=by_quadrant[q].bitcast(I32))
 
         nc.gpsimd.memset(dev_s_raw[:].rearrange("p g n -> p (g n)").bitcast(I32), 0)
-        nc.vector.memset(boot_s[:].rearrange("p g n -> p (g n)").bitcast(I32), 0)
+        nc.vector.memset(boot_s[:].rearrange("p h g n -> p (h g n)").bitcast(I32), 0)
         nc.vector.memset(warm[:], 0.0)
         nc.scalar.dma_start(out=base_raw[:], in_=base.rearrange("(g f) -> g f", f=PASS))
         nc.scalar.activation(out=warm[:, 4:5], in_=warm[:, 0:1], func=ACT.Relu)
@@ -86,9 +87,9 @@ def tile_bootstrap_signature_cosine_s12_kernel(
         make_identity(nc, ident_bf[:])
         make_identity(nc, ident_f32[:])
         load_words(boot_w, boot_words, 0)
-        load_scales(dev_s_raw, dev_scales)
+        load_scales(dev_s_raw[:], dev_scales)
         nc.sync.dma_start(out=dev_w_raw[:].bitcast(I32), in_=dev_words.rearrange("k p n -> p k n").bitcast(I32))
-        load_scales(boot_s, boot_scales)
+        load_scales(boot_s[:, 0], boot_scales[:, :, 0:BANK])
         sig_view = sig.rearrange("(p j) (g f) -> p g j f", j=PACK, f=PASS)
         expo_view = expo.rearrange("(i p) j -> p i j", p=P)
         nc.sync.dma_start(out=sig_raw[:, 0], in_=sig_view[:, 0])
@@ -98,6 +99,7 @@ def tile_bootstrap_signature_cosine_s12_kernel(
         nc.sync.dma_start(out=expo_raw[:, 4:8], in_=expo_view[:, 4:8])
         nc.sync.dma_start(out=rlen_rows[0 : M // P, :], in_=rlen.rearrange("(i p) -> i p", p=P))
         load_words(boot_w, boot_words, 1)
+        load_scales(boot_s[:, 1], boot_scales[:, :, BANK : 2 * BANK])
 
         def order_dev(g):
             nc.vector.tensor_copy(
@@ -151,7 +153,7 @@ def tile_bootstrap_signature_cosine_s12_kernel(
                     lhsT=dev_w[:, g, k, 2 * col : 2 * (col + P)].bitcast(FP4X4),
                     lhsT_scale=dev_s[:, g, k, col : col + P],
                     rhs=boot_w[:, h, k, :].bitcast(FP4X4),
-                    rhs_scale=boot_s[:, k, h * BANK : (h + 1) * BANK],
+                    rhs_scale=boot_s[:, h, k, :],
                     start=(k == 0),
                     stop=(k == KG - 1),
                 )
@@ -187,12 +189,18 @@ def tile_bootstrap_signature_cosine_s12_kernel(
             n = slice(g * PASS, (g + 1) * PASS)
             nc.vector.quantize_mx(out=sig_c[:, n].bitcast(FP8X4), scales=sig_s[:, n], in_=staged[("sig", g)][:])
 
+        def expo_split(h):
+            tiles = slice(4 * h, 4 * h + 4)
+            nc.vector.tensor_copy(
+                out=expo_uw[:, tiles],
+                in_=expo_raw[:, tiles].bitcast(F32).rearrange("p i (w u) -> p i u w", u=2),
+            )
+
         def expo_bank(b, eng):
             bank = psum.tile([P, 2, 2, P], F32, name="expo_bank", tag="bank")
             for i in range(2):
-                words = expo_raw[:, 2 * b + i, :].bitcast(F32)
                 for u in range(2):
-                    nc.tensor.transpose(bank[:, i, u, :], words[:, u : J // 2 : 2], ident_f32[:])
+                    nc.tensor.transpose(bank[:, i, u, :], expo_uw[:, 2 * b + i, u, :], ident_f32[:])
             dst = expo_t[:, b * 2 * PASS : (b + 1) * 2 * PASS].bitcast(F32).rearrange("p (i r u) -> p i r u", i=2, u=2)
             src = bank[:].rearrange("p i u r -> p i r u")
             if eng == "S":
@@ -267,14 +275,15 @@ def tile_bootstrap_signature_cosine_s12_kernel(
         sig_weave(0)
         sig_weave(1)
         sig_quant(0)
+        expo_split(0)
+        sig_quant(1)
+        sig_weave(2)
+        expo_split(1)
+        sig_quant(2)
         cat_bank(0, 0, 0, "S")
         cat_bank(0, 0, 1, "S")
         cat_bank(0, 0, 2, "S")
         cat_bank(0, 0, 3, "S")
-        cat_weave(0, 0)
-        sig_quant(1)
-        sig_weave(2)
-        cat_quant(0, 0)
         cat_bank(0, 1, 0, "S")
         cat_bank(0, 1, 1, "S")
         cat_bank(0, 1, 2, "S")
@@ -284,26 +293,25 @@ def tile_bootstrap_signature_cosine_s12_kernel(
         cat_bank(0, 2, 2, "S")
         cat_bank(0, 2, 3, "S")
         turn_rlen()
-        cat_weave(0, 1)
-        sig_quant(2)
+        cat_weave(0, 0)
         expo_bank(0, "S")
-        expo_quant(0)
         expo_bank(1, "S")
-        expo_quant(1)
+        expo_quant(0)
         expo_bank(2, "S")
+        expo_quant(1)
         expo_bank(3, "S")
-        cat_quant(0, 1)
-        cat_weave(0, 2)
+        cat_quant(0, 0)
+        cat_weave(0, 1)
         cat_bank(1, 0, 0, "S")
         cat_bank(1, 0, 1, "S")
         cat_bank(1, 0, 2, "S")
         cat_bank(1, 0, 3, "S")
+        expo_quant(2)
         mix_bank(0, 0, "S")
         mix_bank(0, 1, "V")
         mix_bank(0, 2, "S")
         mix_bank(0, 3, "V")
-        cat_quant(0, 2)
-        expo_quant(2)
+        cat_quant(0, 1)
         mix_bank(1, 0, "S")
         mix_bank(1, 1, "V")
         mix_bank(1, 2, "S")
@@ -314,28 +322,30 @@ def tile_bootstrap_signature_cosine_s12_kernel(
         mix_bank(2, 2, "S")
         mix_bank(2, 3, "V")
         mix_quant(1, 0, 512)
+        cat_weave(0, 2)
         cat_bank(1, 1, 0, "S")
         cat_bank(1, 1, 1, "S")
         cat_bank(1, 1, 2, "S")
-        cat_bank(1, 1, 3, "V")
+        cat_bank(1, 1, 3, "S")
         mix_quant(2, 0, 512)
-        cat_weave(1, 0)
+        cat_quant(0, 2)
         mix_bank(0, 4, "S")
         mix_bank(0, 5, "S")
         mix_bank(1, 4, "S")
         mix_bank(1, 5, "S")
+        cat_weave(1, 0)
         mix_quant(0, 512, 256)
-        cat_quant(1, 0)
         mix_bank(2, 4, "S")
         mix_bank(2, 5, "S")
         mix_quant(1, 512, 256)
-        cat_weave(1, 1)
+        expo_quant(3)
+        cat_quant(1, 0)
         cat_bank(1, 2, 0, "S")
         cat_bank(1, 2, 1, "S")
         cat_bank(1, 2, 2, "S")
         cat_bank(1, 2, 3, "S")
+        cat_weave(1, 1)
         mix_quant(2, 512, 256)
-        expo_quant(3)
         cat_quant(1, 1)
         cat_weave(1, 2)
         out_bank(0, 0, 512, "S")
@@ -345,12 +355,12 @@ def tile_bootstrap_signature_cosine_s12_kernel(
         cat_quant(1, 2)
         mix_bank(0, 6, "S")
         mix_bank(0, 7, "S")
-        out_bank(0, 512, 256, "V")
+        out_bank(0, 512, 256, "S")
         out_bank(1, 512, 256, "V")
         mix_bank(1, 6, "S")
         mix_bank(1, 7, "S")
         mix_quant(0, 768, 256)
-        out_bank(2, 512, 256, "V")
+        out_bank(2, 512, 256, "S")
         out_bank(3, 512, 256, "V")
         mix_bank(2, 6, "S")
         mix_bank(2, 7, "V")

@@ -23,6 +23,7 @@ BANK = 512
 KG = K // PASS
 FG = F // PASS
 RUN = 4
+PIECE = 256
 
 
 def tile_bootstrap_signature_cosine_s12_kernel(
@@ -35,15 +36,16 @@ def tile_bootstrap_signature_cosine_s12_kernel(
         psum = ctx.enter_context(tc.psum_pool(name="psum", bufs=8))
         ctx.enter_context(tc.manual_schedule())
 
-        dev_w_raw = keep.tile([P, KG, 2 * F], U8, name="dev_w_raw", align_bytes=64)
-        dev_s_raw = keep.tile([P, KG, F], U8, name="dev_s_raw", align_bytes=64)
+        dev_w_raw = keep.tile([P, FG, KG, 2 * PASS], U8, name="dev_w_raw", align_bytes=64)
+        dev_s_first = keep.tile([P, KG, PASS], U8, name="dev_s_first", align_bytes=64)
+        dev_s_rest = keep.tile([P, KG, F - PASS], U8, name="dev_s_rest", align_bytes=64)
         dev_w = keep.tile([P, FG, KG, 2 * PASS], U8, name="dev_w", align_bytes=64)
         dev_s = keep.tile([P, FG, KG, PASS], U8, name="dev_s", align_bytes=64)
         boot_w = keep.tile([P, 2, KG, 2 * BANK], U8, name="boot_w", align_bytes=64)
-        boot_s = keep.tile([P, 2, KG, BANK], U8, name="boot_s", align_bytes=64)
-        base_raw = keep.tile([FG, PASS], BF16, name="base_raw", align_bytes=64)
-        base_rows = keep.tile([P, PACK, P], BF16, name="base_rows", align_bytes=64)
-        base_cols = keep.tile([P, PACK, FG], F32, name="base_cols", align_bytes=64)
+        boot_s = [keep.tile([P, KG, BANK], U8, name="boot_s%d" % h, align_bytes=64) for h in range(2)]
+        base_raw = keep.tile([P, F // 4], BF16, name="base_raw", align_bytes=64)
+        base_rows = keep.tile([P, BANK], BF16, name="base_rows", align_bytes=64)
+        base_cols = keep.tile([P, BANK], BF16, name="base_cols", align_bytes=64)
         rlen_rows = keep.tile([P, P], BF16, name="rlen_rows", align_bytes=64)
         rlen_cols = keep.tile([P, M // P], F32, name="rlen_cols", align_bytes=64)
         ident_bf = keep.tile([P, P], BF16, name="ident_bf", align_bytes=64)
@@ -52,7 +54,7 @@ def tile_bootstrap_signature_cosine_s12_kernel(
         sig_raw = keep.tile([P, FG, PACK, PASS], BF16, name="sig_raw", align_bytes=64)
         sig_c = keep.tile([P, F], U32, name="sig_c", align_bytes=64)
         sig_s = keep.tile([P, F], U8, name="sig_s", align_bytes=64)
-        expo_raw = keep.tile([P, R // P, J], BF16, name="expo_raw", align_bytes=64)
+        expo_raw = [keep.tile([P, 2, 2 * J], BF16, name="expo_raw%d" % h, align_bytes=64) for h in range(2)]
         expo_uw = keep.tile([P, R // P, 2, P], F32, name="expo_uw", align_bytes=64)
         expo_t = keep.tile([P, R * PACK], BF16, name="expo_t", align_bytes=64)
         expo_c = keep.tile([P, R], U32, name="expo_c", align_bytes=64)
@@ -65,76 +67,50 @@ def tile_bootstrap_signature_cosine_s12_kernel(
         mix_s = keep.tile([P, FG, R], U8, name="mix_s", align_bytes=64)
 
         staged = {}
-
-        def load_words(dst, src, part):
-            nc.sync.dma_start(
-                out=dst[:, part].bitcast(I32),
-                in_=src.rearrange("k p (c n) -> p c k n", n=2 * BANK)[:, part].bitcast(I32),
-            )
-
-        def load_scales(dst, src):
-            by_quadrant = src.rearrange("g (q r) n -> q r g n", r=4)
-            for q in (0, 2, 1, 3):
-                nc.sync.dma_start(out=dst[32 * q : 32 * q + 4].bitcast(I32), in_=by_quadrant[q].bitcast(I32))
-
-        nc.gpsimd.memset(dev_s_raw[:].rearrange("p g n -> p (g n)").bitcast(I32), 0)
-        nc.vector.memset(boot_s[:].rearrange("p h g n -> p (h g n)").bitcast(I32), 0)
-        nc.vector.memset(warm[:], 0.0)
-        nc.scalar.dma_start(out=base_raw[:], in_=base.rearrange("(g f) -> g f", f=PASS))
-        nc.scalar.activation(out=warm[:, 4:5], in_=warm[:, 0:1], func=ACT.Relu)
-        nc.vector.memset(base_rows[:], 0.0)
-        nc.vector.memset(rlen_rows[:], 0.0)
-        make_identity(nc, ident_bf[:])
-        make_identity(nc, ident_f32[:])
-        load_words(boot_w, boot_words, 0)
-        load_scales(dev_s_raw[:], dev_scales)
-        nc.sync.dma_start(out=dev_w_raw[:].bitcast(I32), in_=dev_words.rearrange("k p n -> p k n").bitcast(I32))
-        load_scales(boot_s[:, 0], boot_scales[:, :, 0:BANK])
         sig_view = sig.rearrange("(p j) (g f) -> p g j f", j=PACK, f=PASS)
-        expo_view = expo.rearrange("(i p) j -> p i j", p=P)
-        nc.sync.dma_start(out=sig_raw[:, 0], in_=sig_view[:, 0])
-        nc.sync.dma_start(out=sig_raw[:, 1], in_=sig_view[:, 1])
-        nc.sync.dma_start(out=expo_raw[:, 0:4], in_=expo_view[:, 0:4])
-        nc.sync.dma_start(out=sig_raw[:, 2], in_=sig_view[:, 2])
-        nc.sync.dma_start(out=expo_raw[:, 4:8], in_=expo_view[:, 4:8])
-        nc.sync.dma_start(out=rlen_rows[0 : M // P, :], in_=rlen.rearrange("(i p) -> i p", p=P))
-        load_words(boot_w, boot_words, 1)
-        load_scales(boot_s[:, 1], boot_scales[:, :, BANK : 2 * BANK])
+        expo_view = expo.rearrange("(b p i) j -> p b (i j)", p=P, i=2)
+        dev_view = dev_words.rearrange("k p (g n) -> p g k n", g=FG)
+        boot_view = boot_words.rearrange("k p (h n) -> p h k n", h=2)
 
-        def order_dev(g):
+        def load_bytes(dst, src):
+            nc.sync.dma_start(out=dst.bitcast(I32), in_=src.bitcast(I32))
+
+        def load_scale_rows(dst, src, r):
+            load_bytes(dst[r:P:32], src.rearrange("k (q r) n -> r q k n", r=4)[r])
+
+        def order_dev_words(g):
             nc.vector.tensor_copy(
                 out=dev_w[:, g].bitcast(I32).rearrange("p k (t a w) -> p k t a w", t=PACK, w=2),
-                in_=dev_w_raw[:, :, g * 2 * PASS : (g + 1) * 2 * PASS].bitcast(I32).rearrange("p k (a t w) -> p k t a w", t=PACK, w=2),
+                in_=dev_w_raw[:, g].bitcast(I32).rearrange("p k (a t w) -> p k t a w", t=PACK, w=2),
             )
 
-        def order_dev_scales():
+        def order_dev_scales(lo, hi, raw):
             nc.vector.tensor_copy(
-                out=dev_s[:].bitcast(I32).rearrange("p g k (t a) -> p g k t a", t=PACK),
-                in_=dev_s_raw[:].bitcast(I32).rearrange("p k (g a t) -> p g k t a", g=FG, t=PACK),
+                out=dev_s[:, lo:hi].bitcast(I32).rearrange("p g k (t a) -> p k g t a", t=PACK),
+                in_=raw[:].bitcast(I32).rearrange("p k (g a t) -> p k g t a", g=hi - lo, t=PACK),
+            )
+
+        def clear(eng, plane):
+            eng.memset(plane.rearrange("p k n -> p (k n)").bitcast(I32), 0)
+
+        def order_base():
+            nc.vector.tensor_copy(
+                out=base_rows[:, 0 : F // 4].rearrange("p (g t a i) -> p g t a i", g=FG, t=PACK, i=RUN),
+                in_=base_raw[:].rearrange("p (g a t i) -> p g t a i", g=FG, t=PACK, i=RUN),
             )
 
         def turn_base():
-            nc.vector.tensor_copy(
-                out=base_rows[0:FG].rearrange("g t (a i) -> g t a i", i=RUN),
-                in_=base_raw[:].rearrange("g (a t i) -> g t a i", t=PACK, i=RUN),
-            )
-            bank = psum.tile([P, PACK, P], BF16, name="base_bank", tag="bank")
-            for t in range(PACK):
-                nc.tensor.transpose(bank[:, t, :], base_rows[:, t, :], ident_bf[:])
-            staged["base"] = bank
-
-        def fetch_base():
-            nc.vector.tensor_copy(out=base_cols[:], in_=staged["base"][:, :, 0:FG])
+            nc.vector.transpose(base_cols[:], base_rows[:])
 
         def warm_up(passes):
             bank = psum.tile([P, BANK], F32, name="warm_bank", tag="bank")
             for i in range(passes):
                 nc.tensor.matmul_mx(
                     out=bank[:],
-                    lhsT=boot_w[:, 0, 0, 0 : 2 * P].bitcast(FP4X4),
-                    lhsT_scale=dev_s_raw[:, 0, 0:P],
-                    rhs=boot_w[:, 0, 0, :].bitcast(FP4X4),
-                    rhs_scale=dev_s_raw[:, 0, 0:BANK],
+                    lhsT=dev_w_raw[:, 0, 0, 0 : 2 * P].bitcast(FP4X4),
+                    lhsT_scale=dev_s_first[:, 0, 0:P],
+                    rhs=dev_w_raw[:, 0, 0, :].bitcast(FP4X4),
+                    rhs_scale=dev_s_first[:, 0, 0:BANK],
                     start=True,
                     stop=True,
                 )
@@ -153,11 +129,11 @@ def tile_bootstrap_signature_cosine_s12_kernel(
                     lhsT=dev_w[:, g, k, 2 * col : 2 * (col + P)].bitcast(FP4X4),
                     lhsT_scale=dev_s[:, g, k, col : col + P],
                     rhs=boot_w[:, h, k, :].bitcast(FP4X4),
-                    rhs_scale=boot_s[:, h, k, :],
+                    rhs_scale=boot_s[h][:, k, :],
                     start=(k == 0),
                     stop=(k == KG - 1),
                 )
-            bias = base_cols[:, t, g : g + 1]
+            bias = base_cols[:, 32 * (PACK * g + t) : 32 * (PACK * g + t) + 1]
             if eng == "S":
                 nc.scalar.activation(out=cat_rows[:, h, g, t, :], in_=bank[:], func=ACT.Relu, bias=bias)
             else:
@@ -165,20 +141,25 @@ def tile_bootstrap_signature_cosine_s12_kernel(
                     out=cat_rows[:, h, g, t, :], in0=bank[:], scalar1=bias, scalar2=0.0, op0=ALU.add, op1=ALU.max
                 )
 
-        def cat_weave(h, g):
-            woven = ring.tile([P, BANK * PACK], BF16, name="woven", tag="woven", bufs=3, align_bytes=64)
+        def cat_unit(h, g, engs="SSSS"):
+            for t in range(PACK):
+                cat_bank(h, g, t, engs[t])
+
+        def cat_weave(g, lo, width):
+            h, c = divmod(lo, BANK)
+            woven = ring.tile([P, width * PACK], BF16, name="woven", tag="woven", bufs=5, align_bytes=64)
             nc.vector.tensor_copy(
                 out=woven[:].rearrange("p (c i t) -> p c t i", i=RUN, t=PACK),
-                in_=cat_rows[:, h, g].rearrange("p t (c i) -> p c t i", i=RUN),
+                in_=cat_rows[:, h, g, :, c : c + width].rearrange("p t (c i) -> p c t i", i=RUN),
             )
-            staged[("cat", h, g)] = woven
+            staged[("cat", g, lo)] = woven
 
-        def cat_quant(h, g):
-            n = slice(h * BANK, (h + 1) * BANK)
-            nc.vector.quantize_mx(out=cat_c[:, g, n].bitcast(FP8X4), scales=cat_s[:, g, n], in_=staged[("cat", h, g)][:])
+        def cat_quant(g, lo, width):
+            n = slice(lo, lo + width)
+            nc.vector.quantize_mx(out=cat_c[:, g, n].bitcast(FP8X4), scales=cat_s[:, g, n], in_=staged[("cat", g, lo)][:])
 
         def sig_weave(g):
-            woven = ring.tile([P, BANK * PACK], BF16, name="woven", tag="woven", bufs=3, align_bytes=64)
+            woven = ring.tile([P, BANK * PACK], BF16, name="woven", tag="woven", bufs=5, align_bytes=64)
             nc.vector.tensor_copy(
                 out=woven[:].rearrange("p (t a i j) -> p t a j i", t=PACK, i=RUN, j=PACK),
                 in_=sig_raw[:, g].rearrange("p j (a t i) -> p t a j i", t=PACK, i=RUN),
@@ -193,7 +174,7 @@ def tile_bootstrap_signature_cosine_s12_kernel(
             tiles = slice(4 * h, 4 * h + 4)
             nc.vector.tensor_copy(
                 out=expo_uw[:, tiles],
-                in_=expo_raw[:, tiles].bitcast(F32).rearrange("p i (w u) -> p i u w", u=2),
+                in_=expo_raw[h][:].bitcast(F32).rearrange("p b (i w u) -> p (b i) u w", i=2, u=2),
             )
 
         def expo_bank(b, eng):
@@ -201,17 +182,17 @@ def tile_bootstrap_signature_cosine_s12_kernel(
             for i in range(2):
                 for u in range(2):
                     nc.tensor.transpose(bank[:, i, u, :], expo_uw[:, 2 * b + i, u, :], ident_f32[:])
-            dst = expo_t[:, b * 2 * PASS : (b + 1) * 2 * PASS].bitcast(F32).rearrange("p (i r u) -> p i r u", i=2, u=2)
-            src = bank[:].rearrange("p i u r -> p i r u")
+            dst = expo_t[:, b * 2 * PASS : (b + 1) * 2 * PASS].bitcast(F32).rearrange("p (r i u) -> p r i u", i=2, u=2)
+            src = bank[:].rearrange("p i u r -> p r i u")
             if eng == "S":
                 nc.scalar.copy(out=dst, in_=src)
             else:
                 nc.vector.tensor_copy(out=dst, in_=src)
 
-        def expo_quant(b):
-            n = slice(b * 2 * P, (b + 1) * 2 * P)
+        def expo_quant(lo, width):
+            n = slice(lo, lo + width)
             nc.vector.quantize_mx(
-                out=expo_c[:, n].bitcast(FP8X4), scales=expo_s[:, n], in_=expo_t[:, b * 2 * PASS : (b + 1) * 2 * PASS]
+                out=expo_c[:, n].bitcast(FP8X4), scales=expo_s[:, n], in_=expo_t[:, lo * PACK : (lo + width) * PACK]
             )
 
         def mix_bank(g, i, eng):
@@ -265,120 +246,106 @@ def tile_bootstrap_signature_cosine_s12_kernel(
                 nc.vector.tensor_scalar(out=result[:], in0=bank[:], scalar1=factor, scalar2=None, op0=ALU.mult)
             nc.sync.dma_start(out=out[m, n], in_=result[:])
 
+        clear(nc.vector, dev_s_first[:])
+        nc.vector.memset(base_raw[:], 0.0)
+        clear(nc.vector, boot_s[0][:])
+        nc.vector.memset(warm[:], 0.0)
+        nc.scalar.activation(out=warm[:, 4:5], in_=warm[:, 0:1], func=ACT.Relu)
+        nc.vector.memset(base_rows[:, F // 4 : BANK], 0.0)
+        clear(nc.vector, dev_s_rest[:])
+        clear(nc.vector, boot_s[1][:])
+        nc.vector.memset(rlen_rows[:], 0.0)
+        make_identity(nc, ident_bf[:])
+        make_identity(nc, ident_f32[:])
+        load_bytes(dev_w_raw[:, 0], dev_view[:, 0])
+        for r in range(4):
+            load_scale_rows(dev_s_first, dev_scales[:, :, 0:PASS], r)
+        nc.sync.dma_start(
+            out=base_raw[0:P:32, :].rearrange("q (g c) -> q g c", g=FG), in_=base.rearrange("(g q c) -> q g c", g=FG, q=4)
+        )
+        load_bytes(boot_w[:, 0], boot_view[:, 0])
+        for r in range(4):
+            load_scale_rows(boot_s[0], boot_scales[:, :, 0:BANK], r)
+        load_bytes(dev_w_raw[:, 1], dev_view[:, 1])
+        for r in range(4):
+            load_scale_rows(dev_s_rest, dev_scales[:, :, PASS:F], r)
+        nc.sync.dma_start(out=sig_raw[:, 0], in_=sig_view[:, 0])
+        load_bytes(dev_w_raw[:, 2], dev_view[:, 2])
+        nc.sync.dma_start(out=expo_raw[0][:], in_=expo_view[:, 0:2])
+        nc.sync.dma_start(out=sig_raw[:, 1], in_=sig_view[:, 1])
+        load_bytes(boot_w[:, 1], boot_view[:, 1])
+        for r in range(4):
+            load_scale_rows(boot_s[1], boot_scales[:, :, BANK : 2 * BANK], r)
+        nc.sync.dma_start(out=rlen_rows[0 : M // P, :], in_=rlen.rearrange("(i p) -> i p", p=P))
+        nc.sync.dma_start(out=sig_raw[:, 2], in_=sig_view[:, 2])
+        nc.sync.dma_start(out=expo_raw[1][:], in_=expo_view[:, 2:4])
+
+        order_dev_words(0)
+        order_dev_scales(0, 1, dev_s_first)
+        order_base()
+        warm_up(2)
         turn_base()
-        order_dev_scales()
-        fetch_base()
-        order_dev(0)
-        warm_up(3)
-        order_dev(1)
-        order_dev(2)
+        cat_unit(0, 0)
+        order_dev_words(1)
+        order_dev_scales(1, FG, dev_s_rest)
+        cat_unit(0, 1)
         sig_weave(0)
-        sig_weave(1)
+        order_dev_words(2)
         sig_quant(0)
+        cat_unit(0, 2)
         expo_split(0)
-        sig_quant(1)
-        sig_weave(2)
-        expo_split(1)
-        sig_quant(2)
-        cat_bank(0, 0, 0, "S")
-        cat_bank(0, 0, 1, "S")
-        cat_bank(0, 0, 2, "S")
-        cat_bank(0, 0, 3, "S")
-        cat_bank(0, 1, 0, "S")
-        cat_bank(0, 1, 1, "S")
-        cat_bank(0, 1, 2, "S")
-        cat_bank(0, 1, 3, "S")
-        cat_bank(0, 2, 0, "S")
-        cat_bank(0, 2, 1, "S")
-        cat_bank(0, 2, 2, "S")
-        cat_bank(0, 2, 3, "S")
-        turn_rlen()
-        cat_weave(0, 0)
+        cat_weave(0, 0, PIECE)
         expo_bank(0, "S")
         expo_bank(1, "S")
-        expo_quant(0)
+        cat_quant(0, 0, PIECE)
+        sig_weave(1)
+        cat_weave(1, 0, PIECE)
+        sig_quant(1)
+        cat_quant(1, 0, PIECE)
+        cat_unit(1, 0)
+        sig_weave(2)
+        expo_quant(0, BANK)
+        sig_quant(2)
+        cat_weave(2, 0, PIECE)
+        expo_split(1)
+        cat_quant(2, 0, PIECE)
+        cat_unit(1, 1)
+        for g in range(FG):
+            for i in range(4):
+                mix_bank(g, i, "VSVS"[i])
+            if g > 0:
+                mix_quant(g - 1, 0, BANK)
         expo_bank(2, "S")
-        expo_quant(1)
         expo_bank(3, "S")
-        cat_quant(0, 0)
-        cat_weave(0, 1)
-        cat_bank(1, 0, 0, "S")
-        cat_bank(1, 0, 1, "S")
-        cat_bank(1, 0, 2, "S")
-        cat_bank(1, 0, 3, "S")
-        expo_quant(2)
-        mix_bank(0, 0, "S")
-        mix_bank(0, 1, "V")
-        mix_bank(0, 2, "S")
-        mix_bank(0, 3, "V")
-        cat_quant(0, 1)
-        mix_bank(1, 0, "S")
-        mix_bank(1, 1, "V")
-        mix_bank(1, 2, "S")
-        mix_bank(1, 3, "V")
-        mix_quant(0, 0, 512)
-        mix_bank(2, 0, "S")
-        mix_bank(2, 1, "V")
-        mix_bank(2, 2, "S")
-        mix_bank(2, 3, "V")
-        mix_quant(1, 0, 512)
-        cat_weave(0, 2)
-        cat_bank(1, 1, 0, "S")
-        cat_bank(1, 1, 1, "S")
-        cat_bank(1, 1, 2, "S")
-        cat_bank(1, 1, 3, "S")
-        mix_quant(2, 0, 512)
-        cat_quant(0, 2)
-        mix_bank(0, 4, "S")
-        mix_bank(0, 5, "S")
-        mix_bank(1, 4, "S")
-        mix_bank(1, 5, "S")
-        cat_weave(1, 0)
-        mix_quant(0, 512, 256)
-        mix_bank(2, 4, "S")
-        mix_bank(2, 5, "S")
-        mix_quant(1, 512, 256)
-        expo_quant(3)
-        cat_quant(1, 0)
-        cat_bank(1, 2, 0, "S")
-        cat_bank(1, 2, 1, "S")
-        cat_bank(1, 2, 2, "S")
-        cat_bank(1, 2, 3, "S")
-        cat_weave(1, 1)
-        mix_quant(2, 512, 256)
-        cat_quant(1, 1)
-        cat_weave(1, 2)
-        out_bank(0, 0, 512, "S")
-        out_bank(1, 0, 512, "S")
-        out_bank(2, 0, 512, "S")
-        out_bank(3, 0, 512, "V")
-        cat_quant(1, 2)
-        mix_bank(0, 6, "S")
-        mix_bank(0, 7, "S")
-        out_bank(0, 512, 256, "S")
-        out_bank(1, 512, 256, "V")
-        mix_bank(1, 6, "S")
-        mix_bank(1, 7, "S")
-        mix_quant(0, 768, 256)
-        out_bank(2, 512, 256, "S")
-        out_bank(3, 512, 256, "V")
-        mix_bank(2, 6, "S")
-        mix_bank(2, 7, "V")
-        mix_quant(1, 768, 256)
-        out_bank(4, 0, 512, "S")
-        mix_quant(2, 768, 256)
-        out_bank(5, 0, 512, "V")
-        out_bank(6, 0, 512, "S")
-        out_bank(7, 0, 512, "V")
-        out_bank(4, 512, 256, "S")
-        out_bank(5, 512, 256, "V")
-        out_bank(6, 512, 256, "S")
-        out_bank(7, 512, 256, "V")
-        out_bank(0, 768, 256, "S")
-        out_bank(1, 768, 256, "V")
-        out_bank(2, 768, 256, "S")
-        out_bank(3, 768, 256, "V")
-        out_bank(4, 768, 256, "S")
-        out_bank(5, 768, 256, "V")
-        out_bank(6, 768, 256, "S")
-        out_bank(7, 768, 256, "V")
+        turn_rlen()
+        cat_weave(0, PIECE, PIECE)
+        mix_quant(2, 0, BANK)
+        cat_unit(1, 2)
+        cat_weave(1, PIECE, PIECE)
+        expo_quant(BANK, BANK)
+        cat_weave(2, PIECE, PIECE)
+        for g in range(FG):
+            cat_quant(g, PIECE, PIECE)
+        for g in range(FG):
+            if g < 2:
+                out_bank(g, 0, BANK, "S")
+            for i in range(4, 8):
+                mix_bank(g, i, "VSVS"[i - 4])
+            if g > 0:
+                mix_quant(g - 1, BANK, BANK)
+        out_bank(2, 0, BANK, "S")
+        mix_quant(2, BANK, BANK)
+        out_bank(3, 0, BANK, "S")
+        for lo in (BANK, BANK + PIECE):
+            for g in range(FG):
+                cat_weave(g, lo, PIECE)
+            for g in range(FG):
+                cat_quant(g, lo, PIECE)
+        for i in range(4):
+            out_bank(i, BANK, BANK, "S")
+        for i in range(4, 8):
+            out_bank(i, 0, BANK, "V" if i > 5 else "S")
+            if i < 7:
+                out_bank(i, BANK, BANK, "S")
+        out_bank(7, BANK, PIECE, "S")
+        out_bank(7, BANK + PIECE, PIECE, "V")

@@ -50,6 +50,9 @@ def tile_bootstrap_signature_cosine_s12_kernel(
         rlen_cols = keep.tile([P, M // P], F32, name="rlen_cols", align_bytes=64)
         ident_bf = keep.tile([P, P], BF16, name="ident_bf", align_bytes=64)
         ident_f32 = keep.tile([P, P], F32, name="ident_f32", align_bytes=64)
+        zeros = keep.tile([P, PASS], BF16, name="zeros", align_bytes=64)
+        warm_c = keep.tile([P, BANK], U32, name="warm_c", align_bytes=64)
+        warm_s = keep.tile([P, BANK], U8, name="warm_s", align_bytes=64)
         warm = keep.tile([P, 8], F32, name="warm", align_bytes=64)
         sig_raw = keep.tile([P, FG, PACK, PASS], BF16, name="sig_raw", align_bytes=64)
         sig_c = keep.tile([P, F], U32, name="sig_c", align_bytes=64)
@@ -72,11 +75,21 @@ def tile_bootstrap_signature_cosine_s12_kernel(
         dev_view = dev_words.rearrange("k p (g n) -> p g k n", g=FG)
         boot_view = boot_words.rearrange("k p (h n) -> p h k n", h=2)
 
-        def load_bytes(dst, src):
-            nc.sync.dma_start(out=dst.bitcast(I32), in_=src.bitcast(I32))
+        def load_bytes(dst, src, queue=nc.sync):
+            queue.dma_start(out=dst.bitcast(I32), in_=src.bitcast(I32))
 
         def load_scale_rows(dst, src, r):
             load_bytes(dst[r:P:32], src.rearrange("k (q r) n -> r q k n", r=4)[r])
+
+        def load_scale_quadrant(dst, src, q, queue):
+            load_bytes(dst[32 * q : 32 * q + 4], src.rearrange("k (q r) n -> q r k n", r=4)[q], queue)
+
+        def order_first_dev_scales(q):
+            rows = slice(32 * q, 32 * q + 4)
+            nc.vector.tensor_copy(
+                out=dev_s[rows, 0].bitcast(I32).rearrange("p k (t a) -> p k t a", t=PACK),
+                in_=dev_s_first[rows].bitcast(I32).rearrange("p k (a t) -> p k t a", t=PACK),
+            )
 
         def order_dev_words(g):
             nc.vector.tensor_copy(
@@ -103,14 +116,17 @@ def tile_bootstrap_signature_cosine_s12_kernel(
             nc.vector.transpose(base_cols[:], base_rows[:])
 
         def warm_up(passes):
+            for q in range(PACK):
+                n = slice(q * P, (q + 1) * P)
+                nc.vector.quantize_mx(out=warm_c[:, n].bitcast(FP8X4), scales=warm_s[:, n], in_=zeros[:])
             bank = psum.tile([P, BANK], F32, name="warm_bank", tag="bank")
             for i in range(passes):
                 nc.tensor.matmul_mx(
                     out=bank[:],
-                    lhsT=dev_w_raw[:, 0, 0, 0 : 2 * P].bitcast(FP4X4),
-                    lhsT_scale=dev_s_first[:, 0, 0:P],
-                    rhs=dev_w_raw[:, 0, 0, :].bitcast(FP4X4),
-                    rhs_scale=dev_s_first[:, 0, 0:BANK],
+                    lhsT=warm_c[:, 0:P].bitcast(FP8X4),
+                    lhsT_scale=warm_s[:, 0:P],
+                    rhs=warm_c[:].bitcast(FP8X4),
+                    rhs_scale=warm_s[:],
                     start=True,
                     stop=True,
                 )
@@ -157,6 +173,12 @@ def tile_bootstrap_signature_cosine_s12_kernel(
         def cat_quant(g, lo, width):
             n = slice(lo, lo + width)
             nc.vector.quantize_mx(out=cat_c[:, g, n].bitcast(FP8X4), scales=cat_s[:, g, n], in_=staged[("cat", g, lo)][:])
+
+        def cat_piece(lo, width):
+            for g in range(FG):
+                cat_weave(g, lo, width)
+            for g in range(FG):
+                cat_quant(g, lo, width)
 
         def sig_weave(g):
             woven = ring.tile([P, BANK * PACK], BF16, name="woven", tag="woven", bufs=5, align_bytes=64)
@@ -224,53 +246,60 @@ def tile_bootstrap_signature_cosine_s12_kernel(
                 in_=mix_in[:, g, lo * PACK : (lo + width) * PACK],
             )
 
-        def out_bank(i, lo, width, eng):
-            bank = psum.tile([P, width], F32, name="out_bank", tag="bank")
-            m = slice(i * P, (i + 1) * P)
+        def out_banks(tiles, lo, width, engs):
             n = slice(lo, lo + width)
+            banks = [psum.tile([P, width], F32, name="out_bank", tag="bank") for i in tiles]
             for g in range(FG):
-                nc.tensor.matmul_mx(
-                    out=bank[:],
-                    lhsT=cat_c[:, g, m].bitcast(FP8X4),
-                    lhsT_scale=cat_s[:, g, m],
-                    rhs=mix_c[:, g, n].bitcast(FP8X4),
-                    rhs_scale=mix_s[:, g, n],
-                    start=(g == 0),
-                    stop=(g == FG - 1),
-                )
-            result = ring.tile([P, width], F32, name="result", tag="result", bufs=10)
-            factor = rlen_cols[:, i : i + 1]
-            if eng == "S":
-                nc.scalar.activation(out=result[:], in_=bank[:], func=ACT.Copy, scale=factor)
-            else:
-                nc.vector.tensor_scalar(out=result[:], in0=bank[:], scalar1=factor, scalar2=None, op0=ALU.mult)
-            nc.sync.dma_start(out=out[m, n], in_=result[:])
+                for i, bank in zip(tiles, banks):
+                    m = slice(i * P, (i + 1) * P)
+                    nc.tensor.matmul_mx(
+                        out=bank[:],
+                        lhsT=cat_c[:, g, m].bitcast(FP8X4),
+                        lhsT_scale=cat_s[:, g, m],
+                        rhs=mix_c[:, g, n].bitcast(FP8X4),
+                        rhs_scale=mix_s[:, g, n],
+                        start=(g == 0),
+                        stop=(g == FG - 1),
+                    )
+            for i, bank, eng in zip(tiles, banks, engs):
+                result = ring.tile([P, width], F32, name="result", tag="result", bufs=10)
+                factor = rlen_cols[:, i : i + 1]
+                if eng == "S":
+                    nc.scalar.activation(out=result[:], in_=bank[:], func=ACT.Copy, scale=factor)
+                else:
+                    nc.vector.tensor_scalar(out=result[:], in0=bank[:], scalar1=factor, scalar2=None, op0=ALU.mult)
+                nc.sync.dma_start(out=out[i * P : (i + 1) * P, n], in_=result[:])
 
-        clear(nc.vector, dev_s_first[:])
-        nc.vector.memset(base_raw[:], 0.0)
+        def out_bank(i, lo, width, eng):
+            out_banks([i], lo, width, eng)
+
         clear(nc.vector, boot_s[0][:])
+        nc.vector.memset(base_raw[:], 0.0)
+        nc.vector.memset(zeros[:], 0.0)
         nc.vector.memset(warm[:], 0.0)
-        nc.scalar.activation(out=warm[:, 4:5], in_=warm[:, 0:1], func=ACT.Relu)
+        clear(nc.vector, dev_s[:, 0])
+        warm_up(4)
         nc.vector.memset(base_rows[:, F // 4 : BANK], 0.0)
         clear(nc.vector, dev_s_rest[:])
         clear(nc.vector, boot_s[1][:])
         nc.vector.memset(rlen_rows[:], 0.0)
         make_identity(nc, ident_bf[:])
         make_identity(nc, ident_f32[:])
-        load_bytes(dev_w_raw[:, 0], dev_view[:, 0])
-        for r in range(4):
-            load_scale_rows(dev_s_first, dev_scales[:, :, 0:PASS], r)
-        nc.sync.dma_start(
+        for q in (0, 2, 1, 3):
+            load_scale_quadrant(dev_s_first, dev_scales[:, :, 0:PASS], q, nc.scalar)
+        nc.scalar.dma_start(
             out=base_raw[0:P:32, :].rearrange("q (g c) -> q g c", g=FG), in_=base.rearrange("(g q c) -> q g c", g=FG, q=4)
         )
+        nc.scalar.activation(out=warm[:, 4:5], in_=warm[:, 0:1], func=ACT.Relu)
+        load_bytes(dev_w_raw[:, 0], dev_view[:, 0])
         load_bytes(boot_w[:, 0], boot_view[:, 0])
         for r in range(4):
             load_scale_rows(boot_s[0], boot_scales[:, :, 0:BANK], r)
         load_bytes(dev_w_raw[:, 1], dev_view[:, 1])
         for r in range(4):
             load_scale_rows(dev_s_rest, dev_scales[:, :, PASS:F], r)
-        nc.sync.dma_start(out=sig_raw[:, 0], in_=sig_view[:, 0])
         load_bytes(dev_w_raw[:, 2], dev_view[:, 2])
+        nc.sync.dma_start(out=sig_raw[:, 0], in_=sig_view[:, 0])
         nc.sync.dma_start(out=expo_raw[0][:], in_=expo_view[:, 0:2])
         nc.sync.dma_start(out=sig_raw[:, 1], in_=sig_view[:, 1])
         load_bytes(boot_w[:, 1], boot_view[:, 1])
@@ -280,35 +309,30 @@ def tile_bootstrap_signature_cosine_s12_kernel(
         nc.sync.dma_start(out=sig_raw[:, 2], in_=sig_view[:, 2])
         nc.sync.dma_start(out=expo_raw[1][:], in_=expo_view[:, 2:4])
 
-        order_dev_words(0)
-        order_dev_scales(0, 1, dev_s_first)
+        for q in (0, 2, 1, 3):
+            order_first_dev_scales(q)
         order_base()
-        warm_up(2)
+        order_dev_words(0)
         turn_base()
         cat_unit(0, 0)
         order_dev_words(1)
         order_dev_scales(1, FG, dev_s_rest)
         cat_unit(0, 1)
-        sig_weave(0)
         order_dev_words(2)
-        sig_quant(0)
+        sig_weave(0)
         cat_unit(0, 2)
         expo_split(0)
-        cat_weave(0, 0, PIECE)
-        expo_bank(0, "S")
-        expo_bank(1, "S")
-        cat_quant(0, 0, PIECE)
+        sig_quant(0)
         sig_weave(1)
-        cat_weave(1, 0, PIECE)
+        expo_bank(0, "V")
+        expo_bank(1, "S")
         sig_quant(1)
-        cat_quant(1, 0, PIECE)
         cat_unit(1, 0)
         sig_weave(2)
         expo_quant(0, BANK)
         sig_quant(2)
-        cat_weave(2, 0, PIECE)
         expo_split(1)
-        cat_quant(2, 0, PIECE)
+        cat_piece(0, P)
         cat_unit(1, 1)
         for g in range(FG):
             for i in range(4):
@@ -318,32 +342,23 @@ def tile_bootstrap_signature_cosine_s12_kernel(
         expo_bank(2, "S")
         expo_bank(3, "S")
         turn_rlen()
-        cat_weave(0, PIECE, PIECE)
         mix_quant(2, 0, BANK)
         cat_unit(1, 2)
-        cat_weave(1, PIECE, PIECE)
         expo_quant(BANK, BANK)
-        cat_weave(2, PIECE, PIECE)
+        cat_piece(P, 2 * P)
+        out_bank(0, 0, BANK, "S")
         for g in range(FG):
-            cat_quant(g, PIECE, PIECE)
-        for g in range(FG):
-            if g < 2:
-                out_bank(g, 0, BANK, "S")
             for i in range(4, 8):
-                mix_bank(g, i, "VSVS"[i - 4])
+                mix_bank(g, i, ("SSSS", "VSVS", "VSVS")[g][i - 4])
             if g > 0:
                 mix_quant(g - 1, BANK, BANK)
-        out_bank(2, 0, BANK, "S")
+        out_bank(1, 0, BANK, "S")
         mix_quant(2, BANK, BANK)
-        out_bank(3, 0, BANK, "S")
-        for lo in (BANK, BANK + PIECE):
-            for g in range(FG):
-                cat_weave(g, lo, PIECE)
-            for g in range(FG):
-                cat_quant(g, lo, PIECE)
-        for i in range(4):
-            out_bank(i, BANK, BANK, "S")
-        for i in range(4, 8):
+        out_bank(2, 0, BANK, "S")
+        for i in range(3, 8):
+            cat_piece(i * P, P)
+        out_banks([0, 1, 2], BANK, BANK, "SSS")
+        for i in range(3, 8):
             out_bank(i, 0, BANK, "V" if i > 5 else "S")
             if i < 7:
                 out_bank(i, BANK, BANK, "S")

@@ -46,9 +46,9 @@ def tile_bootstrap_signature_cosine_s12_kernel(
         base_raw = keep.tile([P, F // 4], BF16, name="base_raw", align_bytes=64)
         base_rows = keep.tile([P, BANK], BF16, name="base_rows", align_bytes=64)
         base_cols = keep.tile([P, BANK], BF16, name="base_cols", align_bytes=64)
-        rlen_rows = keep.tile([P, P], BF16, name="rlen_rows", align_bytes=64)
+        rlen_raw = keep.tile([M // P, P], BF16, name="rlen_raw", align_bytes=64)
+        rlen_rows = keep.tile([P, P], F32, name="rlen_rows", align_bytes=64)
         rlen_cols = keep.tile([P, M // P], F32, name="rlen_cols", align_bytes=64)
-        ident_bf = keep.tile([P, P], BF16, name="ident_bf", align_bytes=64)
         ident_f32 = keep.tile([P, P], F32, name="ident_f32", align_bytes=64)
         zeros = keep.tile([P, PASS], BF16, name="zeros", align_bytes=64)
         warm_c = keep.tile([P, BANK], U32, name="warm_c", align_bytes=64)
@@ -132,8 +132,8 @@ def tile_bootstrap_signature_cosine_s12_kernel(
                 )
 
         def turn_rlen():
-            bank = psum.tile([P, P], BF16, name="rlen_bank", tag="bank")
-            nc.tensor.transpose(bank[:], rlen_rows[:], ident_bf[:])
+            bank = psum.tile([P, P], F32, name="rlen_bank", tag="bank")
+            nc.tensor.transpose(bank[:], rlen_rows[:], ident_f32[:])
             nc.vector.tensor_copy(out=rlen_cols[:], in_=bank[:, 0 : M // P])
 
         def cat_bank(h, g, t, eng):
@@ -273,47 +273,45 @@ def tile_bootstrap_signature_cosine_s12_kernel(
         def out_bank(i, lo, width, eng):
             out_banks([i], lo, width, eng)
 
-        clear(nc.vector, boot_s[0][:])
         nc.vector.memset(base_raw[:], 0.0)
-        nc.vector.memset(zeros[:], 0.0)
+        clear(nc.vector, boot_s[0][:])
+        nc.gpsimd.memset(zeros[:], 0.0)
         nc.vector.memset(warm[:], 0.0)
-        clear(nc.vector, dev_s[:, 0])
-        warm_up(4)
         nc.vector.memset(base_rows[:, F // 4 : BANK], 0.0)
-        clear(nc.vector, dev_s_rest[:])
-        clear(nc.vector, boot_s[1][:])
-        nc.vector.memset(rlen_rows[:], 0.0)
-        make_identity(nc, ident_bf[:])
+        clear(nc.gpsimd, dev_s[:, 0])
+        warm_up(4)
+        clear(nc.gpsimd, dev_s_rest[:])
         make_identity(nc, ident_f32[:])
-        for q in (0, 2, 1, 3):
-            load_scale_quadrant(dev_s_first, dev_scales[:, :, 0:PASS], q, nc.scalar)
-        nc.scalar.dma_start(
-            out=base_raw[0:P:32, :].rearrange("q (g c) -> q g c", g=FG), in_=base.rearrange("(g q c) -> q g c", g=FG, q=4)
-        )
         nc.scalar.activation(out=warm[:, 4:5], in_=warm[:, 0:1], func=ACT.Relu)
+        for q in (0, 2, 1, 3):
+            load_scale_quadrant(dev_s_first, dev_scales[:, :, 0:PASS], q, nc.sync)
         load_bytes(dev_w_raw[:, 0], dev_view[:, 0])
         load_bytes(boot_w[:, 0], boot_view[:, 0])
-        for r in range(4):
-            load_scale_rows(boot_s[0], boot_scales[:, :, 0:BANK], r)
+        nc.sync.dma_start(
+            out=base_raw[0:P:32, :].rearrange("q (g c) -> q g c", g=FG), in_=base.rearrange("(g q c) -> q g c", g=FG, q=4)
+        )
+        for q in (0, 2, 1, 3):
+            load_scale_quadrant(boot_s[0], boot_scales[:, :, 0:BANK], q, nc.sync)
         load_bytes(dev_w_raw[:, 1], dev_view[:, 1])
-        for r in range(4):
-            load_scale_rows(dev_s_rest, dev_scales[:, :, PASS:F], r)
+        for q in (0, 2, 1, 3):
+            load_scale_quadrant(dev_s_rest, dev_scales[:, :, PASS:F], q, nc.sync)
         load_bytes(dev_w_raw[:, 2], dev_view[:, 2])
         nc.sync.dma_start(out=sig_raw[:, 0], in_=sig_view[:, 0])
         nc.sync.dma_start(out=expo_raw[0][:], in_=expo_view[:, 0:2])
         nc.sync.dma_start(out=sig_raw[:, 1], in_=sig_view[:, 1])
         load_bytes(boot_w[:, 1], boot_view[:, 1])
-        for r in range(4):
-            load_scale_rows(boot_s[1], boot_scales[:, :, BANK : 2 * BANK], r)
-        nc.sync.dma_start(out=rlen_rows[0 : M // P, :], in_=rlen.rearrange("(i p) -> i p", p=P))
-        nc.sync.dma_start(out=sig_raw[:, 2], in_=sig_view[:, 2])
-        nc.sync.dma_start(out=expo_raw[1][:], in_=expo_view[:, 2:4])
-
         for q in (0, 2, 1, 3):
             order_first_dev_scales(q)
-        order_base()
         order_dev_words(0)
+        order_base()
         turn_base()
+        clear(nc.vector, boot_s[1][:])
+        nc.vector.memset(rlen_rows[:], 0.0)
+        for q in (0, 2, 1, 3):
+            load_scale_quadrant(boot_s[1], boot_scales[:, :, BANK : 2 * BANK], q, nc.sync)
+        nc.sync.dma_start(out=rlen_raw[:], in_=rlen.rearrange("(i p) -> i p", p=P))
+        nc.sync.dma_start(out=sig_raw[:, 2], in_=sig_view[:, 2])
+        nc.sync.dma_start(out=expo_raw[1][:], in_=expo_view[:, 2:4])
         cat_unit(0, 0)
         order_dev_words(1)
         order_dev_scales(1, FG, dev_s_rest)
@@ -332,6 +330,7 @@ def tile_bootstrap_signature_cosine_s12_kernel(
         expo_quant(0, BANK)
         sig_quant(2)
         expo_split(1)
+        nc.vector.tensor_copy(out=rlen_rows[0 : M // P, :], in_=rlen_raw[:])
         cat_piece(0, P)
         cat_unit(1, 1)
         for g in range(FG):
@@ -358,9 +357,9 @@ def tile_bootstrap_signature_cosine_s12_kernel(
         for i in range(3, 8):
             cat_piece(i * P, P)
         out_banks([0, 1, 2], BANK, BANK, "SSS")
-        for i in range(3, 8):
-            out_bank(i, 0, BANK, "V" if i > 5 else "S")
-            if i < 7:
-                out_bank(i, BANK, BANK, "S")
-        out_bank(7, BANK, PIECE, "S")
-        out_bank(7, BANK + PIECE, PIECE, "V")
+        for i in range(3, 6):
+            out_bank(i, 0, BANK, "S")
+            out_bank(i, BANK, BANK, "S")
+        for i in range(6, 8):
+            for q in range(4):
+                out_bank(i, q * PIECE, PIECE, "SV"[q % 2])

@@ -58,7 +58,6 @@ def tile_bootstrap_signature_cosine_s12_kernel(
         sig_c = keep.tile([P, F], U32, name="sig_c", align_bytes=64)
         sig_s = keep.tile([P, F], U8, name="sig_s", align_bytes=64)
         expo_raw = [keep.tile([P, 2, 2 * J], BF16, name="expo_raw%d" % h, align_bytes=64) for h in range(2)]
-        expo_uw = keep.tile([P, R // P, 2, P], F32, name="expo_uw", align_bytes=64)
         expo_t = keep.tile([P, R * PACK], BF16, name="expo_t", align_bytes=64)
         expo_c = keep.tile([P, R], U32, name="expo_c", align_bytes=64)
         expo_s = keep.tile([P, R], U8, name="expo_s", align_bytes=64)
@@ -192,18 +191,12 @@ def tile_bootstrap_signature_cosine_s12_kernel(
             n = slice(g * PASS, (g + 1) * PASS)
             nc.vector.quantize_mx(out=sig_c[:, n].bitcast(FP8X4), scales=sig_s[:, n], in_=staged[("sig", g)][:])
 
-        def expo_split(h):
-            tiles = slice(4 * h, 4 * h + 4)
-            nc.vector.tensor_copy(
-                out=expo_uw[:, tiles],
-                in_=expo_raw[h][:].bitcast(F32).rearrange("p b (i w u) -> p (b i) u w", i=2, u=2),
-            )
-
         def expo_bank(b, eng):
             bank = psum.tile([P, 2, 2, P], F32, name="expo_bank", tag="bank")
             for i in range(2):
                 for u in range(2):
-                    nc.tensor.transpose(bank[:, i, u, :], expo_uw[:, 2 * b + i, u, :], ident_f32[:])
+                    words = expo_raw[b // 2][:, b % 2, i * J : (i + 1) * J].bitcast(F32)
+                    nc.tensor.transpose(bank[:, i, u, :], words[:, u : J // 2 : 2], ident_f32[:])
             dst = expo_t[:, b * 2 * PASS : (b + 1) * 2 * PASS].bitcast(F32).rearrange("p (r i u) -> p r i u", i=2, u=2)
             src = bank[:].rearrange("p i u r -> p r i u")
             if eng == "S":
@@ -319,7 +312,6 @@ def tile_bootstrap_signature_cosine_s12_kernel(
         order_dev_words(2)
         sig_weave(0)
         cat_unit(0, 2)
-        expo_split(0)
         sig_quant(0)
         sig_weave(1)
         expo_bank(0, "V")
@@ -329,7 +321,6 @@ def tile_bootstrap_signature_cosine_s12_kernel(
         sig_weave(2)
         expo_quant(0, BANK)
         sig_quant(2)
-        expo_split(1)
         nc.vector.tensor_copy(out=rlen_rows[0 : M // P, :], in_=rlen_raw[:])
         cat_piece(0, P)
         cat_unit(1, 1)

@@ -23,7 +23,14 @@ BANK = 512
 KG = K // PASS
 FG = F // PASS
 RUN = 4
-PIECE = 256
+QUAD = 32
+SCALE_ROWS = 4
+QUADRANTS = (0, 2, 1, 3)
+M_TILES = M // P
+HALF_TILES = BANK // P
+SMALL_BANK = 256
+WARM_PASSES = 2
+ALIGN = 64
 
 
 def tile_bootstrap_signature_cosine_s12_kernel(
@@ -36,37 +43,34 @@ def tile_bootstrap_signature_cosine_s12_kernel(
         psum = ctx.enter_context(tc.psum_pool(name="psum", bufs=8))
         ctx.enter_context(tc.manual_schedule())
 
-        dev_w_raw = keep.tile([P, FG, KG, 2 * PASS], U8, name="dev_w_raw", align_bytes=64)
-        dev_s_first = keep.tile([P, KG, PASS], U8, name="dev_s_first", align_bytes=64)
-        dev_s_rest = keep.tile([P, KG, F - PASS], U8, name="dev_s_rest", align_bytes=64)
-        dev_w = keep.tile([P, FG, KG, 2 * PASS], U8, name="dev_w", align_bytes=64)
-        dev_s = keep.tile([P, FG, KG, PASS], U8, name="dev_s", align_bytes=64)
-        boot_w = keep.tile([P, 2, KG, 2 * BANK], U8, name="boot_w", align_bytes=64)
-        boot_s = [keep.tile([P, KG, BANK], U8, name="boot_s%d" % h, align_bytes=64) for h in range(2)]
-        base_raw = keep.tile([P, F // 4], BF16, name="base_raw", align_bytes=64)
-        base_rows = keep.tile([P, BANK], BF16, name="base_rows", align_bytes=64)
-        base_cols = keep.tile([P, BANK], BF16, name="base_cols", align_bytes=64)
-        rlen_raw = keep.tile([M // P, P], BF16, name="rlen_raw", align_bytes=64)
-        rlen_rows = keep.tile([P, P], F32, name="rlen_rows", align_bytes=64)
-        rlen_cols = keep.tile([P, M // P], F32, name="rlen_cols", align_bytes=64)
-        ident_f32 = keep.tile([P, P], F32, name="ident_f32", align_bytes=64)
-        zeros = keep.tile([P, PASS], BF16, name="zeros", align_bytes=64)
-        warm_c = keep.tile([P, BANK], U32, name="warm_c", align_bytes=64)
-        warm_s = keep.tile([P, BANK], U8, name="warm_s", align_bytes=64)
-        warm = keep.tile([P, 8], F32, name="warm", align_bytes=64)
-        sig_raw = keep.tile([P, FG, PACK, PASS], BF16, name="sig_raw", align_bytes=64)
-        sig_c = keep.tile([P, F], U32, name="sig_c", align_bytes=64)
-        sig_s = keep.tile([P, F], U8, name="sig_s", align_bytes=64)
-        expo_raw = [keep.tile([P, 2, 2 * J], BF16, name="expo_raw%d" % h, align_bytes=64) for h in range(2)]
-        expo_t = keep.tile([P, R * PACK], BF16, name="expo_t", align_bytes=64)
-        expo_c = keep.tile([P, R], U32, name="expo_c", align_bytes=64)
-        expo_s = keep.tile([P, R], U8, name="expo_s", align_bytes=64)
-        cat_rows = keep.tile([P, 2, FG, PACK, BANK], BF16, name="cat_rows", align_bytes=64)
-        cat_c = keep.tile([P, FG, M], U32, name="cat_c", align_bytes=64)
-        cat_s = keep.tile([P, FG, M], U8, name="cat_s", align_bytes=64)
-        mix_in = keep.tile([P, FG, R * PACK], BF16, name="mix_in", align_bytes=64)
-        mix_c = keep.tile([P, FG, R], U32, name="mix_c", align_bytes=64)
-        mix_s = keep.tile([P, FG, R], U8, name="mix_s", align_bytes=64)
+        dev_w_raw = keep.tile([P, FG, KG, 2 * PASS], U8, name="dev_w_raw", align_bytes=ALIGN)
+        dev_s_first = keep.tile([P, KG, PASS], U8, name="dev_s_first", align_bytes=ALIGN)
+        dev_s_rest = keep.tile([P, KG, F - PASS], U8, name="dev_s_rest", align_bytes=ALIGN)
+        dev_w = keep.tile([P, FG, KG, 2 * PASS], U8, name="dev_w", align_bytes=ALIGN)
+        dev_s = keep.tile([P, FG, KG, PASS], U8, name="dev_s", align_bytes=ALIGN)
+        boot_w = keep.tile([P, 2, KG, 2 * BANK], U8, name="boot_w", align_bytes=ALIGN)
+        boot_s = [keep.tile([P, KG, BANK], U8, name="boot_s%d" % h, align_bytes=ALIGN) for h in range(2)]
+        base_raw = keep.tile([P, F // 4], BF16, name="base_raw", align_bytes=ALIGN)
+        base_rows = keep.tile([P, BANK], BF16, name="base_rows", align_bytes=ALIGN)
+        base_cols = keep.tile([P, BANK], BF16, name="base_cols", align_bytes=ALIGN)
+        rlen_raw = keep.tile([M_TILES, P], BF16, name="rlen_raw", align_bytes=ALIGN)
+        rlen_rows = keep.tile([P, P], F32, name="rlen_rows", align_bytes=ALIGN)
+        rlen_cols = keep.tile([P, M_TILES], F32, name="rlen_cols", align_bytes=ALIGN)
+        ident_f32 = keep.tile([P, P], F32, name="ident_f32", align_bytes=ALIGN)
+        warm = keep.tile([P, 8], F32, name="warm", align_bytes=ALIGN)
+        sig_raw = keep.tile([P, FG, PACK, PASS], BF16, name="sig_raw", align_bytes=ALIGN)
+        sig_c = keep.tile([P, F], U32, name="sig_c", align_bytes=ALIGN)
+        sig_s = keep.tile([P, F], U8, name="sig_s", align_bytes=ALIGN)
+        expo_raw = [keep.tile([P, 2, 2 * J], BF16, name="expo_raw%d" % h, align_bytes=ALIGN) for h in range(2)]
+        expo_t = keep.tile([P, R * PACK], BF16, name="expo_t", align_bytes=ALIGN)
+        expo_c = keep.tile([P, R], U32, name="expo_c", align_bytes=ALIGN)
+        expo_s = keep.tile([P, R], U8, name="expo_s", align_bytes=ALIGN)
+        cat_rows = keep.tile([P, 2, FG, PACK, BANK], BF16, name="cat_rows", align_bytes=ALIGN)
+        cat_c = keep.tile([P, FG, M], U32, name="cat_c", align_bytes=ALIGN)
+        cat_s = keep.tile([P, FG, M], U8, name="cat_s", align_bytes=ALIGN)
+        mix_in = keep.tile([P, FG, R * PACK], BF16, name="mix_in", align_bytes=ALIGN)
+        mix_c = keep.tile([P, FG, R], U32, name="mix_c", align_bytes=ALIGN)
+        mix_s = keep.tile([P, FG, R], U8, name="mix_s", align_bytes=ALIGN)
 
         staged = {}
         sig_view = sig.rearrange("(p j) (g f) -> p g j f", j=PACK, f=PASS)
@@ -74,17 +78,16 @@ def tile_bootstrap_signature_cosine_s12_kernel(
         dev_view = dev_words.rearrange("k p (g n) -> p g k n", g=FG)
         boot_view = boot_words.rearrange("k p (h n) -> p h k n", h=2)
 
-        def load_bytes(dst, src, queue=nc.sync):
-            queue.dma_start(out=dst.bitcast(I32), in_=src.bitcast(I32))
+        def load_bytes(dst, src):
+            nc.sync.dma_start(out=dst.bitcast(I32), in_=src.bitcast(I32))
 
-        def load_scale_rows(dst, src, r):
-            load_bytes(dst[r:P:32], src.rearrange("k (q r) n -> r q k n", r=4)[r])
-
-        def load_scale_quadrant(dst, src, q, queue):
-            load_bytes(dst[32 * q : 32 * q + 4], src.rearrange("k (q r) n -> q r k n", r=4)[q], queue)
+        def load_scales(dst, src):
+            for q in QUADRANTS:
+                rows = slice(QUAD * q, QUAD * q + SCALE_ROWS)
+                load_bytes(dst[rows], src.rearrange("k (q r) n -> q r k n", r=SCALE_ROWS)[q])
 
         def order_first_dev_scales(q):
-            rows = slice(32 * q, 32 * q + 4)
+            rows = slice(QUAD * q, QUAD * q + SCALE_ROWS)
             nc.vector.tensor_copy(
                 out=dev_s[rows, 0].bitcast(I32).rearrange("p k (t a) -> p k t a", t=PACK),
                 in_=dev_s_first[rows].bitcast(I32).rearrange("p k (a t) -> p k t a", t=PACK),
@@ -96,10 +99,10 @@ def tile_bootstrap_signature_cosine_s12_kernel(
                 in_=dev_w_raw[:, g].bitcast(I32).rearrange("p k (a t w) -> p k t a w", t=PACK, w=2),
             )
 
-        def order_dev_scales(lo, hi, raw):
+        def order_other_dev_scales():
             nc.vector.tensor_copy(
-                out=dev_s[:, lo:hi].bitcast(I32).rearrange("p g k (t a) -> p k g t a", t=PACK),
-                in_=raw[:].bitcast(I32).rearrange("p k (g a t) -> p k g t a", g=hi - lo, t=PACK),
+                out=dev_s[:, 1:FG].bitcast(I32).rearrange("p g k (t a) -> p k g t a", t=PACK),
+                in_=dev_s_rest[:].bitcast(I32).rearrange("p k (g a t) -> p k g t a", g=FG - 1, t=PACK),
             )
 
         def clear(eng, plane):
@@ -114,55 +117,56 @@ def tile_bootstrap_signature_cosine_s12_kernel(
         def turn_base():
             nc.vector.transpose(base_cols[:], base_rows[:])
 
-        def warm_up(passes):
-            for q in range(PACK):
-                n = slice(q * P, (q + 1) * P)
-                nc.vector.quantize_mx(out=warm_c[:, n].bitcast(FP8X4), scales=warm_s[:, n], in_=zeros[:])
+        def warm_up_tensor():
             bank = psum.tile([P, BANK], F32, name="warm_bank", tag="bank")
-            for i in range(passes):
+            for _ in range(WARM_PASSES):
                 nc.tensor.matmul_mx(
                     out=bank[:],
-                    lhsT=warm_c[:, 0:P].bitcast(FP8X4),
-                    lhsT_scale=warm_s[:, 0:P],
-                    rhs=warm_c[:].bitcast(FP8X4),
-                    rhs_scale=warm_s[:],
+                    lhsT=dev_w_raw[:, 0, 0, 0 : 2 * P].bitcast(FP4X4),
+                    lhsT_scale=dev_s[:, 0, 0, 0:P],
+                    rhs=dev_w_raw[:, 0, 0, :].bitcast(FP4X4),
+                    rhs_scale=dev_s[:, 0, 0, :],
                     start=True,
                     stop=True,
                 )
 
+        def warm_up_scalar():
+            nc.vector.memset(warm[:], 0.0)
+            nc.scalar.activation(out=warm[:, 4:5], in_=warm[:, 0:1], func=ACT.Relu)
+
+        def copy_out(eng, dst, src):
+            if eng is nc.scalar:
+                nc.scalar.copy(out=dst, in_=src)
+            else:
+                nc.vector.tensor_copy(out=dst, in_=src)
+
         def turn_rlen():
             bank = psum.tile([P, P], F32, name="rlen_bank", tag="bank")
             nc.tensor.transpose(bank[:], rlen_rows[:], ident_f32[:])
-            nc.vector.tensor_copy(out=rlen_cols[:], in_=bank[:, 0 : M // P])
+            nc.vector.tensor_copy(out=rlen_cols[:], in_=bank[:, 0:M_TILES])
 
-        def cat_bank(h, g, t, eng):
-            bank = psum.tile([P, BANK], F32, name="cat_bank", tag="bank")
-            col = t * P
-            for k in range(KG):
-                nc.tensor.matmul_mx(
-                    out=bank[:],
-                    lhsT=dev_w[:, g, k, 2 * col : 2 * (col + P)].bitcast(FP4X4),
-                    lhsT_scale=dev_s[:, g, k, col : col + P],
-                    rhs=boot_w[:, h, k, :].bitcast(FP4X4),
-                    rhs_scale=boot_s[h][:, k, :],
-                    start=(k == 0),
-                    stop=(k == KG - 1),
-                )
-            bias = base_cols[:, 32 * (PACK * g + t) : 32 * (PACK * g + t) + 1]
-            if eng == "S":
-                nc.scalar.activation(out=cat_rows[:, h, g, t, :], in_=bank[:], func=ACT.Relu, bias=bias)
-            else:
-                nc.vector.tensor_scalar(
-                    out=cat_rows[:, h, g, t, :], in0=bank[:], scalar1=bias, scalar2=0.0, op0=ALU.add, op1=ALU.max
-                )
-
-        def cat_unit(h, g, engs="SSSS"):
+        def cat_unit(h, g):
             for t in range(PACK):
-                cat_bank(h, g, t, engs[t])
+                bank = psum.tile([P, BANK], F32, name="cat_bank", tag="bank")
+                col = t * P
+                for k in range(KG):
+                    nc.tensor.matmul_mx(
+                        out=bank[:],
+                        lhsT=dev_w[:, g, k, 2 * col : 2 * (col + P)].bitcast(FP4X4),
+                        lhsT_scale=dev_s[:, g, k, col : col + P],
+                        rhs=boot_w[:, h, k, :].bitcast(FP4X4),
+                        rhs_scale=boot_s[h][:, k, :],
+                        start=(k == 0),
+                        stop=(k == KG - 1),
+                    )
+                column = QUAD * (PACK * g + t)
+                nc.scalar.activation(
+                    out=cat_rows[:, h, g, t, :], in_=bank[:], func=ACT.Relu, bias=base_cols[:, column : column + 1]
+                )
 
         def cat_weave(g, lo, width):
             h, c = divmod(lo, BANK)
-            woven = ring.tile([P, width * PACK], BF16, name="woven", tag="woven", bufs=5, align_bytes=64)
+            woven = ring.tile([P, width * PACK], BF16, name="woven", tag="woven", bufs=5, align_bytes=ALIGN)
             nc.vector.tensor_copy(
                 out=woven[:].rearrange("p (c i t) -> p c t i", i=RUN, t=PACK),
                 in_=cat_rows[:, h, g, :, c : c + width].rearrange("p t (c i) -> p c t i", i=RUN),
@@ -173,14 +177,15 @@ def tile_bootstrap_signature_cosine_s12_kernel(
             n = slice(lo, lo + width)
             nc.vector.quantize_mx(out=cat_c[:, g, n].bitcast(FP8X4), scales=cat_s[:, g, n], in_=staged[("cat", g, lo)][:])
 
-        def cat_piece(lo, width):
+        def cat_piece(first, count):
+            lo, width = first * P, count * P
             for g in range(FG):
                 cat_weave(g, lo, width)
             for g in range(FG):
                 cat_quant(g, lo, width)
 
         def sig_weave(g):
-            woven = ring.tile([P, BANK * PACK], BF16, name="woven", tag="woven", bufs=5, align_bytes=64)
+            woven = ring.tile([P, BANK * PACK], BF16, name="woven", tag="woven", bufs=5, align_bytes=ALIGN)
             nc.vector.tensor_copy(
                 out=woven[:].rearrange("p (t a i j) -> p t a j i", t=PACK, i=RUN, j=PACK),
                 in_=sig_raw[:, g].rearrange("p j (a t i) -> p t a j i", t=PACK, i=RUN),
@@ -199,15 +204,12 @@ def tile_bootstrap_signature_cosine_s12_kernel(
                     nc.tensor.transpose(bank[:, i, u, :], words[:, u : J // 2 : 2], ident_f32[:])
             dst = expo_t[:, b * 2 * PASS : (b + 1) * 2 * PASS].bitcast(F32).rearrange("p (r i u) -> p r i u", i=2, u=2)
             src = bank[:].rearrange("p i u r -> p r i u")
-            if eng == "S":
-                nc.scalar.copy(out=dst, in_=src)
-            else:
-                nc.vector.tensor_copy(out=dst, in_=src)
+            copy_out(eng, dst, src)
 
-        def expo_quant(lo, width):
-            n = slice(lo, lo + width)
+        def expo_quant(h):
+            n = slice(h * BANK, (h + 1) * BANK)
             nc.vector.quantize_mx(
-                out=expo_c[:, n].bitcast(FP8X4), scales=expo_s[:, n], in_=expo_t[:, lo * PACK : (lo + width) * PACK]
+                out=expo_c[:, n].bitcast(FP8X4), scales=expo_s[:, n], in_=expo_t[:, n.start * PACK : n.stop * PACK]
             )
 
         def mix_bank(g, i, eng):
@@ -226,22 +228,26 @@ def tile_bootstrap_signature_cosine_s12_kernel(
                 )
             dst = mix_in[:, g, i * PASS : (i + 1) * PASS].rearrange("p (r t) -> p r t", t=PACK)
             src = bank[:].rearrange("p t r -> p r t")
-            if eng == "S":
-                nc.scalar.copy(out=dst, in_=src)
-            else:
-                nc.vector.tensor_copy(out=dst, in_=src)
+            copy_out(eng, dst, src)
 
-        def mix_quant(g, lo, width):
-            n = slice(lo, lo + width)
+        def mix_quant(g, h):
+            n = slice(h * BANK, (h + 1) * BANK)
             nc.vector.quantize_mx(
                 out=mix_c[:, g, n].bitcast(FP8X4),
                 scales=mix_s[:, g, n],
-                in_=mix_in[:, g, lo * PACK : (lo + width) * PACK],
+                in_=mix_in[:, g, n.start * PACK : n.stop * PACK],
             )
 
-        def out_banks(tiles, lo, width, engs):
+        def mix_half(h, engines_of):
+            for g in range(FG):
+                for i in range(HALF_TILES):
+                    mix_bank(g, h * HALF_TILES + i, engines_of(g)[i % 2])
+                if g > 0:
+                    mix_quant(g - 1, h)
+
+        def out_banks(tiles, lo, width, eng):
             n = slice(lo, lo + width)
-            banks = [psum.tile([P, width], F32, name="out_bank", tag="bank") for i in tiles]
+            banks = [psum.tile([P, width], F32, name="out_bank", tag="bank") for _ in tiles]
             for g in range(FG):
                 for i, bank in zip(tiles, banks):
                     m = slice(i * P, (i + 1) * P)
@@ -254,103 +260,96 @@ def tile_bootstrap_signature_cosine_s12_kernel(
                         start=(g == 0),
                         stop=(g == FG - 1),
                     )
-            for i, bank, eng in zip(tiles, banks, engs):
+            for i, bank in zip(tiles, banks):
                 result = ring.tile([P, width], F32, name="result", tag="result", bufs=10)
                 factor = rlen_cols[:, i : i + 1]
-                if eng == "S":
+                if eng is nc.scalar:
                     nc.scalar.activation(out=result[:], in_=bank[:], func=ACT.Copy, scale=factor)
                 else:
                     nc.vector.tensor_scalar(out=result[:], in0=bank[:], scalar1=factor, scalar2=None, op0=ALU.mult)
                 nc.sync.dma_start(out=out[i * P : (i + 1) * P, n], in_=result[:])
 
-        def out_bank(i, lo, width, eng):
-            out_banks([i], lo, width, eng)
+        in_turn = (nc.vector, nc.scalar)
+        scalar_only = (nc.scalar, nc.scalar)
 
         nc.vector.memset(base_raw[:], 0.0)
         clear(nc.vector, boot_s[0][:])
-        nc.gpsimd.memset(zeros[:], 0.0)
-        nc.vector.memset(warm[:], 0.0)
+        warm_up_scalar()
         nc.vector.memset(base_rows[:, F // 4 : BANK], 0.0)
         clear(nc.gpsimd, dev_s[:, 0])
-        warm_up(4)
         clear(nc.gpsimd, dev_s_rest[:])
         make_identity(nc, ident_f32[:])
-        nc.scalar.activation(out=warm[:, 4:5], in_=warm[:, 0:1], func=ACT.Relu)
-        for q in (0, 2, 1, 3):
-            load_scale_quadrant(dev_s_first, dev_scales[:, :, 0:PASS], q, nc.sync)
+
+        load_scales(dev_s_first, dev_scales[:, :, 0:PASS])
         load_bytes(dev_w_raw[:, 0], dev_view[:, 0])
         load_bytes(boot_w[:, 0], boot_view[:, 0])
         nc.sync.dma_start(
-            out=base_raw[0:P:32, :].rearrange("q (g c) -> q g c", g=FG), in_=base.rearrange("(g q c) -> q g c", g=FG, q=4)
+            out=base_raw[0:P:QUAD, :].rearrange("q (g c) -> q g c", g=FG),
+            in_=base.rearrange("(g q c) -> q g c", g=FG, q=P // QUAD),
         )
-        for q in (0, 2, 1, 3):
-            load_scale_quadrant(boot_s[0], boot_scales[:, :, 0:BANK], q, nc.sync)
+        load_scales(boot_s[0], boot_scales[:, :, 0:BANK])
         load_bytes(dev_w_raw[:, 1], dev_view[:, 1])
-        for q in (0, 2, 1, 3):
-            load_scale_quadrant(dev_s_rest, dev_scales[:, :, PASS:F], q, nc.sync)
+        load_scales(dev_s_rest, dev_scales[:, :, PASS:F])
         load_bytes(dev_w_raw[:, 2], dev_view[:, 2])
         nc.sync.dma_start(out=sig_raw[:, 0], in_=sig_view[:, 0])
         nc.sync.dma_start(out=expo_raw[0][:], in_=expo_view[:, 0:2])
         nc.sync.dma_start(out=sig_raw[:, 1], in_=sig_view[:, 1])
         load_bytes(boot_w[:, 1], boot_view[:, 1])
-        for q in (0, 2, 1, 3):
+
+        for q in QUADRANTS:
             order_first_dev_scales(q)
+        warm_up_tensor()
         order_dev_words(0)
         order_base()
         turn_base()
         clear(nc.vector, boot_s[1][:])
         nc.vector.memset(rlen_rows[:], 0.0)
-        for q in (0, 2, 1, 3):
-            load_scale_quadrant(boot_s[1], boot_scales[:, :, BANK : 2 * BANK], q, nc.sync)
+        load_scales(boot_s[1], boot_scales[:, :, BANK : 2 * BANK])
         nc.sync.dma_start(out=rlen_raw[:], in_=rlen.rearrange("(i p) -> i p", p=P))
         nc.sync.dma_start(out=sig_raw[:, 2], in_=sig_view[:, 2])
         nc.sync.dma_start(out=expo_raw[1][:], in_=expo_view[:, 2:4])
+
         cat_unit(0, 0)
         order_dev_words(1)
-        order_dev_scales(1, FG, dev_s_rest)
+        order_other_dev_scales()
         cat_unit(0, 1)
         order_dev_words(2)
         sig_weave(0)
         cat_unit(0, 2)
         sig_quant(0)
         sig_weave(1)
-        expo_bank(0, "V")
-        expo_bank(1, "S")
+        for b in range(2):
+            expo_bank(b, in_turn[b])
         sig_quant(1)
         cat_unit(1, 0)
         sig_weave(2)
-        expo_quant(0, BANK)
+        expo_quant(0)
         sig_quant(2)
-        nc.vector.tensor_copy(out=rlen_rows[0 : M // P, :], in_=rlen_raw[:])
-        cat_piece(0, P)
+        nc.vector.tensor_copy(out=rlen_rows[0:M_TILES, :], in_=rlen_raw[:])
+        cat_piece(0, 1)
         cat_unit(1, 1)
-        for g in range(FG):
-            for i in range(4):
-                mix_bank(g, i, "VSVS"[i])
-            if g > 0:
-                mix_quant(g - 1, 0, BANK)
-        expo_bank(2, "S")
-        expo_bank(3, "S")
+
+        mix_half(0, lambda g: in_turn)
+        for b in range(2, 4):
+            expo_bank(b, nc.scalar)
         turn_rlen()
-        mix_quant(2, 0, BANK)
+        mix_quant(FG - 1, 0)
         cat_unit(1, 2)
-        expo_quant(BANK, BANK)
-        cat_piece(P, 2 * P)
-        out_bank(0, 0, BANK, "S")
-        for g in range(FG):
-            for i in range(4, 8):
-                mix_bank(g, i, ("SSSS", "VSVS", "VSVS")[g][i - 4])
-            if g > 0:
-                mix_quant(g - 1, BANK, BANK)
-        out_bank(1, 0, BANK, "S")
-        mix_quant(2, BANK, BANK)
-        out_bank(2, 0, BANK, "S")
-        for i in range(3, 8):
-            cat_piece(i * P, P)
-        out_banks([0, 1, 2], BANK, BANK, "SSS")
-        for i in range(3, 6):
-            out_bank(i, 0, BANK, "S")
-            out_bank(i, BANK, BANK, "S")
-        for i in range(6, 8):
-            for q in range(4):
-                out_bank(i, q * PIECE, PIECE, "SV"[q % 2])
+        expo_quant(1)
+
+        cat_piece(1, 2)
+        out_banks([0], 0, BANK, nc.scalar)
+        mix_half(1, lambda g: in_turn if g > 0 else scalar_only)
+        out_banks([1], 0, BANK, nc.scalar)
+        mix_quant(FG - 1, 1)
+        out_banks([2], 0, BANK, nc.scalar)
+
+        for i in range(3, M_TILES):
+            cat_piece(i, 1)
+        out_banks([0, 1, 2], BANK, BANK, nc.scalar)
+        for i in range(3, M_TILES - 2):
+            for lo in range(0, R, BANK):
+                out_banks([i], lo, BANK, nc.scalar)
+        for i in range(M_TILES - 2, M_TILES):
+            for q in range(R // SMALL_BANK):
+                out_banks([i], q * SMALL_BANK, SMALL_BANK, in_turn[(q + 1) % 2])

@@ -89,8 +89,8 @@ def tile_bootstrap_signature_cosine_s12_kernel(
         def order_first_dev_scales(q):
             rows = slice(QUAD * q, QUAD * q + SCALE_ROWS)
             nc.vector.tensor_copy(
-                out=dev_s[rows, 0].bitcast(I32).rearrange("p k (t a) -> p k t a", t=PACK),
-                in_=dev_s_first[rows].bitcast(I32).rearrange("p k (a t) -> p k t a", t=PACK),
+                out=dev_s[rows, 0].bitcast(I32).rearrange("p k (t a) -> p k a t", t=PACK),
+                in_=dev_s_first[rows].bitcast(I32).rearrange("p k (a t) -> p k a t", t=PACK),
             )
 
         def order_dev_words(g):
@@ -101,8 +101,8 @@ def tile_bootstrap_signature_cosine_s12_kernel(
 
         def order_other_dev_scales():
             nc.vector.tensor_copy(
-                out=dev_s[:, 1:FG].bitcast(I32).rearrange("p g k (t a) -> p k g t a", t=PACK),
-                in_=dev_s_rest[:].bitcast(I32).rearrange("p k (g a t) -> p k g t a", g=FG - 1, t=PACK),
+                out=dev_s[:, 1:FG].bitcast(I32).rearrange("p g k (t a) -> p k g a t", t=PACK),
+                in_=dev_s_rest[:].bitcast(I32).rearrange("p k (g a t) -> p k g a t", g=FG - 1, t=PACK),
             )
 
         def clear(eng, plane):

@@ -29,7 +29,7 @@ QUADRANTS = (0, 2, 1, 3)
 M_TILES = M // P
 HALF_TILES = BANK // P
 SMALL_BANK = 256
-WARM_PASSES = 2
+EXPO_BANKS = R // (2 * P)
 ALIGN = 64
 
 
@@ -45,16 +45,23 @@ def tile_bootstrap_signature_cosine_s12_kernel(
 
         dev_w_raw = keep.tile([P, FG, KG, 2 * PASS], U8, name="dev_w_raw", align_bytes=ALIGN)
         dev_s_first = keep.tile([P, KG, PASS], U8, name="dev_s_first", align_bytes=ALIGN)
-        dev_s_rest = keep.tile([P, KG, F - PASS], U8, name="dev_s_rest", align_bytes=ALIGN)
+        cleared = keep.tile([P, 4 * KG * BANK], U8, name="cleared", align_bytes=ALIGN)
+        plane = KG * BANK
+        boot_s_first = cleared[:, 0:plane].rearrange("p (k n) -> p k n", k=KG)
+        dev_s_head = cleared[:, plane : 2 * plane].rearrange("p (k n) -> p k n", k=KG)
+        dev_s_rest = cleared[:, 2 * plane : 4 * plane].rearrange("p (k n) -> p k n", k=KG)
+        zero_c = keep.tile([P, BANK], U32, name="zero_c", align_bytes=ALIGN)
+        zero_s = keep.tile([P, BANK], U8, name="zero_s", align_bytes=ALIGN)
         dev_w = keep.tile([P, FG, KG, 2 * PASS], U8, name="dev_w", align_bytes=ALIGN)
-        dev_s = keep.tile([P, FG, KG, PASS], U8, name="dev_s", align_bytes=ALIGN)
+        dev_s_tail = keep.tile([P, FG - 1, KG, PASS], U8, name="dev_s_tail", align_bytes=ALIGN)
+        dev_s = [dev_s_head] + [dev_s_tail[:, g] for g in range(FG - 1)]
         boot_w = keep.tile([P, 2, KG, 2 * BANK], U8, name="boot_w", align_bytes=ALIGN)
-        boot_s = [keep.tile([P, KG, BANK], U8, name="boot_s%d" % h, align_bytes=ALIGN) for h in range(2)]
+        boot_s_second = keep.tile([P, KG, BANK], U8, name="boot_s_second", align_bytes=ALIGN)
+        boot_s = [boot_s_first, boot_s_second[:]]
         base_raw = keep.tile([P, F // 4], BF16, name="base_raw", align_bytes=ALIGN)
         base_rows = keep.tile([P, BANK], BF16, name="base_rows", align_bytes=ALIGN)
         base_cols = keep.tile([P, BANK], BF16, name="base_cols", align_bytes=ALIGN)
-        rlen_raw = keep.tile([M_TILES, P], BF16, name="rlen_raw", align_bytes=ALIGN)
-        rlen_rows = keep.tile([P, P], F32, name="rlen_rows", align_bytes=ALIGN)
+        rlen_raw = keep.tile([P, M_TILES, 2], BF16, name="rlen_raw", align_bytes=ALIGN)
         rlen_cols = keep.tile([P, M_TILES], F32, name="rlen_cols", align_bytes=ALIGN)
         ident_f32 = keep.tile([P, P], F32, name="ident_f32", align_bytes=ALIGN)
         warm = keep.tile([P, 8], F32, name="warm", align_bytes=ALIGN)
@@ -62,6 +69,7 @@ def tile_bootstrap_signature_cosine_s12_kernel(
         sig_c = keep.tile([P, F], U32, name="sig_c", align_bytes=ALIGN)
         sig_s = keep.tile([P, F], U8, name="sig_s", align_bytes=ALIGN)
         expo_raw = [keep.tile([P, 2, 2 * J], BF16, name="expo_raw%d" % h, align_bytes=ALIGN) for h in range(2)]
+        expo_sorted = keep.tile([P, 2, 2, 2, 2, P], F32, name="expo_sorted", align_bytes=ALIGN)
         expo_t = keep.tile([P, R * PACK], BF16, name="expo_t", align_bytes=ALIGN)
         expo_c = keep.tile([P, R], U32, name="expo_c", align_bytes=ALIGN)
         expo_s = keep.tile([P, R], U8, name="expo_s", align_bytes=ALIGN)
@@ -89,7 +97,7 @@ def tile_bootstrap_signature_cosine_s12_kernel(
         def order_first_dev_scales(q):
             rows = slice(QUAD * q, QUAD * q + SCALE_ROWS)
             nc.vector.tensor_copy(
-                out=dev_s[rows, 0].bitcast(I32).rearrange("p k (t a) -> p k a t", t=PACK),
+                out=dev_s_head[rows].bitcast(I32).rearrange("p k (t a) -> p k a t", t=PACK),
                 in_=dev_s_first[rows].bitcast(I32).rearrange("p k (a t) -> p k a t", t=PACK),
             )
 
@@ -101,8 +109,8 @@ def tile_bootstrap_signature_cosine_s12_kernel(
 
         def order_other_dev_scales():
             nc.vector.tensor_copy(
-                out=dev_s[:, 1:FG].bitcast(I32).rearrange("p g k (t a) -> p k g a t", t=PACK),
-                in_=dev_s_rest[:].bitcast(I32).rearrange("p k (g a t) -> p k g a t", g=FG - 1, t=PACK),
+                out=dev_s_tail[:].bitcast(I32).rearrange("p g k (t a) -> p k g a t", t=PACK),
+                in_=dev_s_rest.bitcast(I32).rearrange("p k (g a t) -> p k g a t", g=FG - 1, t=PACK),
             )
 
         def clear(eng, plane):
@@ -117,15 +125,15 @@ def tile_bootstrap_signature_cosine_s12_kernel(
         def turn_base():
             nc.vector.transpose(base_cols[:], base_rows[:])
 
-        def warm_up_tensor():
+        def warm_up_tensor(passes):
             bank = psum.tile([P, BANK], F32, name="warm_bank", tag="bank")
-            for _ in range(WARM_PASSES):
+            for _ in range(passes):
                 nc.tensor.matmul_mx(
                     out=bank[:],
-                    lhsT=dev_w_raw[:, 0, 0, 0 : 2 * P].bitcast(FP4X4),
-                    lhsT_scale=dev_s[:, 0, 0, 0:P],
-                    rhs=dev_w_raw[:, 0, 0, :].bitcast(FP4X4),
-                    rhs_scale=dev_s[:, 0, 0, :],
+                    lhsT=zero_c[:, 0:P].bitcast(FP8X4),
+                    lhsT_scale=zero_s[:, 0:P],
+                    rhs=zero_c[:].bitcast(FP8X4),
+                    rhs_scale=zero_s[:],
                     start=True,
                     stop=True,
                 )
@@ -140,29 +148,38 @@ def tile_bootstrap_signature_cosine_s12_kernel(
             else:
                 nc.vector.tensor_copy(out=dst, in_=src)
 
-        def turn_rlen():
-            bank = psum.tile([P, P], F32, name="rlen_bank", tag="bank")
-            nc.tensor.transpose(bank[:], rlen_rows[:], ident_f32[:])
-            nc.vector.tensor_copy(out=rlen_cols[:], in_=bank[:, 0:M_TILES])
+        def load_rlen():
+            with nc.allow_non_contiguous_dma(reason="one factor to a partition and tile"):
+                nc.sync.dma_start(out=rlen_raw[:, :, 0:1], in_=rlen.rearrange("(i p o) -> p i o", p=P, o=1))
+
+        def widen_rlen():
+            nc.vector.tensor_copy(out=rlen_cols[:], in_=rlen_raw[:, :, 0])
+
+        def cat_bank(h, g, t, eng):
+            bank = psum.tile([P, BANK], F32, name="cat_bank", tag="bank")
+            col = t * P
+            for k in range(KG):
+                nc.tensor.matmul_mx(
+                    out=bank[:],
+                    lhsT=dev_w[:, g, k, 2 * col : 2 * (col + P)].bitcast(FP4X4),
+                    lhsT_scale=dev_s[g][:, k, col : col + P],
+                    rhs=boot_w[:, h, k, :].bitcast(FP4X4),
+                    rhs_scale=boot_s[h][:, k, :],
+                    start=(k == 0),
+                    stop=(k == KG - 1),
+                )
+            column = QUAD * (PACK * g + t)
+            bias = base_cols[:, column : column + 1]
+            if eng is nc.scalar:
+                nc.scalar.activation(out=cat_rows[:, h, g, t, :], in_=bank[:], func=ACT.Relu, bias=bias)
+            else:
+                nc.vector.tensor_scalar(
+                    out=cat_rows[:, h, g, t, :], in0=bank[:], scalar1=bias, scalar2=0.0, op0=ALU.add, op1=ALU.max
+                )
 
         def cat_unit(h, g):
             for t in range(PACK):
-                bank = psum.tile([P, BANK], F32, name="cat_bank", tag="bank")
-                col = t * P
-                for k in range(KG):
-                    nc.tensor.matmul_mx(
-                        out=bank[:],
-                        lhsT=dev_w[:, g, k, 2 * col : 2 * (col + P)].bitcast(FP4X4),
-                        lhsT_scale=dev_s[:, g, k, col : col + P],
-                        rhs=boot_w[:, h, k, :].bitcast(FP4X4),
-                        rhs_scale=boot_s[h][:, k, :],
-                        start=(k == 0),
-                        stop=(k == KG - 1),
-                    )
-                column = QUAD * (PACK * g + t)
-                nc.scalar.activation(
-                    out=cat_rows[:, h, g, t, :], in_=bank[:], func=ACT.Relu, bias=base_cols[:, column : column + 1]
-                )
+                cat_bank(h, g, t, nc.scalar)
 
         def cat_weave(g, lo, width):
             h, c = divmod(lo, BANK)
@@ -196,18 +213,23 @@ def tile_bootstrap_signature_cosine_s12_kernel(
             n = slice(g * PASS, (g + 1) * PASS)
             nc.vector.quantize_mx(out=sig_c[:, n].bitcast(FP8X4), scales=sig_s[:, n], in_=staged[("sig", g)][:])
 
+        def expo_sort(h):
+            nc.vector.tensor_copy(
+                out=expo_sorted[:, h].rearrange("p b i u w -> p (b i) u w"),
+                in_=expo_raw[h][:].bitcast(F32).rearrange("p b (i w u) -> p (b i) u w", i=2, u=2),
+            )
+
         def expo_bank(b, eng):
             bank = psum.tile([P, 2, 2, P], F32, name="expo_bank", tag="bank")
             for i in range(2):
                 for u in range(2):
-                    words = expo_raw[b // 2][:, b % 2, i * J : (i + 1) * J].bitcast(F32)
-                    nc.tensor.transpose(bank[:, i, u, :], words[:, u : J // 2 : 2], ident_f32[:])
+                    nc.tensor.transpose(bank[:, i, u, :], expo_sorted[:, b // 2, b % 2, i, u, :], ident_f32[:])
             dst = expo_t[:, b * 2 * PASS : (b + 1) * 2 * PASS].bitcast(F32).rearrange("p (r i u) -> p r i u", i=2, u=2)
             src = bank[:].rearrange("p i u r -> p r i u")
             copy_out(eng, dst, src)
 
-        def expo_quant(h):
-            n = slice(h * BANK, (h + 1) * BANK)
+        def expo_quant(first, count):
+            n = slice(first * 2 * P, (first + count) * 2 * P)
             nc.vector.quantize_mx(
                 out=expo_c[:, n].bitcast(FP8X4), scales=expo_s[:, n], in_=expo_t[:, n.start * PACK : n.stop * PACK]
             )
@@ -238,13 +260,6 @@ def tile_bootstrap_signature_cosine_s12_kernel(
                 in_=mix_in[:, g, n.start * PACK : n.stop * PACK],
             )
 
-        def mix_half(h, engines_of):
-            for g in range(FG):
-                for i in range(HALF_TILES):
-                    mix_bank(g, h * HALF_TILES + i, engines_of(g)[i % 2])
-                if g > 0:
-                    mix_quant(g - 1, h)
-
         def out_banks(tiles, lo, width, eng):
             n = slice(lo, lo + width)
             banks = [psum.tile([P, width], F32, name="out_bank", tag="bank") for _ in tiles]
@@ -269,15 +284,14 @@ def tile_bootstrap_signature_cosine_s12_kernel(
                     nc.vector.tensor_scalar(out=result[:], in0=bank[:], scalar1=factor, scalar2=None, op0=ALU.mult)
                 nc.sync.dma_start(out=out[i * P : (i + 1) * P, n], in_=result[:])
 
-        in_turn = (nc.vector, nc.scalar)
-        scalar_only = (nc.scalar, nc.scalar)
+        V, S = nc.vector, nc.scalar
 
-        nc.vector.memset(base_raw[:], 0.0)
-        clear(nc.vector, boot_s[0][:])
+        nc.vector.memset(cleared[:].bitcast(I32), 0)
         warm_up_scalar()
+        nc.vector.memset(base_raw[:], 0.0)
         nc.vector.memset(base_rows[:, F // 4 : BANK], 0.0)
-        clear(nc.gpsimd, dev_s[:, 0])
-        clear(nc.gpsimd, dev_s_rest[:])
+        nc.vector.quantize_mx(out=zero_c[:].bitcast(FP8X4), scales=zero_s[:], in_=cleared[:].bitcast(BF16))
+        clear(nc.vector, boot_s[1])
         make_identity(nc, ident_f32[:])
 
         load_scales(dev_s_first, dev_scales[:, :, 0:PASS])
@@ -288,68 +302,116 @@ def tile_bootstrap_signature_cosine_s12_kernel(
             in_=base.rearrange("(g q c) -> q g c", g=FG, q=P // QUAD),
         )
         load_scales(boot_s[0], boot_scales[:, :, 0:BANK])
+        nc.sync.dma_start(out=sig_raw[:, 0], in_=sig_view[:, 0])
+        load_bytes(boot_w[:, 1], boot_view[:, 1])
+        load_scales(boot_s[1], boot_scales[:, :, BANK : 2 * BANK])
+        for h in range(2):
+            nc.sync.dma_start(out=expo_raw[h][:], in_=expo_view[:, 2 * h : 2 * h + 2])
         load_bytes(dev_w_raw[:, 1], dev_view[:, 1])
         load_scales(dev_s_rest, dev_scales[:, :, PASS:F])
         load_bytes(dev_w_raw[:, 2], dev_view[:, 2])
-        nc.sync.dma_start(out=sig_raw[:, 0], in_=sig_view[:, 0])
-        nc.sync.dma_start(out=expo_raw[0][:], in_=expo_view[:, 0:2])
         nc.sync.dma_start(out=sig_raw[:, 1], in_=sig_view[:, 1])
-        load_bytes(boot_w[:, 1], boot_view[:, 1])
+        nc.sync.dma_start(out=sig_raw[:, 2], in_=sig_view[:, 2])
+        load_rlen()
 
+        warm_up_tensor(4)
         for q in QUADRANTS:
             order_first_dev_scales(q)
-        warm_up_tensor()
         order_dev_words(0)
         order_base()
         turn_base()
-        clear(nc.vector, boot_s[1][:])
-        nc.vector.memset(rlen_rows[:], 0.0)
-        load_scales(boot_s[1], boot_scales[:, :, BANK : 2 * BANK])
-        nc.sync.dma_start(out=rlen_raw[:], in_=rlen.rearrange("(i p) -> i p", p=P))
-        nc.sync.dma_start(out=sig_raw[:, 2], in_=sig_view[:, 2])
-        nc.sync.dma_start(out=expo_raw[1][:], in_=expo_view[:, 2:4])
 
-        cat_unit(0, 0)
+        for t in range(PACK - 1):
+            cat_bank(0, 0, t, S)
+        sig_weave(0)
+        cat_bank(0, 0, PACK - 1, V)
+        cat_unit(1, 0)
+        expo_sort(0)
+        sig_quant(0)
+        expo_sort(1)
         order_dev_words(1)
         order_other_dev_scales()
-        cat_unit(0, 1)
+        for b in range(EXPO_BANKS):
+            expo_bank(b, S)
         order_dev_words(2)
-        sig_weave(0)
-        cat_unit(0, 2)
-        sig_quant(0)
+        cat_weave(0, 0, 2 * P)
+        cat_unit(0, 1)
+        expo_quant(0, 2)
         sig_weave(1)
-        for b in range(2):
-            expo_bank(b, in_turn[b])
+        cat_quant(0, 0, 2 * P)
+
         sig_quant(1)
-        cat_unit(1, 0)
+        cat_bank(0, 2, 0, S)
+        mix_bank(0, 0, V)
+        cat_bank(0, 2, 1, S)
+        mix_bank(0, 1, V)
         sig_weave(2)
-        expo_quant(0)
+        cat_bank(0, 2, 2, S)
+        mix_bank(0, 2, S)
+        cat_bank(0, 2, 3, S)
+        mix_bank(0, 3, V)
         sig_quant(2)
-        nc.vector.tensor_copy(out=rlen_rows[0:M_TILES, :], in_=rlen_raw[:])
-        cat_piece(0, 1)
-        cat_unit(1, 1)
 
-        mix_half(0, lambda g: in_turn)
-        for b in range(2, 4):
-            expo_bank(b, nc.scalar)
-        turn_rlen()
-        mix_quant(FG - 1, 0)
-        cat_unit(1, 2)
-        expo_quant(1)
+        cat_bank(1, 1, 0, S)
+        mix_bank(1, 0, V)
+        mix_quant(0, 0)
+        cat_bank(1, 1, 1, S)
+        mix_bank(1, 1, S)
+        cat_weave(1, 0, 2 * P)
+        cat_bank(1, 1, 2, S)
+        mix_bank(1, 2, V)
+        cat_quant(1, 0, 2 * P)
+        cat_weave(2, 0, 2 * P)
+        cat_bank(1, 1, 3, S)
+        mix_bank(1, 3, S)
+        expo_quant(2, 2)
+        cat_quant(2, 0, 2 * P)
 
-        cat_piece(1, 2)
-        out_banks([0], 0, BANK, nc.scalar)
-        mix_half(1, lambda g: in_turn if g > 0 else scalar_only)
-        out_banks([1], 0, BANK, nc.scalar)
-        mix_quant(FG - 1, 1)
-        out_banks([2], 0, BANK, nc.scalar)
+        mix_bank(2, 0, S)
+        mix_quant(1, 0)
+        mix_bank(2, 1, S)
+        cat_bank(1, 2, 0, S)
+        mix_bank(2, 2, V)
+        widen_rlen()
+        for g in range(FG):
+            cat_weave(g, 2 * P, P)
+        cat_bank(1, 2, 1, S)
+        mix_bank(2, 3, S)
+        cat_bank(1, 2, 2, S)
+        cat_bank(1, 2, 3, S)
+        mix_quant(2, 0)
 
-        for i in range(3, M_TILES):
+        mix_bank(0, 4, V)
+        mix_bank(0, 5, V)
+        mix_bank(0, 6, S)
+        mix_bank(0, 7, S)
+        for g in range(FG):
+            cat_quant(g, 2 * P, P)
+        mix_bank(1, 4, V)
+        mix_bank(1, 5, S)
+        out_banks([0], 0, BANK, S)
+        mix_quant(0, 1)
+        mix_bank(1, 6, V)
+        mix_bank(1, 7, S)
+        cat_weave(0, 3 * P, P)
+        mix_bank(2, 4, S)
+        out_banks([1], 0, BANK, S)
+        mix_quant(1, 1)
+        mix_bank(2, 5, V)
+        mix_bank(2, 6, S)
+        mix_bank(2, 7, S)
+        cat_weave(1, 3 * P, P)
+        cat_weave(2, 3 * P, P)
+        mix_quant(2, 1)
+        for g in range(FG):
+            cat_quant(g, 3 * P, P)
+        out_banks([2], 0, BANK, S)
+        for i in range(4, M_TILES):
             cat_piece(i, 1)
-        out_banks([0, 1, 2], BANK, BANK, nc.scalar)
+        out_banks([0, 1, 2], BANK, BANK, S)
         for i in range(3, M_TILES - 2):
             for lo in range(0, R, BANK):
-                out_banks([i], lo, BANK, nc.scalar)
+                out_banks([i], lo, BANK, S)
         for i in range(M_TILES - 2, M_TILES):
             for q in range(R // SMALL_BANK):
-                out_banks([i], q * SMALL_BANK, SMALL_BANK, in_turn[(q + 1) % 2])
+                out_banks([i], q * SMALL_BANK, SMALL_BANK, (S, V)[q % 2])

@@ -341,47 +341,29 @@ def tile_bootstrap_signature_cosine_s12_kernel(
         cat_quant(0, 0, 2 * P)
 
         sig_quant(1)
-        cat_bank(0, 2, 0, S)
-        mix_bank(0, 0, V)
-        cat_bank(0, 2, 1, S)
-        mix_bank(0, 1, V)
+        cat_unit(0, 2)
         sig_weave(2)
-        cat_bank(0, 2, 2, S)
-        mix_bank(0, 2, S)
-        cat_bank(0, 2, 3, S)
-        mix_bank(0, 3, V)
-        sig_quant(2)
-
-        cat_bank(1, 1, 0, S)
-        mix_bank(1, 0, V)
-        mix_quant(0, 0)
-        cat_bank(1, 1, 1, S)
-        mix_bank(1, 1, S)
         cat_weave(1, 0, 2 * P)
-        cat_bank(1, 1, 2, S)
-        mix_bank(1, 2, V)
+        sig_quant(2)
         cat_quant(1, 0, 2 * P)
+        cat_unit(1, 1)
         cat_weave(2, 0, 2 * P)
-        cat_bank(1, 1, 3, S)
-        mix_bank(1, 3, S)
         expo_quant(2, 2)
         cat_quant(2, 0, 2 * P)
-
-        mix_bank(2, 0, S)
+        for i in range(4):
+            mix_bank(0, i, (V, V, S, V)[i])
+        for i in range(4):
+            mix_bank(1, i, (S, V, S, V)[i])
+        for i in range(4):
+            mix_bank(2, i, (S, V, S, V)[i])
+        mix_quant(0, 0)
+        cat_unit(1, 2)
         mix_quant(1, 0)
-        mix_bank(2, 1, S)
-        cat_bank(1, 2, 0, S)
-        mix_bank(2, 2, V)
+        mix_quant(2, 0)
         widen_rlen()
         for g in range(FG):
             cat_weave(g, 2 * P, P)
-        cat_bank(1, 2, 1, S)
-        mix_bank(2, 3, S)
-        cat_bank(1, 2, 2, S)
-        cat_bank(1, 2, 3, S)
-        mix_quant(2, 0)
-
-        mix_bank(0, 4, V)
+        mix_bank(0, 4, S)
         mix_bank(0, 5, V)
         mix_bank(0, 6, S)
         mix_bank(0, 7, S)

@@ -30,6 +30,7 @@ M_TILES = M // P
 HALF_TILES = BANK // P
 SMALL_BANK = 256
 EXPO_BANKS = R // (2 * P)
+WARM_N = 512
 ALIGN = 64
 
 
@@ -45,22 +46,19 @@ def tile_bootstrap_signature_cosine_s12_kernel(
 
         dev_w_raw = keep.tile([P, FG, KG, 2 * PASS], U8, name="dev_w_raw", align_bytes=ALIGN)
         dev_s_first = keep.tile([P, KG, PASS], U8, name="dev_s_first", align_bytes=ALIGN)
-        cleared = keep.tile([P, 4 * KG * BANK], U8, name="cleared", align_bytes=ALIGN)
-        plane = KG * BANK
-        boot_s_first = cleared[:, 0:plane].rearrange("p (k n) -> p k n", k=KG)
-        dev_s_head = cleared[:, plane : 2 * plane].rearrange("p (k n) -> p k n", k=KG)
-        dev_s_rest = cleared[:, 2 * plane : 4 * plane].rearrange("p (k n) -> p k n", k=KG)
-        zero_c = keep.tile([P, BANK], U32, name="zero_c", align_bytes=ALIGN)
-        zero_s = keep.tile([P, BANK], U8, name="zero_s", align_bytes=ALIGN)
+        cleared = keep.tile([P, FG * KG * PASS], U8, name="cleared", align_bytes=ALIGN)
+        dev_s_head = cleared[:, 0 : KG * PASS].rearrange("p (k n) -> p k n", k=KG)
+        dev_s_rest = cleared[:, KG * PASS :].rearrange("p (k n) -> p k n", k=KG)
+        zero_c = keep.tile([P, WARM_N], U32, name="zero_c", align_bytes=ALIGN)
+        zero_s = keep.tile([P, WARM_N], U8, name="zero_s", align_bytes=ALIGN)
         dev_w = keep.tile([P, FG, KG, 2 * PASS], U8, name="dev_w", align_bytes=ALIGN)
         dev_s_tail = keep.tile([P, FG - 1, KG, PASS], U8, name="dev_s_tail", align_bytes=ALIGN)
         dev_s = [dev_s_head] + [dev_s_tail[:, g] for g in range(FG - 1)]
         boot_w = keep.tile([P, 2, KG, 2 * BANK], U8, name="boot_w", align_bytes=ALIGN)
-        boot_s_second = keep.tile([P, KG, BANK], U8, name="boot_s_second", align_bytes=ALIGN)
-        boot_s = [boot_s_first, boot_s_second[:]]
+        boot_s = keep.tile([P, KG, M], U8, name="boot_s", align_bytes=ALIGN)
         base_raw = keep.tile([P, F // 4], BF16, name="base_raw", align_bytes=ALIGN)
-        base_rows = keep.tile([P, BANK], BF16, name="base_rows", align_bytes=ALIGN)
-        base_cols = keep.tile([P, BANK], BF16, name="base_cols", align_bytes=ALIGN)
+        base_rows = keep.tile([P, F // 4], BF16, name="base_rows", align_bytes=ALIGN)
+        base_cols = keep.tile([P, F // 4], BF16, name="base_cols", align_bytes=ALIGN)
         rlen_raw = keep.tile([P, M_TILES, 2], BF16, name="rlen_raw", align_bytes=ALIGN)
         rlen_cols = keep.tile([P, M_TILES], F32, name="rlen_cols", align_bytes=ALIGN)
         ident_f32 = keep.tile([P, P], F32, name="ident_f32", align_bytes=ALIGN)
@@ -89,8 +87,8 @@ def tile_bootstrap_signature_cosine_s12_kernel(
         def load_bytes(dst, src):
             nc.sync.dma_start(out=dst.bitcast(I32), in_=src.bitcast(I32))
 
-        def load_scales(dst, src):
-            for q in QUADRANTS:
+        def load_scales(dst, src, quadrants=QUADRANTS):
+            for q in quadrants:
                 rows = slice(QUAD * q, QUAD * q + SCALE_ROWS)
                 load_bytes(dst[rows], src.rearrange("k (q r) n -> q r k n", r=SCALE_ROWS)[q])
 
@@ -118,15 +116,15 @@ def tile_bootstrap_signature_cosine_s12_kernel(
 
         def order_base():
             nc.vector.tensor_copy(
-                out=base_rows[:, 0 : F // 4].rearrange("p (g t a i) -> p g t a i", g=FG, t=PACK, i=RUN),
+                out=base_rows[:].rearrange("p (g t a i) -> p g t a i", g=FG, t=PACK, i=RUN),
                 in_=base_raw[:].rearrange("p (g a t i) -> p g t a i", g=FG, t=PACK, i=RUN),
             )
 
-        def turn_base():
-            nc.vector.transpose(base_cols[:], base_rows[:])
+        def turn_base(lo, hi):
+            nc.vector.transpose(base_cols[:, lo:hi], base_rows[:, lo:hi])
 
         def warm_up_tensor(passes):
-            bank = psum.tile([P, BANK], F32, name="warm_bank", tag="bank")
+            bank = psum.tile([P, WARM_N], F32, name="warm_bank", tag="bank")
             for _ in range(passes):
                 nc.tensor.matmul_mx(
                     out=bank[:],
@@ -164,7 +162,7 @@ def tile_bootstrap_signature_cosine_s12_kernel(
                     lhsT=dev_w[:, g, k, 2 * col : 2 * (col + P)].bitcast(FP4X4),
                     lhsT_scale=dev_s[g][:, k, col : col + P],
                     rhs=boot_w[:, h, k, :].bitcast(FP4X4),
-                    rhs_scale=boot_s[h][:, k, :],
+                    rhs_scale=boot_s[:, k, h * BANK : (h + 1) * BANK],
                     start=(k == 0),
                     stop=(k == KG - 1),
                 )
@@ -181,12 +179,13 @@ def tile_bootstrap_signature_cosine_s12_kernel(
             for t in range(PACK):
                 cat_bank(h, g, t, nc.scalar)
 
-        def cat_weave(g, lo, width):
+        def cat_weave(g, lo, width, eng=nc.vector):
             h, c = divmod(lo, BANK)
-            woven = ring.tile([P, width * PACK], BF16, name="woven", tag="woven", bufs=5, align_bytes=ALIGN)
-            nc.vector.tensor_copy(
-                out=woven[:].rearrange("p (c i t) -> p c t i", i=RUN, t=PACK),
-                in_=cat_rows[:, h, g, :, c : c + width].rearrange("p t (c i) -> p c t i", i=RUN),
+            woven = ring.tile([P, width * PACK], BF16, name="woven", tag="woven", bufs=8, align_bytes=ALIGN)
+            copy_out(
+                eng,
+                woven[:].rearrange("p (c i t) -> p c t i", i=RUN, t=PACK),
+                cat_rows[:, h, g, :, c : c + width].rearrange("p t (c i) -> p c t i", i=RUN),
             )
             staged[("cat", g, lo)] = woven
 
@@ -202,7 +201,7 @@ def tile_bootstrap_signature_cosine_s12_kernel(
                 cat_quant(g, lo, width)
 
         def sig_weave(g):
-            woven = ring.tile([P, BANK * PACK], BF16, name="woven", tag="woven", bufs=5, align_bytes=ALIGN)
+            woven = ring.tile([P, BANK * PACK], BF16, name="woven", tag="woven", bufs=8, align_bytes=ALIGN)
             nc.vector.tensor_copy(
                 out=woven[:].rearrange("p (t a i j) -> p t a j i", t=PACK, i=RUN, j=PACK),
                 in_=sig_raw[:, g].rearrange("p j (a t i) -> p t a j i", t=PACK, i=RUN),
@@ -215,8 +214,8 @@ def tile_bootstrap_signature_cosine_s12_kernel(
 
         def expo_sort(h):
             nc.vector.tensor_copy(
-                out=expo_sorted[:, h].rearrange("p b i u w -> p (b i) u w"),
-                in_=expo_raw[h][:].bitcast(F32).rearrange("p b (i w u) -> p (b i) u w", i=2, u=2),
+                out=expo_sorted[:, h].rearrange("p b i u w -> p (b i) w u"),
+                in_=expo_raw[h][:].bitcast(F32).rearrange("p b (i w u) -> p (b i) w u", i=2, u=2),
             )
 
         def expo_bank(b, eng):
@@ -260,7 +259,7 @@ def tile_bootstrap_signature_cosine_s12_kernel(
                 in_=mix_in[:, g, n.start * PACK : n.stop * PACK],
             )
 
-        def out_banks(tiles, lo, width, eng):
+        def out_passes(tiles, lo, width):
             n = slice(lo, lo + width)
             banks = [psum.tile([P, width], F32, name="out_bank", tag="bank") for _ in tiles]
             for g in range(FG):
@@ -276,6 +275,12 @@ def tile_bootstrap_signature_cosine_s12_kernel(
                         stop=(g == FG - 1),
                     )
             for i, bank in zip(tiles, banks):
+                staged[("out", i, lo)] = bank
+
+        def out_store(tiles, lo, width, eng):
+            n = slice(lo, lo + width)
+            for i in tiles:
+                bank = staged[("out", i, lo)]
                 result = ring.tile([P, width], F32, name="result", tag="result", bufs=10)
                 factor = rlen_cols[:, i : i + 1]
                 if eng is nc.scalar:
@@ -284,31 +289,37 @@ def tile_bootstrap_signature_cosine_s12_kernel(
                     nc.vector.tensor_scalar(out=result[:], in0=bank[:], scalar1=factor, scalar2=None, op0=ALU.mult)
                 nc.sync.dma_start(out=out[i * P : (i + 1) * P, n], in_=result[:])
 
+        def out_banks(tiles, lo, width, eng):
+            out_passes(tiles, lo, width)
+            out_store(tiles, lo, width, eng)
+
         V, S = nc.vector, nc.scalar
 
-        nc.vector.memset(cleared[:].bitcast(I32), 0)
         warm_up_scalar()
-        nc.vector.memset(base_raw[:], 0.0)
-        nc.vector.memset(base_rows[:, F // 4 : BANK], 0.0)
-        nc.vector.quantize_mx(out=zero_c[:].bitcast(FP8X4), scales=zero_s[:], in_=cleared[:].bitcast(BF16))
-        clear(nc.vector, boot_s[1])
-        make_identity(nc, ident_f32[:])
+        nc.vector.memset(cleared[:].bitcast(I32), 0)
+        clear(nc.vector, boot_s[:])
+        for n in (slice(0, WARM_N // 2), slice(WARM_N // 2, WARM_N)):
+            nc.vector.quantize_mx(
+                out=zero_c[:, n].bitcast(FP8X4), scales=zero_s[:, n], in_=cleared[:, 0 : PACK * WARM_N].bitcast(BF16)
+            )
+        nc.vector.memset(base_raw[:].bitcast(I32), 0)
+        nc.vector.memset(ident_f32[:], 0.0)
+        make_identity(nc, ident_f32[:], nomemset=True)
 
         load_scales(dev_s_first, dev_scales[:, :, 0:PASS])
         load_bytes(dev_w_raw[:, 0], dev_view[:, 0])
         load_bytes(boot_w[:, 0], boot_view[:, 0])
+        load_scales(boot_s, boot_scales)
         nc.sync.dma_start(
             out=base_raw[0:P:QUAD, :].rearrange("q (g c) -> q g c", g=FG),
             in_=base.rearrange("(g q c) -> q g c", g=FG, q=P // QUAD),
         )
-        load_scales(boot_s[0], boot_scales[:, :, 0:BANK])
-        nc.sync.dma_start(out=sig_raw[:, 0], in_=sig_view[:, 0])
         load_bytes(boot_w[:, 1], boot_view[:, 1])
-        load_scales(boot_s[1], boot_scales[:, :, BANK : 2 * BANK])
-        for h in range(2):
-            nc.sync.dma_start(out=expo_raw[h][:], in_=expo_view[:, 2 * h : 2 * h + 2])
+        nc.sync.dma_start(out=sig_raw[:, 0], in_=sig_view[:, 0])
         load_bytes(dev_w_raw[:, 1], dev_view[:, 1])
         load_scales(dev_s_rest, dev_scales[:, :, PASS:F])
+        for h in range(2):
+            nc.sync.dma_start(out=expo_raw[h][:], in_=expo_view[:, 2 * h : 2 * h + 2])
         load_bytes(dev_w_raw[:, 2], dev_view[:, 2])
         nc.sync.dma_start(out=sig_raw[:, 1], in_=sig_view[:, 1])
         nc.sync.dma_start(out=sig_raw[:, 2], in_=sig_view[:, 2])
@@ -319,43 +330,39 @@ def tile_bootstrap_signature_cosine_s12_kernel(
             order_first_dev_scales(q)
         order_dev_words(0)
         order_base()
-        turn_base()
+        turn_base(0, P)
 
-        for t in range(PACK - 1):
-            cat_bank(0, 0, t, S)
+        cat_unit(0, 0)
+        turn_base(P, F // 4)
         sig_weave(0)
-        cat_bank(0, 0, PACK - 1, V)
         cat_unit(1, 0)
-        expo_sort(0)
-        sig_quant(0)
-        expo_sort(1)
         order_dev_words(1)
         order_other_dev_scales()
+        sig_quant(0)
+        expo_sort(0)
+        cat_weave(0, 0, 2 * P)
+        expo_sort(1)
+        cat_quant(0, 0, 2 * P)
+        order_dev_words(2)
+        for t in range(PACK):
+            cat_bank(0, 1, t, (S, S, V, S)[t])
+        sig_weave(1)
         for b in range(EXPO_BANKS):
             expo_bank(b, S)
-        order_dev_words(2)
-        cat_weave(0, 0, 2 * P)
-        cat_unit(0, 1)
-        expo_quant(0, 2)
-        sig_weave(1)
-        cat_quant(0, 0, 2 * P)
-
-        sig_quant(1)
         cat_unit(0, 2)
-        sig_weave(2)
         cat_weave(1, 0, 2 * P)
-        sig_quant(2)
+        sig_quant(1)
+        sig_weave(2)
+        expo_quant(0, 2)
         cat_quant(1, 0, 2 * P)
+        sig_quant(2)
         cat_unit(1, 1)
-        cat_weave(2, 0, 2 * P)
         expo_quant(2, 2)
+        cat_weave(2, 0, 2 * P)
+        for g in range(FG):
+            for i in range(HALF_TILES):
+                mix_bank(g, i, ((V, V, S, V), (S, V, S, S), (V, S, S, V))[g][i])
         cat_quant(2, 0, 2 * P)
-        for i in range(4):
-            mix_bank(0, i, (V, V, S, V)[i])
-        for i in range(4):
-            mix_bank(1, i, (S, V, S, V)[i])
-        for i in range(4):
-            mix_bank(2, i, (S, V, S, V)[i])
         mix_quant(0, 0)
         cat_unit(1, 2)
         mix_quant(1, 0)
@@ -366,29 +373,36 @@ def tile_bootstrap_signature_cosine_s12_kernel(
         mix_bank(0, 4, S)
         mix_bank(0, 5, V)
         mix_bank(0, 6, S)
-        mix_bank(0, 7, S)
+        mix_bank(0, 7, V)
         for g in range(FG):
             cat_quant(g, 2 * P, P)
-        mix_bank(1, 4, V)
-        mix_bank(1, 5, S)
-        out_banks([0], 0, BANK, S)
+        mix_bank(1, 4, S)
+        mix_bank(1, 5, V)
+        out_passes([0], 0, BANK)
         mix_quant(0, 1)
-        mix_bank(1, 6, V)
+        mix_bank(1, 6, S)
         mix_bank(1, 7, S)
+        mix_bank(2, 4, V)
+        out_store([0], 0, BANK, S)
+        out_passes([1], 0, BANK)
         cat_weave(0, 3 * P, P)
-        mix_bank(2, 4, S)
-        out_banks([1], 0, BANK, S)
         mix_quant(1, 1)
-        mix_bank(2, 5, V)
-        mix_bank(2, 6, S)
+        mix_bank(2, 5, S)
+        mix_bank(2, 6, V)
         mix_bank(2, 7, S)
         cat_weave(1, 3 * P, P)
-        cat_weave(2, 3 * P, P)
         mix_quant(2, 1)
+        cat_weave(2, 3 * P, P)
+        out_store([1], 0, BANK, S)
+        out_banks([2], 0, BANK, S)
+        cat_weave(0, 4 * P, P, S)
         for g in range(FG):
             cat_quant(g, 3 * P, P)
-        out_banks([2], 0, BANK, S)
-        for i in range(4, M_TILES):
+        for g in range(1, FG):
+            cat_weave(g, 4 * P, P)
+        for g in range(FG):
+            cat_quant(g, 4 * P, P)
+        for i in range(5, M_TILES):
             cat_piece(i, 1)
         out_banks([0, 1, 2], BANK, BANK, S)
         for i in range(3, M_TILES - 2):

@@ -67,7 +67,6 @@ def tile_bootstrap_signature_cosine_s12_kernel(
         sig_c = keep.tile([P, F], U32, name="sig_c", align_bytes=ALIGN)
         sig_s = keep.tile([P, F], U8, name="sig_s", align_bytes=ALIGN)
         expo_raw = [keep.tile([P, 2, 2 * J], BF16, name="expo_raw%d" % h, align_bytes=ALIGN) for h in range(2)]
-        expo_sorted = keep.tile([P, 2, 2, 2, 2, P], F32, name="expo_sorted", align_bytes=ALIGN)
         expo_t = keep.tile([P, R * PACK], BF16, name="expo_t", align_bytes=ALIGN)
         expo_c = keep.tile([P, R], U32, name="expo_c", align_bytes=ALIGN)
         expo_s = keep.tile([P, R], U8, name="expo_s", align_bytes=ALIGN)
@@ -151,7 +150,7 @@ def tile_bootstrap_signature_cosine_s12_kernel(
                 nc.sync.dma_start(out=rlen_raw[:, :, 0:1], in_=rlen.rearrange("(i p o) -> p i o", p=P, o=1))
 
         def widen_rlen():
-            nc.vector.tensor_copy(out=rlen_cols[:], in_=rlen_raw[:, :, 0])
+            nc.scalar.copy(out=rlen_cols[:], in_=rlen_raw[:, :, 0])
 
         def cat_bank(h, g, t, eng):
             bank = psum.tile([P, BANK], F32, name="cat_bank", tag="bank")
@@ -212,17 +211,12 @@ def tile_bootstrap_signature_cosine_s12_kernel(
             n = slice(g * PASS, (g + 1) * PASS)
             nc.vector.quantize_mx(out=sig_c[:, n].bitcast(FP8X4), scales=sig_s[:, n], in_=staged[("sig", g)][:])
 
-        def expo_sort(h):
-            nc.vector.tensor_copy(
-                out=expo_sorted[:, h].rearrange("p b i u w -> p (b i) w u"),
-                in_=expo_raw[h][:].bitcast(F32).rearrange("p b (i w u) -> p (b i) w u", i=2, u=2),
-            )
-
         def expo_bank(b, eng):
             bank = psum.tile([P, 2, 2, P], F32, name="expo_bank", tag="bank")
             for i in range(2):
                 for u in range(2):
-                    nc.tensor.transpose(bank[:, i, u, :], expo_sorted[:, b // 2, b % 2, i, u, :], ident_f32[:])
+                    words = expo_raw[b // 2][:, b % 2, i * J : (i + 1) * J].bitcast(F32)
+                    nc.tensor.transpose(bank[:, i, u, :], words[:, u : J // 2 : 2], ident_f32[:])
             dst = expo_t[:, b * 2 * PASS : (b + 1) * 2 * PASS].bitcast(F32).rearrange("p (r i u) -> p r i u", i=2, u=2)
             src = bank[:].rearrange("p i u r -> p r i u")
             copy_out(eng, dst, src)
@@ -314,14 +308,14 @@ def tile_bootstrap_signature_cosine_s12_kernel(
             out=base_raw[0:P:QUAD, :].rearrange("q (g c) -> q g c", g=FG),
             in_=base.rearrange("(g q c) -> q g c", g=FG, q=P // QUAD),
         )
-        load_bytes(boot_w[:, 1], boot_view[:, 1])
         nc.sync.dma_start(out=sig_raw[:, 0], in_=sig_view[:, 0])
+        load_bytes(boot_w[:, 1], boot_view[:, 1])
         load_bytes(dev_w_raw[:, 1], dev_view[:, 1])
         load_scales(dev_s_rest, dev_scales[:, :, PASS:F])
-        for h in range(2):
-            nc.sync.dma_start(out=expo_raw[h][:], in_=expo_view[:, 2 * h : 2 * h + 2])
+        nc.sync.dma_start(out=expo_raw[0][:], in_=expo_view[:, 0:2])
         load_bytes(dev_w_raw[:, 2], dev_view[:, 2])
         nc.sync.dma_start(out=sig_raw[:, 1], in_=sig_view[:, 1])
+        nc.sync.dma_start(out=expo_raw[1][:], in_=expo_view[:, 2:4])
         nc.sync.dma_start(out=sig_raw[:, 2], in_=sig_view[:, 2])
         load_rlen()
 
@@ -333,79 +327,64 @@ def tile_bootstrap_signature_cosine_s12_kernel(
         turn_base(0, P)
 
         cat_unit(0, 0)
-        turn_base(P, F // 4)
         sig_weave(0)
         cat_unit(1, 0)
         order_dev_words(1)
         order_other_dev_scales()
+        turn_base(P, F // 4)
+        cat_unit(0, 1)
+        cat_weave(0, 0, BANK)
         sig_quant(0)
-        expo_sort(0)
-        cat_weave(0, 0, 2 * P)
-        expo_sort(1)
-        cat_quant(0, 0, 2 * P)
+        cat_quant(0, 0, BANK)
         order_dev_words(2)
-        for t in range(PACK):
-            cat_bank(0, 1, t, (S, S, V, S)[t])
-        sig_weave(1)
-        for b in range(EXPO_BANKS):
+        for b in range(2):
             expo_bank(b, S)
+        sig_weave(1)
         cat_unit(0, 2)
-        cat_weave(1, 0, 2 * P)
-        sig_quant(1)
+        cat_weave(1, 0, BANK)
         sig_weave(2)
+        for b in range(2, 4):
+            expo_bank(b, S)
+        sig_quant(1)
         expo_quant(0, 2)
-        cat_quant(1, 0, 2 * P)
+        cat_quant(1, 0, BANK)
         sig_quant(2)
         cat_unit(1, 1)
-        expo_quant(2, 2)
-        cat_weave(2, 0, 2 * P)
+        cat_weave(2, 0, BANK)
         for g in range(FG):
             for i in range(HALF_TILES):
-                mix_bank(g, i, ((V, V, S, V), (S, V, S, S), (V, S, S, V))[g][i])
-        cat_quant(2, 0, 2 * P)
+                mix_bank(g, i, ((V, S, V, S), (V, S, V, S), (V, S, S, S))[g][i])
+        expo_quant(2, 2)
         mix_quant(0, 0)
         cat_unit(1, 2)
         mix_quant(1, 0)
         mix_quant(2, 0)
+        cat_quant(2, 0, BANK)
         widen_rlen()
-        for g in range(FG):
-            cat_weave(g, 2 * P, P)
-        mix_bank(0, 4, S)
-        mix_bank(0, 5, V)
-        mix_bank(0, 6, S)
-        mix_bank(0, 7, V)
-        for g in range(FG):
-            cat_quant(g, 2 * P, P)
+
+        for i in range(HALF_TILES):
+            mix_bank(0, HALF_TILES + i, (V, V, S, V)[i])
         mix_bank(1, 4, S)
-        mix_bank(1, 5, V)
+        mix_bank(1, 5, S)
         out_passes([0], 0, BANK)
-        mix_quant(0, 1)
         mix_bank(1, 6, S)
         mix_bank(1, 7, S)
-        mix_bank(2, 4, V)
+        mix_quant(0, 1)
+        mix_quant(1, 1)
         out_store([0], 0, BANK, S)
         out_passes([1], 0, BANK)
-        cat_weave(0, 3 * P, P)
-        mix_quant(1, 1)
-        mix_bank(2, 5, S)
-        mix_bank(2, 6, V)
-        mix_bank(2, 7, S)
-        cat_weave(1, 3 * P, P)
+        for i in range(HALF_TILES):
+            mix_bank(2, HALF_TILES + i, (V, S, V, S)[i])
         mix_quant(2, 1)
-        cat_weave(2, 3 * P, P)
         out_store([1], 0, BANK, S)
-        out_banks([2], 0, BANK, S)
-        cat_weave(0, 4 * P, P, S)
-        for g in range(FG):
-            cat_quant(g, 3 * P, P)
-        for g in range(1, FG):
-            cat_weave(g, 4 * P, P)
-        for g in range(FG):
-            cat_quant(g, 4 * P, P)
-        for i in range(5, M_TILES):
+        for i in range(2, HALF_TILES):
+            out_banks([i], 0, BANK, S)
+        for i in range(HALF_TILES, M_TILES):
             cat_piece(i, 1)
-        out_banks([0, 1, 2], BANK, BANK, S)
-        for i in range(3, M_TILES - 2):
+        out_banks([0, 1], BANK, BANK, S)
+        for i in range(2, HALF_TILES):
+            out_banks([i], BANK, BANK, S)
+        for i in range(HALF_TILES, M_TILES - 2):
             for lo in range(0, R, BANK):
                 out_banks([i], lo, BANK, S)
         for i in range(M_TILES - 2, M_TILES):

@@ -31,6 +31,7 @@ HALF_TILES = BANK // P
 SMALL_BANK = 256
 EXPO_BANKS = R // (2 * P)
 WARM_N = 512
+PIECES = 4
 ALIGN = 64
 
 
@@ -178,14 +179,14 @@ def tile_bootstrap_signature_cosine_s12_kernel(
             for t in range(PACK):
                 cat_bank(h, g, t, nc.scalar)
 
-        def cat_weave(g, lo, width, eng=nc.vector):
+        def cat_weave(g, lo, width):
             h, c = divmod(lo, BANK)
             woven = ring.tile([P, width * PACK], BF16, name="woven", tag="woven", bufs=8, align_bytes=ALIGN)
-            copy_out(
-                eng,
-                woven[:].rearrange("p (c i t) -> p c t i", i=RUN, t=PACK),
-                cat_rows[:, h, g, :, c : c + width].rearrange("p t (c i) -> p c t i", i=RUN),
-            )
+            for m in range(0, width, P):
+                nc.vector.tensor_copy(
+                    out=woven[:, m * PACK : (m + P) * PACK].rearrange("p (c i t) -> p c t i", i=RUN, t=PACK),
+                    in_=cat_rows[:, h, g, :, c + m : c + m + P].rearrange("p t (c i) -> p c t i", i=RUN),
+                )
             staged[("cat", g, lo)] = woven
 
         def cat_quant(g, lo, width):
@@ -201,10 +202,10 @@ def tile_bootstrap_signature_cosine_s12_kernel(
 
         def sig_weave(g):
             woven = ring.tile([P, BANK * PACK], BF16, name="woven", tag="woven", bufs=8, align_bytes=ALIGN)
-            nc.vector.tensor_copy(
-                out=woven[:].rearrange("p (t a i j) -> p t a j i", t=PACK, i=RUN, j=PACK),
-                in_=sig_raw[:, g].rearrange("p j (a t i) -> p t a j i", t=PACK, i=RUN),
-            )
+            dst = woven[:].rearrange("p (t q a i j) -> p q a t j i", t=PACK, q=PIECES, i=RUN, j=PACK)
+            src = sig_raw[:, g].rearrange("p j (q a t i) -> p q a t j i", q=PIECES, t=PACK, i=RUN)
+            for q in range(PIECES):
+                nc.vector.tensor_copy(out=dst[:, q], in_=src[:, q])
             staged[("sig", g)] = woven
 
         def sig_quant(g):

@@ -60,7 +60,8 @@ def tile_bootstrap_signature_cosine_s12_kernel(
         base_raw = keep.tile([P, F // 4], BF16, name="base_raw", align_bytes=ALIGN)
         base_rows = keep.tile([P, F // 4], BF16, name="base_rows", align_bytes=ALIGN)
         base_cols = keep.tile([P, F // 4], BF16, name="base_cols", align_bytes=ALIGN)
-        rlen_raw = keep.tile([P, M_TILES, 2], BF16, name="rlen_raw", align_bytes=ALIGN)
+        rlen_rows = keep.tile([P, M_TILES * QUAD], BF16, name="rlen_rows", align_bytes=ALIGN)
+        rlen_turned = keep.tile([P, M_TILES * QUAD], BF16, name="rlen_turned", align_bytes=ALIGN)
         rlen_cols = keep.tile([P, M_TILES], F32, name="rlen_cols", align_bytes=ALIGN)
         ident_f32 = keep.tile([P, P], F32, name="ident_f32", align_bytes=ALIGN)
         warm = keep.tile([P, 8], F32, name="warm", align_bytes=ALIGN)
@@ -123,18 +124,18 @@ def tile_bootstrap_signature_cosine_s12_kernel(
         def turn_base(lo, hi):
             nc.vector.transpose(base_cols[:, lo:hi], base_rows[:, lo:hi])
 
-        def warm_up_tensor(passes):
-            bank = psum.tile([P, WARM_N], F32, name="warm_bank", tag="bank")
-            for _ in range(passes):
-                nc.tensor.matmul_mx(
-                    out=bank[:],
-                    lhsT=zero_c[:, 0:P].bitcast(FP8X4),
-                    lhsT_scale=zero_s[:, 0:P],
-                    rhs=zero_c[:].bitcast(FP8X4),
-                    rhs_scale=zero_s[:],
-                    start=True,
-                    stop=True,
-                )
+        def warm_up_tensor(words, scales, dtype):
+            bank = psum.tile([P, BANK], F32, name="warm_bank", tag="bank")
+            codes = words.bitcast(dtype)
+            nc.tensor.matmul_mx(
+                out=bank[:],
+                lhsT=codes[:, 0:P],
+                lhsT_scale=scales[:, 0:P],
+                rhs=codes,
+                rhs_scale=scales,
+                start=True,
+                stop=True,
+            )
 
         def warm_up_scalar():
             nc.vector.memset(warm[:], 0.0)
@@ -147,11 +148,16 @@ def tile_bootstrap_signature_cosine_s12_kernel(
                 nc.vector.tensor_copy(out=dst, in_=src)
 
         def load_rlen():
-            with nc.allow_non_contiguous_dma(reason="one factor to a partition and tile"):
-                nc.sync.dma_start(out=rlen_raw[:, :, 0:1], in_=rlen.rearrange("(i p o) -> p i o", p=P, o=1))
+            nc.sync.dma_start(
+                out=rlen_rows[0:P:QUAD, :].rearrange("q (i c) -> q i c", c=QUAD),
+                in_=rlen.rearrange("(i q c) -> q i c", i=M_TILES, c=QUAD),
+            )
+
+        def turn_rlen():
+            nc.vector.transpose(rlen_turned[:], rlen_rows[:])
 
         def widen_rlen():
-            nc.scalar.copy(out=rlen_cols[:], in_=rlen_raw[:, :, 0])
+            nc.scalar.copy(out=rlen_cols[:], in_=rlen_turned[:, 0 : M_TILES * QUAD : QUAD])
 
         def cat_bank(h, g, t, eng):
             bank = psum.tile([P, BANK], F32, name="cat_bank", tag="bank")
@@ -298,6 +304,7 @@ def tile_bootstrap_signature_cosine_s12_kernel(
                 out=zero_c[:, n].bitcast(FP8X4), scales=zero_s[:, n], in_=cleared[:, 0 : PACK * WARM_N].bitcast(BF16)
             )
         nc.vector.memset(base_raw[:].bitcast(I32), 0)
+        nc.vector.memset(rlen_rows[:].bitcast(I32), 0)
         nc.vector.memset(ident_f32[:], 0.0)
         make_identity(nc, ident_f32[:], nomemset=True)
 
@@ -320,9 +327,12 @@ def tile_bootstrap_signature_cosine_s12_kernel(
         nc.sync.dma_start(out=sig_raw[:, 2], in_=sig_view[:, 2])
         load_rlen()
 
-        warm_up_tensor(4)
+        warm_up_tensor(zero_c[:], zero_s[:], FP8X4)
+        warm_up_tensor(zero_c[:], zero_s[:], FP8X4)
         for q in QUADRANTS:
             order_first_dev_scales(q)
+        warm_up_tensor(dev_w_raw[:, 0, 0, :], dev_s_head[:, 0, :], FP4X4)
+        warm_up_tensor(boot_w[:, 0, 0, :], dev_s_head[:, 0, :], FP4X4)
         order_dev_words(0)
         order_base()
         turn_base(0, P)
@@ -361,16 +371,17 @@ def tile_bootstrap_signature_cosine_s12_kernel(
         mix_quant(1, 0)
         mix_quant(2, 0)
         cat_quant(2, 0, BANK)
-        widen_rlen()
 
         for i in range(HALF_TILES):
             mix_bank(0, HALF_TILES + i, (V, V, S, V)[i])
+        turn_rlen()
         mix_bank(1, 4, S)
         mix_bank(1, 5, S)
+        widen_rlen()
         out_passes([0], 0, BANK)
-        mix_bank(1, 6, S)
-        mix_bank(1, 7, S)
         mix_quant(0, 1)
+        mix_bank(1, 6, S)
+        mix_bank(1, 7, V)
         mix_quant(1, 1)
         out_store([0], 0, BANK, S)
         out_passes([1], 0, BANK)

@@ -60,8 +60,8 @@ def tile_bootstrap_signature_cosine_s12_kernel(
         base_raw = keep.tile([P, F // 4], BF16, name="base_raw", align_bytes=ALIGN)
         base_rows = keep.tile([P, F // 4], BF16, name="base_rows", align_bytes=ALIGN)
         base_cols = keep.tile([P, F // 4], BF16, name="base_cols", align_bytes=ALIGN)
-        rlen_rows = keep.tile([P, M_TILES * QUAD], BF16, name="rlen_rows", align_bytes=ALIGN)
-        rlen_turned = keep.tile([P, M_TILES * QUAD], BF16, name="rlen_turned", align_bytes=ALIGN)
+        rlen_raw = keep.tile([M_TILES, P], BF16, name="rlen_raw", align_bytes=ALIGN)
+        rlen_rows = keep.tile([P, P], F32, name="rlen_rows", align_bytes=ALIGN)
         rlen_cols = keep.tile([P, M_TILES], F32, name="rlen_cols", align_bytes=ALIGN)
         ident_f32 = keep.tile([P, P], F32, name="ident_f32", align_bytes=ALIGN)
         warm = keep.tile([P, 8], F32, name="warm", align_bytes=ALIGN)
@@ -147,17 +147,10 @@ def tile_bootstrap_signature_cosine_s12_kernel(
             else:
                 nc.vector.tensor_copy(out=dst, in_=src)
 
-        def load_rlen():
-            nc.sync.dma_start(
-                out=rlen_rows[0:P:QUAD, :].rearrange("q (i c) -> q i c", c=QUAD),
-                in_=rlen.rearrange("(i q c) -> q i c", i=M_TILES, c=QUAD),
-            )
-
         def turn_rlen():
-            nc.vector.transpose(rlen_turned[:], rlen_rows[:])
-
-        def widen_rlen():
-            nc.scalar.copy(out=rlen_cols[:], in_=rlen_turned[:, 0 : M_TILES * QUAD : QUAD])
+            bank = psum.tile([P, P], F32, name="rlen_bank", tag="bank")
+            nc.tensor.transpose(bank[:], rlen_rows[:], ident_f32[:])
+            nc.scalar.copy(out=rlen_cols[:], in_=bank[:, 0:M_TILES])
 
         def cat_bank(h, g, t, eng):
             bank = psum.tile([P, BANK], F32, name="cat_bank", tag="bank")
@@ -195,6 +188,18 @@ def tile_bootstrap_signature_cosine_s12_kernel(
                 )
             staged[("cat", g, lo)] = woven
 
+        def cat_weave_aside(g, tag):
+            woven = ring.tile([P, BANK * PACK], BF16, name="woven_aside", tag=tag, bufs=1, align_bytes=ALIGN)
+            nc.gpsimd.tensor_scalar(
+                out=woven[:].rearrange("p (c t) -> p c t", t=PACK),
+                in0=cat_rows[:, 0, g].rearrange("p t c -> p c t"),
+                scalar1=1.0,
+                scalar2=0.0,
+                op0=ALU.mult,
+                op1=ALU.add,
+            )
+            staged[("cat", g, 0)] = woven
+
         def cat_quant(g, lo, width):
             n = slice(lo, lo + width)
             nc.vector.quantize_mx(out=cat_c[:, g, n].bitcast(FP8X4), scales=cat_s[:, g, n], in_=staged[("cat", g, lo)][:])
@@ -207,7 +212,7 @@ def tile_bootstrap_signature_cosine_s12_kernel(
                 cat_quant(g, lo, width)
 
         def sig_weave(g):
-            woven = ring.tile([P, BANK * PACK], BF16, name="woven", tag="woven", bufs=8, align_bytes=ALIGN)
+            woven = ring.tile([P, BANK * PACK], BF16, name="sig_woven", tag="sig%d" % g, bufs=1, align_bytes=ALIGN)
             dst = woven[:].rearrange("p (t q a i j) -> p q a t j i", t=PACK, q=PIECES, i=RUN, j=PACK)
             src = sig_raw[:, g].rearrange("p j (q a t i) -> p q a t j i", q=PIECES, t=PACK, i=RUN)
             for q in range(PIECES):
@@ -296,6 +301,7 @@ def tile_bootstrap_signature_cosine_s12_kernel(
 
         V, S = nc.vector, nc.scalar
 
+        make_identity(nc, ident_f32[:])
         warm_up_scalar()
         nc.vector.memset(cleared[:].bitcast(I32), 0)
         clear(nc.vector, boot_s[:])
@@ -304,9 +310,7 @@ def tile_bootstrap_signature_cosine_s12_kernel(
                 out=zero_c[:, n].bitcast(FP8X4), scales=zero_s[:, n], in_=cleared[:, 0 : PACK * WARM_N].bitcast(BF16)
             )
         nc.vector.memset(base_raw[:].bitcast(I32), 0)
-        nc.vector.memset(rlen_rows[:].bitcast(I32), 0)
-        nc.vector.memset(ident_f32[:], 0.0)
-        make_identity(nc, ident_f32[:], nomemset=True)
+        nc.vector.memset(rlen_rows[:], 0.0)
 
         load_scales(dev_s_first, dev_scales[:, :, 0:PASS])
         load_bytes(dev_w_raw[:, 0], dev_view[:, 0])
@@ -322,10 +326,10 @@ def tile_bootstrap_signature_cosine_s12_kernel(
         load_scales(dev_s_rest, dev_scales[:, :, PASS:F])
         nc.sync.dma_start(out=expo_raw[0][:], in_=expo_view[:, 0:2])
         load_bytes(dev_w_raw[:, 2], dev_view[:, 2])
+        nc.sync.dma_start(out=rlen_raw[:], in_=rlen.rearrange("(i p) -> i p", p=P))
         nc.sync.dma_start(out=sig_raw[:, 1], in_=sig_view[:, 1])
         nc.sync.dma_start(out=expo_raw[1][:], in_=expo_view[:, 2:4])
         nc.sync.dma_start(out=sig_raw[:, 2], in_=sig_view[:, 2])
-        load_rlen()
 
         warm_up_tensor(zero_c[:], zero_s[:], FP8X4)
         warm_up_tensor(zero_c[:], zero_s[:], FP8X4)
@@ -338,33 +342,35 @@ def tile_bootstrap_signature_cosine_s12_kernel(
         turn_base(0, P)
 
         cat_unit(0, 0)
+        turn_base(P, F // 4)
         sig_weave(0)
         cat_unit(1, 0)
         order_dev_words(1)
         order_other_dev_scales()
-        turn_base(P, F // 4)
         cat_unit(0, 1)
         cat_weave(0, 0, BANK)
         sig_quant(0)
         cat_quant(0, 0, BANK)
         order_dev_words(2)
-        for b in range(2):
-            expo_bank(b, S)
+        nc.scalar.copy(out=rlen_rows[0:M_TILES, :], in_=rlen_raw[:])
         sig_weave(1)
+        for b in range(2):
+            expo_bank(b, (V, S)[b])
         cat_unit(0, 2)
         cat_weave(1, 0, BANK)
         sig_weave(2)
         for b in range(2, 4):
             expo_bank(b, S)
+        turn_rlen()
         sig_quant(1)
         expo_quant(0, 2)
         cat_quant(1, 0, BANK)
         sig_quant(2)
+        cat_weave_aside(2, "sig2")
         cat_unit(1, 1)
-        cat_weave(2, 0, BANK)
         for g in range(FG):
             for i in range(HALF_TILES):
-                mix_bank(g, i, ((V, S, V, S), (V, S, V, S), (V, S, S, S))[g][i])
+                mix_bank(g, i, ((V, V, S, V), (S, V, S, V), (S, V, S, S))[g][i])
         expo_quant(2, 2)
         mix_quant(0, 0)
         cat_unit(1, 2)
@@ -374,10 +380,8 @@ def tile_bootstrap_signature_cosine_s12_kernel(
 
         for i in range(HALF_TILES):
             mix_bank(0, HALF_TILES + i, (V, V, S, V)[i])
-        turn_rlen()
         mix_bank(1, 4, S)
         mix_bank(1, 5, S)
-        widen_rlen()
         out_passes([0], 0, BANK)
         mix_quant(0, 1)
         mix_bank(1, 6, S)

@@ -47,16 +47,15 @@ def tile_bootstrap_signature_cosine_s12_kernel(
 
         dev_w_raw = keep.tile([P, FG, KG, 2 * PASS], U8, name="dev_w_raw", align_bytes=ALIGN)
         dev_s_first = keep.tile([P, KG, PASS], U8, name="dev_s_first", align_bytes=ALIGN)
-        cleared = keep.tile([P, FG * KG * PASS], U8, name="cleared", align_bytes=ALIGN)
-        dev_s_head = cleared[:, 0 : KG * PASS].rearrange("p (k n) -> p k n", k=KG)
-        dev_s_rest = cleared[:, KG * PASS :].rearrange("p (k n) -> p k n", k=KG)
+        dev_s_head = keep.tile([P, KG, PASS], U8, name="dev_s_head", align_bytes=ALIGN)
+        dev_s_rest = keep.tile([P, KG, F - PASS], U8, name="dev_s_rest", align_bytes=ALIGN)
         zero_c = keep.tile([P, WARM_N], U32, name="zero_c", align_bytes=ALIGN)
         zero_s = keep.tile([P, WARM_N], U8, name="zero_s", align_bytes=ALIGN)
         dev_w = keep.tile([P, FG, KG, 2 * PASS], U8, name="dev_w", align_bytes=ALIGN)
         dev_s_tail = keep.tile([P, FG - 1, KG, PASS], U8, name="dev_s_tail", align_bytes=ALIGN)
-        dev_s = [dev_s_head] + [dev_s_tail[:, g] for g in range(FG - 1)]
+        dev_s = [dev_s_head[:]] + [dev_s_tail[:, g] for g in range(FG - 1)]
         boot_w = keep.tile([P, 2, KG, 2 * BANK], U8, name="boot_w", align_bytes=ALIGN)
-        boot_s = keep.tile([P, KG, M], U8, name="boot_s", align_bytes=ALIGN)
+        boot_s = [keep.tile([P, KG, BANK], U8, name="boot_s%d" % h, align_bytes=ALIGN) for h in range(2)]
         base_raw = keep.tile([P, F // 4], BF16, name="base_raw", align_bytes=ALIGN)
         base_rows = keep.tile([P, F // 4], BF16, name="base_rows", align_bytes=ALIGN)
         base_cols = keep.tile([P, F // 4], BF16, name="base_cols", align_bytes=ALIGN)
@@ -88,10 +87,9 @@ def tile_bootstrap_signature_cosine_s12_kernel(
         def load_bytes(dst, src):
             nc.sync.dma_start(out=dst.bitcast(I32), in_=src.bitcast(I32))
 
-        def load_scales(dst, src, quadrants=QUADRANTS):
-            for q in quadrants:
-                rows = slice(QUAD * q, QUAD * q + SCALE_ROWS)
-                load_bytes(dst[rows], src.rearrange("k (q r) n -> q r k n", r=SCALE_ROWS)[q])
+        def load_scales(dst, src, rows=range(SCALE_ROWS)):
+            for r in rows:
+                load_bytes(dst[r:P:QUAD], src.rearrange("k (q r) n -> r q k n", r=SCALE_ROWS)[r])
 
         def order_first_dev_scales(q):
             rows = slice(QUAD * q, QUAD * q + SCALE_ROWS)
@@ -100,16 +98,16 @@ def tile_bootstrap_signature_cosine_s12_kernel(
                 in_=dev_s_first[rows].bitcast(I32).rearrange("p k (a t) -> p k a t", t=PACK),
             )
 
-        def order_dev_words(g):
+        def order_dev_words(g, k=slice(0, KG)):
             nc.vector.tensor_copy(
-                out=dev_w[:, g].bitcast(I32).rearrange("p k (t a w) -> p k t a w", t=PACK, w=2),
-                in_=dev_w_raw[:, g].bitcast(I32).rearrange("p k (a t w) -> p k t a w", t=PACK, w=2),
+                out=dev_w[:, g, k].bitcast(I32).rearrange("p k (t a w) -> p k t a w", t=PACK, w=2),
+                in_=dev_w_raw[:, g, k].bitcast(I32).rearrange("p k (a t w) -> p k t a w", t=PACK, w=2),
             )
 
         def order_other_dev_scales():
             nc.vector.tensor_copy(
                 out=dev_s_tail[:].bitcast(I32).rearrange("p g k (t a) -> p k g a t", t=PACK),
-                in_=dev_s_rest.bitcast(I32).rearrange("p k (g a t) -> p k g a t", g=FG - 1, t=PACK),
+                in_=dev_s_rest[:].bitcast(I32).rearrange("p k (g a t) -> p k g a t", g=FG - 1, t=PACK),
             )
 
         def clear(eng, plane):
@@ -152,31 +150,30 @@ def tile_bootstrap_signature_cosine_s12_kernel(
             nc.tensor.transpose(bank[:], rlen_rows[:], ident_f32[:])
             nc.scalar.copy(out=rlen_cols[:], in_=bank[:, 0:M_TILES])
 
-        def cat_bank(h, g, t, eng):
-            bank = psum.tile([P, BANK], F32, name="cat_bank", tag="bank")
+        def cat_pass(bank, h, g, t, k):
             col = t * P
-            for k in range(KG):
-                nc.tensor.matmul_mx(
-                    out=bank[:],
-                    lhsT=dev_w[:, g, k, 2 * col : 2 * (col + P)].bitcast(FP4X4),
-                    lhsT_scale=dev_s[g][:, k, col : col + P],
-                    rhs=boot_w[:, h, k, :].bitcast(FP4X4),
-                    rhs_scale=boot_s[:, k, h * BANK : (h + 1) * BANK],
-                    start=(k == 0),
-                    stop=(k == KG - 1),
-                )
+            nc.tensor.matmul_mx(
+                out=bank[:],
+                lhsT=dev_w[:, g, k, 2 * col : 2 * (col + P)].bitcast(FP4X4),
+                lhsT_scale=dev_s[g][:, k, col : col + P],
+                rhs=boot_w[:, h, k, :].bitcast(FP4X4),
+                rhs_scale=boot_s[h][:, k, :],
+                start=(k == 0),
+                stop=(k == KG - 1),
+            )
+
+        def cat_empty(bank, h, g, t):
             column = QUAD * (PACK * g + t)
-            bias = base_cols[:, column : column + 1]
-            if eng is nc.scalar:
-                nc.scalar.activation(out=cat_rows[:, h, g, t, :], in_=bank[:], func=ACT.Relu, bias=bias)
-            else:
-                nc.vector.tensor_scalar(
-                    out=cat_rows[:, h, g, t, :], in0=bank[:], scalar1=bias, scalar2=0.0, op0=ALU.add, op1=ALU.max
-                )
+            nc.scalar.activation(
+                out=cat_rows[:, h, g, t, :], in_=bank[:], func=ACT.Relu, bias=base_cols[:, column : column + 1]
+            )
 
         def cat_unit(h, g):
             for t in range(PACK):
-                cat_bank(h, g, t, nc.scalar)
+                bank = psum.tile([P, BANK], F32, name="cat_bank", tag="bank")
+                for k in range(KG):
+                    cat_pass(bank, h, g, t, k)
+                cat_empty(bank, h, g, t)
 
         def cat_weave(g, lo, width):
             h, c = divmod(lo, BANK)
@@ -303,33 +300,37 @@ def tile_bootstrap_signature_cosine_s12_kernel(
 
         make_identity(nc, ident_f32[:])
         warm_up_scalar()
-        nc.vector.memset(cleared[:].bitcast(I32), 0)
-        clear(nc.vector, boot_s[:])
+        clear(nc.vector, dev_s_rest[:])
+        clear(nc.vector, boot_s[0][:])
+        zeros = dev_s_rest[:].rearrange("p k n -> p (k n)").bitcast(BF16)
         for n in (slice(0, WARM_N // 2), slice(WARM_N // 2, WARM_N)):
             nc.vector.quantize_mx(
-                out=zero_c[:, n].bitcast(FP8X4), scales=zero_s[:, n], in_=cleared[:, 0 : PACK * WARM_N].bitcast(BF16)
+                out=zero_c[:, n].bitcast(FP8X4), scales=zero_s[:, n], in_=zeros
             )
+        clear(nc.vector, dev_s_head[:])
         nc.vector.memset(base_raw[:].bitcast(I32), 0)
+        clear(nc.vector, boot_s[1][:])
         nc.vector.memset(rlen_rows[:], 0.0)
 
         load_scales(dev_s_first, dev_scales[:, :, 0:PASS])
         load_bytes(dev_w_raw[:, 0], dev_view[:, 0])
         load_bytes(boot_w[:, 0], boot_view[:, 0])
-        load_scales(boot_s, boot_scales)
+        load_scales(boot_s[0], boot_scales[:, :, 0:BANK])
         nc.sync.dma_start(
             out=base_raw[0:P:QUAD, :].rearrange("q (g c) -> q g c", g=FG),
             in_=base.rearrange("(g q c) -> q g c", g=FG, q=P // QUAD),
         )
-        nc.sync.dma_start(out=sig_raw[:, 0], in_=sig_view[:, 0])
         load_bytes(boot_w[:, 1], boot_view[:, 1])
+        load_scales(boot_s[1], boot_scales[:, :, BANK:M])
         load_bytes(dev_w_raw[:, 1], dev_view[:, 1])
         load_scales(dev_s_rest, dev_scales[:, :, PASS:F])
-        nc.sync.dma_start(out=expo_raw[0][:], in_=expo_view[:, 0:2])
+        nc.sync.dma_start(out=sig_raw[:, 0], in_=sig_view[:, 0])
         load_bytes(dev_w_raw[:, 2], dev_view[:, 2])
-        nc.sync.dma_start(out=rlen_raw[:], in_=rlen.rearrange("(i p) -> i p", p=P))
         nc.sync.dma_start(out=sig_raw[:, 1], in_=sig_view[:, 1])
-        nc.sync.dma_start(out=expo_raw[1][:], in_=expo_view[:, 2:4])
+        nc.sync.dma_start(out=expo_raw[0][:], in_=expo_view[:, 0:2])
+        nc.sync.dma_start(out=rlen_raw[:], in_=rlen.rearrange("(i p) -> i p", p=P))
         nc.sync.dma_start(out=sig_raw[:, 2], in_=sig_view[:, 2])
+        nc.sync.dma_start(out=expo_raw[1][:], in_=expo_view[:, 2:4])
 
         warm_up_tensor(zero_c[:], zero_s[:], FP8X4)
         warm_up_tensor(zero_c[:], zero_s[:], FP8X4)
@@ -343,31 +344,31 @@ def tile_bootstrap_signature_cosine_s12_kernel(
 
         cat_unit(0, 0)
         turn_base(P, F // 4)
-        sig_weave(0)
         cat_unit(1, 0)
         order_dev_words(1)
         order_other_dev_scales()
         cat_unit(0, 1)
         cat_weave(0, 0, BANK)
-        sig_quant(0)
-        cat_quant(0, 0, BANK)
+        sig_weave(0)
         order_dev_words(2)
-        nc.scalar.copy(out=rlen_rows[0:M_TILES, :], in_=rlen_raw[:])
+        cat_quant(0, 0, BANK)
+        sig_quant(0)
+        cat_unit(1, 1)
         sig_weave(1)
-        for b in range(2):
-            expo_bank(b, (V, S)[b])
-        cat_unit(0, 2)
+        nc.scalar.copy(out=rlen_rows[0:M_TILES, :], in_=rlen_raw[:])
         cat_weave(1, 0, BANK)
+        for b in range(2):
+            expo_bank(b, S)
         sig_weave(2)
+        cat_unit(0, 2)
+        expo_quant(0, 2)
+        sig_quant(1)
+        cat_quant(1, 0, BANK)
         for b in range(2, 4):
             expo_bank(b, S)
         turn_rlen()
-        sig_quant(1)
-        expo_quant(0, 2)
-        cat_quant(1, 0, BANK)
         sig_quant(2)
         cat_weave_aside(2, "sig2")
-        cat_unit(1, 1)
         for g in range(FG):
             for i in range(HALF_TILES):
                 mix_bank(g, i, ((V, V, S, V), (S, V, S, V), (S, V, S, S))[g][i])

@@ -29,10 +29,10 @@ QUADRANTS = (0, 2, 1, 3)
 M_TILES = M // P
 HALF_TILES = BANK // P
 SMALL_BANK = 256
-EXPO_BANKS = R // (2 * P)
-WARM_N = 512
 PIECES = 4
 ALIGN = 64
+WOVEN_BUFS = 8
+RESULT_BUFS = 10
 
 
 def tile_bootstrap_signature_cosine_s12_kernel(
@@ -49,8 +49,8 @@ def tile_bootstrap_signature_cosine_s12_kernel(
         dev_s_first = keep.tile([P, KG, PASS], U8, name="dev_s_first", align_bytes=ALIGN)
         dev_s_head = keep.tile([P, KG, PASS], U8, name="dev_s_head", align_bytes=ALIGN)
         dev_s_rest = keep.tile([P, KG, F - PASS], U8, name="dev_s_rest", align_bytes=ALIGN)
-        zero_c = keep.tile([P, WARM_N], U32, name="zero_c", align_bytes=ALIGN)
-        zero_s = keep.tile([P, WARM_N], U8, name="zero_s", align_bytes=ALIGN)
+        zero_c = keep.tile([P, BANK], U32, name="zero_c", align_bytes=ALIGN)
+        zero_s = keep.tile([P, BANK], U8, name="zero_s", align_bytes=ALIGN)
         dev_w = keep.tile([P, FG, KG, 2 * PASS], U8, name="dev_w", align_bytes=ALIGN)
         dev_s_tail = keep.tile([P, FG - 1, KG, PASS], U8, name="dev_s_tail", align_bytes=ALIGN)
         dev_s = [dev_s_head[:]] + [dev_s_tail[:, g] for g in range(FG - 1)]
@@ -78,6 +78,7 @@ def tile_bootstrap_signature_cosine_s12_kernel(
         mix_c = keep.tile([P, FG, R], U32, name="mix_c", align_bytes=ALIGN)
         mix_s = keep.tile([P, FG, R], U8, name="mix_s", align_bytes=ALIGN)
 
+        in_turn = (nc.vector, nc.scalar)
         staged = {}
         sig_view = sig.rearrange("(p j) (g f) -> p g j f", j=PACK, f=PASS)
         expo_view = expo.rearrange("(b p i) j -> p b (i j)", p=P, i=2)
@@ -87,8 +88,8 @@ def tile_bootstrap_signature_cosine_s12_kernel(
         def load_bytes(dst, src):
             nc.sync.dma_start(out=dst.bitcast(I32), in_=src.bitcast(I32))
 
-        def load_scales(dst, src, rows=range(SCALE_ROWS)):
-            for r in rows:
+        def load_scales(dst, src):
+            for r in range(SCALE_ROWS):
                 load_bytes(dst[r:P:QUAD], src.rearrange("k (q r) n -> r q k n", r=SCALE_ROWS)[r])
 
         def order_first_dev_scales(q):
@@ -98,10 +99,10 @@ def tile_bootstrap_signature_cosine_s12_kernel(
                 in_=dev_s_first[rows].bitcast(I32).rearrange("p k (a t) -> p k a t", t=PACK),
             )
 
-        def order_dev_words(g, k=slice(0, KG)):
+        def order_dev_words(g):
             nc.vector.tensor_copy(
-                out=dev_w[:, g, k].bitcast(I32).rearrange("p k (t a w) -> p k t a w", t=PACK, w=2),
-                in_=dev_w_raw[:, g, k].bitcast(I32).rearrange("p k (a t w) -> p k t a w", t=PACK, w=2),
+                out=dev_w[:, g].bitcast(I32).rearrange("p k (t a w) -> p k t a w", t=PACK, w=2),
+                in_=dev_w_raw[:, g].bitcast(I32).rearrange("p k (a t w) -> p k t a w", t=PACK, w=2),
             )
 
         def order_other_dev_scales():
@@ -110,8 +111,8 @@ def tile_bootstrap_signature_cosine_s12_kernel(
                 in_=dev_s_rest[:].bitcast(I32).rearrange("p k (g a t) -> p k g a t", g=FG - 1, t=PACK),
             )
 
-        def clear(eng, plane):
-            eng.memset(plane.rearrange("p k n -> p (k n)").bitcast(I32), 0)
+        def clear(plane):
+            nc.vector.memset(plane.rearrange("p k n -> p (k n)").bitcast(I32), 0)
 
         def order_base():
             nc.vector.tensor_copy(
@@ -150,34 +151,28 @@ def tile_bootstrap_signature_cosine_s12_kernel(
             nc.tensor.transpose(bank[:], rlen_rows[:], ident_f32[:])
             nc.scalar.copy(out=rlen_cols[:], in_=bank[:, 0:M_TILES])
 
-        def cat_pass(bank, h, g, t, k):
-            col = t * P
-            nc.tensor.matmul_mx(
-                out=bank[:],
-                lhsT=dev_w[:, g, k, 2 * col : 2 * (col + P)].bitcast(FP4X4),
-                lhsT_scale=dev_s[g][:, k, col : col + P],
-                rhs=boot_w[:, h, k, :].bitcast(FP4X4),
-                rhs_scale=boot_s[h][:, k, :],
-                start=(k == 0),
-                stop=(k == KG - 1),
-            )
-
-        def cat_empty(bank, h, g, t):
-            column = QUAD * (PACK * g + t)
-            nc.scalar.activation(
-                out=cat_rows[:, h, g, t, :], in_=bank[:], func=ACT.Relu, bias=base_cols[:, column : column + 1]
-            )
-
         def cat_unit(h, g):
             for t in range(PACK):
                 bank = psum.tile([P, BANK], F32, name="cat_bank", tag="bank")
+                col = t * P
                 for k in range(KG):
-                    cat_pass(bank, h, g, t, k)
-                cat_empty(bank, h, g, t)
+                    nc.tensor.matmul_mx(
+                        out=bank[:],
+                        lhsT=dev_w[:, g, k, 2 * col : 2 * (col + P)].bitcast(FP4X4),
+                        lhsT_scale=dev_s[g][:, k, col : col + P],
+                        rhs=boot_w[:, h, k, :].bitcast(FP4X4),
+                        rhs_scale=boot_s[h][:, k, :],
+                        start=(k == 0),
+                        stop=(k == KG - 1),
+                    )
+                column = QUAD * (PACK * g + t)
+                nc.scalar.activation(
+                    out=cat_rows[:, h, g, t, :], in_=bank[:], func=ACT.Relu, bias=base_cols[:, column : column + 1]
+                )
 
         def cat_weave(g, lo, width):
             h, c = divmod(lo, BANK)
-            woven = ring.tile([P, width * PACK], BF16, name="woven", tag="woven", bufs=8, align_bytes=ALIGN)
+            woven = ring.tile([P, width * PACK], BF16, name="woven", tag="woven", bufs=WOVEN_BUFS, align_bytes=ALIGN)
             for m in range(0, width, P):
                 nc.vector.tensor_copy(
                     out=woven[:, m * PACK : (m + P) * PACK].rearrange("p (c i t) -> p c t i", i=RUN, t=PACK),
@@ -254,6 +249,11 @@ def tile_bootstrap_signature_cosine_s12_kernel(
             src = bank[:].rearrange("p t r -> p r t")
             copy_out(eng, dst, src)
 
+        def mix_banks(first, count, h):
+            for n in range(first, first + count):
+                g, i = divmod(n, HALF_TILES)
+                mix_bank(g, h * HALF_TILES + i, in_turn[n % 2])
+
         def mix_quant(g, h):
             n = slice(h * BANK, (h + 1) * BANK)
             nc.vector.quantize_mx(
@@ -284,7 +284,7 @@ def tile_bootstrap_signature_cosine_s12_kernel(
             n = slice(lo, lo + width)
             for i in tiles:
                 bank = staged[("out", i, lo)]
-                result = ring.tile([P, width], F32, name="result", tag="result", bufs=10)
+                result = ring.tile([P, width], F32, name="result", tag="result", bufs=RESULT_BUFS)
                 factor = rlen_cols[:, i : i + 1]
                 if eng is nc.scalar:
                     nc.scalar.activation(out=result[:], in_=bank[:], func=ACT.Copy, scale=factor)
@@ -296,20 +296,17 @@ def tile_bootstrap_signature_cosine_s12_kernel(
             out_passes(tiles, lo, width)
             out_store(tiles, lo, width, eng)
 
-        V, S = nc.vector, nc.scalar
 
         make_identity(nc, ident_f32[:])
         warm_up_scalar()
-        clear(nc.vector, dev_s_rest[:])
-        clear(nc.vector, boot_s[0][:])
+        clear(dev_s_rest[:])
+        clear(boot_s[0][:])
         zeros = dev_s_rest[:].rearrange("p k n -> p (k n)").bitcast(BF16)
-        for n in (slice(0, WARM_N // 2), slice(WARM_N // 2, WARM_N)):
-            nc.vector.quantize_mx(
-                out=zero_c[:, n].bitcast(FP8X4), scales=zero_s[:, n], in_=zeros
-            )
-        clear(nc.vector, dev_s_head[:])
+        for n in (slice(0, BANK // 2), slice(BANK // 2, BANK)):
+            nc.vector.quantize_mx(out=zero_c[:, n].bitcast(FP8X4), scales=zero_s[:, n], in_=zeros)
+        clear(dev_s_head[:])
         nc.vector.memset(base_raw[:].bitcast(I32), 0)
-        clear(nc.vector, boot_s[1][:])
+        clear(boot_s[1][:])
         nc.vector.memset(rlen_rows[:], 0.0)
 
         load_scales(dev_s_first, dev_scales[:, :, 0:PASS])
@@ -358,20 +355,19 @@ def tile_bootstrap_signature_cosine_s12_kernel(
         nc.scalar.copy(out=rlen_rows[0:M_TILES, :], in_=rlen_raw[:])
         cat_weave(1, 0, BANK)
         for b in range(2):
-            expo_bank(b, S)
+            expo_bank(b, nc.scalar)
         sig_weave(2)
         cat_unit(0, 2)
         expo_quant(0, 2)
         sig_quant(1)
         cat_quant(1, 0, BANK)
         for b in range(2, 4):
-            expo_bank(b, S)
+            expo_bank(b, nc.scalar)
         turn_rlen()
         sig_quant(2)
         cat_weave_aside(2, "sig2")
-        for g in range(FG):
-            for i in range(HALF_TILES):
-                mix_bank(g, i, ((V, V, S, V), (S, V, S, V), (S, V, S, S))[g][i])
+
+        mix_banks(0, FG * HALF_TILES, 0)
         expo_quant(2, 2)
         mix_quant(0, 0)
         cat_unit(1, 2)
@@ -379,31 +375,26 @@ def tile_bootstrap_signature_cosine_s12_kernel(
         mix_quant(2, 0)
         cat_quant(2, 0, BANK)
 
-        for i in range(HALF_TILES):
-            mix_bank(0, HALF_TILES + i, (V, V, S, V)[i])
-        mix_bank(1, 4, S)
-        mix_bank(1, 5, S)
+        mix_banks(0, 6, 1)
         out_passes([0], 0, BANK)
         mix_quant(0, 1)
-        mix_bank(1, 6, S)
-        mix_bank(1, 7, V)
+        mix_banks(6, 2, 1)
         mix_quant(1, 1)
-        out_store([0], 0, BANK, S)
+        out_store([0], 0, BANK, nc.scalar)
         out_passes([1], 0, BANK)
-        for i in range(HALF_TILES):
-            mix_bank(2, HALF_TILES + i, (V, S, V, S)[i])
+        mix_banks(8, 4, 1)
         mix_quant(2, 1)
-        out_store([1], 0, BANK, S)
+        out_store([1], 0, BANK, nc.scalar)
         for i in range(2, HALF_TILES):
-            out_banks([i], 0, BANK, S)
+            out_banks([i], 0, BANK, nc.scalar)
         for i in range(HALF_TILES, M_TILES):
             cat_piece(i, 1)
-        out_banks([0, 1], BANK, BANK, S)
+        out_banks([0, 1], BANK, BANK, nc.scalar)
         for i in range(2, HALF_TILES):
-            out_banks([i], BANK, BANK, S)
+            out_banks([i], BANK, BANK, nc.scalar)
         for i in range(HALF_TILES, M_TILES - 2):
             for lo in range(0, R, BANK):
-                out_banks([i], lo, BANK, S)
+                out_banks([i], lo, BANK, nc.scalar)
         for i in range(M_TILES - 2, M_TILES):
             for q in range(R // SMALL_BANK):
-                out_banks([i], q * SMALL_BANK, SMALL_BANK, (S, V)[q % 2])
+                out_banks([i], q * SMALL_BANK, SMALL_BANK, in_turn[(q + 1) % 2])

@@ -22,14 +22,15 @@ PASS = P * PACK
 BANK = 512
 KG = K // PASS
 FG = F // PASS
-RUN = 4
+RUN = 8
+NEAR = 4
 QUAD = 32
 SCALE_ROWS = 4
+ROWS = 4
 QUADRANTS = (0, 2, 1, 3)
 M_TILES = M // P
 HALF_TILES = BANK // P
 SMALL_BANK = 256
-PIECES = 4
 ALIGN = 64
 WOVEN_BUFS = 8
 RESULT_BUFS = 10
@@ -45,43 +46,46 @@ def tile_bootstrap_signature_cosine_s12_kernel(
         psum = ctx.enter_context(tc.psum_pool(name="psum", bufs=8))
         ctx.enter_context(tc.manual_schedule())
 
-        dev_w_raw = keep.tile([P, FG, KG, 2 * PASS], U8, name="dev_w_raw", align_bytes=ALIGN)
-        dev_s_first = keep.tile([P, KG, PASS], U8, name="dev_s_first", align_bytes=ALIGN)
-        dev_s_head = keep.tile([P, KG, PASS], U8, name="dev_s_head", align_bytes=ALIGN)
-        dev_s_rest = keep.tile([P, KG, F - PASS], U8, name="dev_s_rest", align_bytes=ALIGN)
-        zero_c = keep.tile([P, BANK], U32, name="zero_c", align_bytes=ALIGN)
-        zero_s = keep.tile([P, BANK], U8, name="zero_s", align_bytes=ALIGN)
-        dev_w = keep.tile([P, FG, KG, 2 * PASS], U8, name="dev_w", align_bytes=ALIGN)
-        dev_s_tail = keep.tile([P, FG - 1, KG, PASS], U8, name="dev_s_tail", align_bytes=ALIGN)
-        dev_s = [dev_s_head[:]] + [dev_s_tail[:, g] for g in range(FG - 1)]
-        boot_w = keep.tile([P, 2, KG, 2 * BANK], U8, name="boot_w", align_bytes=ALIGN)
-        boot_s = [keep.tile([P, KG, BANK], U8, name="boot_s%d" % h, align_bytes=ALIGN) for h in range(2)]
-        base_raw = keep.tile([P, F // 4], BF16, name="base_raw", align_bytes=ALIGN)
-        base_rows = keep.tile([P, F // 4], BF16, name="base_rows", align_bytes=ALIGN)
-        base_cols = keep.tile([P, F // 4], BF16, name="base_cols", align_bytes=ALIGN)
-        rlen_raw = keep.tile([M_TILES, P], BF16, name="rlen_raw", align_bytes=ALIGN)
-        rlen_rows = keep.tile([P, P], F32, name="rlen_rows", align_bytes=ALIGN)
-        rlen_cols = keep.tile([P, M_TILES], F32, name="rlen_cols", align_bytes=ALIGN)
-        ident_f32 = keep.tile([P, P], F32, name="ident_f32", align_bytes=ALIGN)
-        warm = keep.tile([P, 8], F32, name="warm", align_bytes=ALIGN)
-        sig_raw = keep.tile([P, FG, PACK, PASS], BF16, name="sig_raw", align_bytes=ALIGN)
-        sig_c = keep.tile([P, F], U32, name="sig_c", align_bytes=ALIGN)
-        sig_s = keep.tile([P, F], U8, name="sig_s", align_bytes=ALIGN)
-        expo_raw = [keep.tile([P, 2, 2 * J], BF16, name="expo_raw%d" % h, align_bytes=ALIGN) for h in range(2)]
-        expo_t = keep.tile([P, R * PACK], BF16, name="expo_t", align_bytes=ALIGN)
-        expo_c = keep.tile([P, R], U32, name="expo_c", align_bytes=ALIGN)
-        expo_s = keep.tile([P, R], U8, name="expo_s", align_bytes=ALIGN)
-        cat_rows = keep.tile([P, 2, FG, PACK, BANK], BF16, name="cat_rows", align_bytes=ALIGN)
-        cat_c = keep.tile([P, FG, M], U32, name="cat_c", align_bytes=ALIGN)
-        cat_s = keep.tile([P, FG, M], U8, name="cat_s", align_bytes=ALIGN)
-        mix_in = keep.tile([P, FG, R * PACK], BF16, name="mix_in", align_bytes=ALIGN)
-        mix_c = keep.tile([P, FG, R], U32, name="mix_c", align_bytes=ALIGN)
-        mix_s = keep.tile([P, FG, R], U8, name="mix_s", align_bytes=ALIGN)
+        def kept(name, shape, dtype):
+            return keep.tile(shape, dtype, name=name, align_bytes=ALIGN)
+
+        dev_w_raw = [kept("dev_w_raw%d" % g, [P, KG, 2 * PASS], U8) for g in range(FG)]
+        dev_w = [kept("dev_w%d" % g, [P, KG, 2 * PASS], U8) for g in range(FG)]
+        dev_s_first = kept("dev_s_first", [P, KG, PASS], U8)
+        dev_s_head = kept("dev_s_head", [P, KG, PASS], U8)
+        dev_s_rest = kept("dev_s_rest", [P, KG, F - PASS], U8)
+        dev_s_tail = kept("dev_s_tail", [P, KG, F - PASS], U8)
+        dev_s = [dev_s_head[:]] + [dev_s_tail[:, :, g * PASS : (g + 1) * PASS] for g in range(FG - 1)]
+        zero_c = kept("zero_c", [P, BANK], U32)
+        zero_s = kept("zero_s", [P, BANK], U8)
+        boot_w = [kept("boot_w%d" % h, [P, KG, 2 * BANK], U8) for h in range(2)]
+        boot_s = [kept("boot_s%d" % h, [P, KG, BANK], U8) for h in range(2)]
+        base_raw = kept("base_raw", [P, F // 4], BF16)
+        base_rows = kept("base_rows", [P, F // 4], BF16)
+        base_cols = kept("base_cols", [P, F // 4], BF16)
+        rlen_raw = kept("rlen_raw", [P, M_TILES], BF16)
+        rlen_cols = kept("rlen_cols", [P, M_TILES], F32)
+        ident_f32 = kept("ident_f32", [P, P], F32)
+        warm = kept("warm", [P, 8], F32)
+        sig_raw = [kept("sig_raw%d" % g, [P, PACK, PASS], BF16) for g in range(FG)]
+        sig_c = kept("sig_c", [P, F], U32)
+        sig_s = kept("sig_s", [P, F], U8)
+        expo_raw = [kept("expo_raw%d" % h, [P, ROWS * J], BF16) for h in range(2)]
+        expo_sorted = [kept("expo_sorted%d" % h, [P, ROWS * J], BF16) for h in range(2)]
+        expo_t = [kept("expo_t%d" % h, [P, BANK * PACK], BF16) for h in range(2)]
+        expo_c = kept("expo_c", [P, R], U32)
+        expo_s = kept("expo_s", [P, R], U8)
+        cat_rows = kept("cat_rows", [P, 2, FG, PACK, BANK], BF16)
+        cat_c = kept("cat_c", [P, FG, M], U32)
+        cat_s = kept("cat_s", [P, FG, M], U8)
+        mix_in = kept("mix_in", [P, FG, R * PACK], BF16)
+        mix_c = kept("mix_c", [P, FG, R], U32)
+        mix_s = kept("mix_s", [P, FG, R], U8)
 
         in_turn = (nc.vector, nc.scalar)
         staged = {}
         sig_view = sig.rearrange("(p j) (g f) -> p g j f", j=PACK, f=PASS)
-        expo_view = expo.rearrange("(b p i) j -> p b (i j)", p=P, i=2)
+        expo_view = expo.rearrange("(h p i) j -> h p (i j)", p=P, i=ROWS)
         dev_view = dev_words.rearrange("k p (g n) -> p g k n", g=FG)
         boot_view = boot_words.rearrange("k p (h n) -> p h k n", h=2)
 
@@ -92,48 +96,35 @@ def tile_bootstrap_signature_cosine_s12_kernel(
             for r in range(SCALE_ROWS):
                 load_bytes(dst[r:P:QUAD], src.rearrange("k (q r) n -> r q k n", r=SCALE_ROWS)[r])
 
-        def order_first_dev_scales(q):
-            rows = slice(QUAD * q, QUAD * q + SCALE_ROWS)
+        def order_dev(dst, src, words):
             nc.vector.tensor_copy(
-                out=dev_s_head[rows].bitcast(I32).rearrange("p k (t a) -> p k a t", t=PACK),
-                in_=dev_s_first[rows].bitcast(I32).rearrange("p k (a t) -> p k a t", t=PACK),
+                out=dst.rearrange("p k n -> p (k n)").bitcast(I32).rearrange("p (c t q w) -> p c q t w", t=PACK, q=P // RUN, w=words),
+                in_=src.rearrange("p k n -> p (k n)").bitcast(I32).rearrange("p (c q t w) -> p c q t w", t=PACK, q=P // RUN, w=words),
             )
+
+        def order_first_dev_scales(u):
+            rows = slice(QUAD * u, QUAD * u + SCALE_ROWS)
+            order_dev(dev_s_head[rows], dev_s_first[rows], RUN // 4)
 
         def order_dev_words(g):
-            nc.vector.tensor_copy(
-                out=dev_w[:, g].bitcast(I32).rearrange("p k (t a w) -> p k t a w", t=PACK, w=2),
-                in_=dev_w_raw[:, g].bitcast(I32).rearrange("p k (a t w) -> p k t a w", t=PACK, w=2),
-            )
-
-        def order_other_dev_scales():
-            nc.vector.tensor_copy(
-                out=dev_s_tail[:].bitcast(I32).rearrange("p g k (t a) -> p k g a t", t=PACK),
-                in_=dev_s_rest[:].bitcast(I32).rearrange("p k (g a t) -> p k g a t", g=FG - 1, t=PACK),
-            )
+            order_dev(dev_w[g][:], dev_w_raw[g][:], RUN // 2)
 
         def clear(plane):
             nc.vector.memset(plane.rearrange("p k n -> p (k n)").bitcast(I32), 0)
 
         def order_base():
             nc.vector.tensor_copy(
-                out=base_rows[:].rearrange("p (g t a i) -> p g t a i", g=FG, t=PACK, i=RUN),
-                in_=base_raw[:].rearrange("p (g a t i) -> p g t a i", g=FG, t=PACK, i=RUN),
+                out=base_rows[:].rearrange("p (g t q s) -> p g t q s", g=FG, t=PACK, s=RUN),
+                in_=base_raw[:].rearrange("p (g q t s) -> p g t q s", g=FG, t=PACK, s=RUN),
             )
 
         def turn_base(lo, hi):
             nc.vector.transpose(base_cols[:, lo:hi], base_rows[:, lo:hi])
 
-        def warm_up_tensor(words, scales, dtype):
+        def warm_up_tensor(codes):
             bank = psum.tile([P, BANK], F32, name="warm_bank", tag="bank")
-            codes = words.bitcast(dtype)
             nc.tensor.matmul_mx(
-                out=bank[:],
-                lhsT=codes[:, 0:P],
-                lhsT_scale=scales[:, 0:P],
-                rhs=codes,
-                rhs_scale=scales,
-                start=True,
-                stop=True,
+                out=bank[:], lhsT=codes[:, 0:P], lhsT_scale=zero_s[:, 0:P], rhs=codes, rhs_scale=zero_s[:], start=True, stop=True
             )
 
         def warm_up_scalar():
@@ -146,37 +137,35 @@ def tile_bootstrap_signature_cosine_s12_kernel(
             else:
                 nc.vector.tensor_copy(out=dst, in_=src)
 
-        def turn_rlen():
-            bank = psum.tile([P, P], F32, name="rlen_bank", tag="bank")
-            nc.tensor.transpose(bank[:], rlen_rows[:], ident_f32[:])
-            nc.scalar.copy(out=rlen_cols[:], in_=bank[:, 0:M_TILES])
+        def cat_bank(h, g, t):
+            bank = psum.tile([P, BANK], F32, name="cat_bank", tag="bank")
+            col = t * P
+            for k in range(KG):
+                nc.tensor.matmul_mx(
+                    out=bank[:],
+                    lhsT=dev_w[g][:, k, 2 * col : 2 * (col + P)].bitcast(FP4X4),
+                    lhsT_scale=dev_s[g][:, k, col : col + P],
+                    rhs=boot_w[h][:, k, :].bitcast(FP4X4),
+                    rhs_scale=boot_s[h][:, k, :],
+                    start=(k == 0),
+                    stop=(k == KG - 1),
+                )
+            column = QUAD * (PACK * g + t)
+            nc.scalar.activation(
+                out=cat_rows[:, h, g, t, :], in_=bank[:], func=ACT.Relu, bias=base_cols[:, column : column + 1]
+            )
 
         def cat_unit(h, g):
             for t in range(PACK):
-                bank = psum.tile([P, BANK], F32, name="cat_bank", tag="bank")
-                col = t * P
-                for k in range(KG):
-                    nc.tensor.matmul_mx(
-                        out=bank[:],
-                        lhsT=dev_w[:, g, k, 2 * col : 2 * (col + P)].bitcast(FP4X4),
-                        lhsT_scale=dev_s[g][:, k, col : col + P],
-                        rhs=boot_w[:, h, k, :].bitcast(FP4X4),
-                        rhs_scale=boot_s[h][:, k, :],
-                        start=(k == 0),
-                        stop=(k == KG - 1),
-                    )
-                column = QUAD * (PACK * g + t)
-                nc.scalar.activation(
-                    out=cat_rows[:, h, g, t, :], in_=bank[:], func=ACT.Relu, bias=base_cols[:, column : column + 1]
-                )
+                cat_bank(h, g, t)
 
         def cat_weave(g, lo, width):
             h, c = divmod(lo, BANK)
             woven = ring.tile([P, width * PACK], BF16, name="woven", tag="woven", bufs=WOVEN_BUFS, align_bytes=ALIGN)
             for m in range(0, width, P):
                 nc.vector.tensor_copy(
-                    out=woven[:, m * PACK : (m + P) * PACK].rearrange("p (c i t) -> p c t i", i=RUN, t=PACK),
-                    in_=cat_rows[:, h, g, :, c + m : c + m + P].rearrange("p t (c i) -> p c t i", i=RUN),
+                    out=woven[:, m * PACK : (m + P) * PACK].rearrange("p (c i t) -> p c t i", i=NEAR, t=PACK),
+                    in_=cat_rows[:, h, g, :, c + m : c + m + P].rearrange("p t (c i) -> p c t i", i=NEAR),
                 )
             staged[("cat", g, lo)] = woven
 
@@ -205,54 +194,57 @@ def tile_bootstrap_signature_cosine_s12_kernel(
 
         def sig_weave(g):
             woven = ring.tile([P, BANK * PACK], BF16, name="sig_woven", tag="sig%d" % g, bufs=1, align_bytes=ALIGN)
-            dst = woven[:].rearrange("p (t q a i j) -> p q a t j i", t=PACK, q=PIECES, i=RUN, j=PACK)
-            src = sig_raw[:, g].rearrange("p j (q a t i) -> p q a t j i", q=PIECES, t=PACK, i=RUN)
-            for q in range(PIECES):
-                nc.vector.tensor_copy(out=dst[:, q], in_=src[:, q])
+            dst = woven[:].rearrange("p (t q a i j) -> p t q a j i", t=PACK, a=RUN // NEAR, i=NEAR, j=PACK)
+            src = sig_raw[g][:].rearrange("p j (q t a i) -> p t q a j i", t=PACK, a=RUN // NEAR, i=NEAR)
+            for t in range(PACK):
+                nc.vector.tensor_copy(out=dst[:, t], in_=src[:, t])
             staged[("sig", g)] = woven
 
         def sig_quant(g):
             n = slice(g * PASS, (g + 1) * PASS)
             nc.vector.quantize_mx(out=sig_c[:, n].bitcast(FP8X4), scales=sig_s[:, n], in_=staged[("sig", g)][:])
 
-        def expo_bank(b, eng):
+        def expo_sort(h):
+            nc.vector.tensor_copy(
+                out=expo_sorted[h][:].bitcast(F32).rearrange("p (i u w) -> p i w u", i=ROWS, u=2),
+                in_=expo_raw[h][:].bitcast(F32).rearrange("p (i w u) -> p i w u", i=ROWS, u=2),
+            )
+
+        def expo_bank(h, b, eng):
             bank = psum.tile([P, 2, 2, P], F32, name="expo_bank", tag="bank")
             for i in range(2):
                 for u in range(2):
-                    words = expo_raw[b // 2][:, b % 2, i * J : (i + 1) * J].bitcast(F32)
-                    nc.tensor.transpose(bank[:, i, u, :], words[:, u : J // 2 : 2], ident_f32[:])
-            dst = expo_t[:, b * 2 * PASS : (b + 1) * 2 * PASS].bitcast(F32).rearrange("p (r i u) -> p r i u", i=2, u=2)
-            src = bank[:].rearrange("p i u r -> p r i u")
-            copy_out(eng, dst, src)
+                    first = (2 * (2 * b + i) + u) * P
+                    nc.tensor.transpose(bank[:, i, u, :], expo_sorted[h][:].bitcast(F32)[:, first : first + P], ident_f32[:])
+            dst = expo_t[h][:].bitcast(F32).rearrange("p (r b i u) -> p b r i u", b=2, i=2, u=2)
+            copy_out(eng, dst[:, b], bank[:].rearrange("p i u r -> p r i u"))
 
-        def expo_quant(first, count):
-            n = slice(first * 2 * P, (first + count) * 2 * P)
-            nc.vector.quantize_mx(
-                out=expo_c[:, n].bitcast(FP8X4), scales=expo_s[:, n], in_=expo_t[:, n.start * PACK : n.stop * PACK]
-            )
+        def expo_quant(h):
+            n = slice(h * BANK, (h + 1) * BANK)
+            nc.vector.quantize_mx(out=expo_c[:, n].bitcast(FP8X4), scales=expo_s[:, n], in_=expo_t[h][:])
 
-        def mix_bank(g, i, eng):
+        def mix_bank(n, h, eng):
+            g, i = divmod(n, HALF_TILES)
+            tile = h * HALF_TILES + i
             bank = psum.tile([P, PACK, P], F32, name="mix_bank", tag="bank")
-            n = slice(i * P, (i + 1) * P)
+            r = slice(tile * P, (tile + 1) * P)
             for t in range(PACK):
                 c = slice(g * PASS + t * P, g * PASS + (t + 1) * P)
                 nc.tensor.matmul_mx(
                     out=bank[:, t, :],
                     lhsT=sig_c[:, c].bitcast(FP8X4),
                     lhsT_scale=sig_s[:, c],
-                    rhs=expo_c[:, n].bitcast(FP8X4),
-                    rhs_scale=expo_s[:, n],
+                    rhs=expo_c[:, r].bitcast(FP8X4),
+                    rhs_scale=expo_s[:, r],
                     start=True,
                     stop=True,
                 )
-            dst = mix_in[:, g, i * PASS : (i + 1) * PASS].rearrange("p (r t) -> p r t", t=PACK)
-            src = bank[:].rearrange("p t r -> p r t")
-            copy_out(eng, dst, src)
+            dst = mix_in[:, g, tile * PASS : (tile + 1) * PASS].rearrange("p (r t) -> p r t", t=PACK)
+            copy_out(eng, dst, bank[:].rearrange("p t r -> p r t"))
 
         def mix_banks(first, count, h):
             for n in range(first, first + count):
-                g, i = divmod(n, HALF_TILES)
-                mix_bank(g, h * HALF_TILES + i, in_turn[n % 2])
+                mix_bank(n, h, in_turn[n % 2])
 
         def mix_quant(g, h):
             n = slice(h * BANK, (h + 1) * BANK)
@@ -264,7 +256,7 @@ def tile_bootstrap_signature_cosine_s12_kernel(
 
         def out_passes(tiles, lo, width):
             n = slice(lo, lo + width)
-            banks = [psum.tile([P, width], F32, name="out_bank", tag="bank") for _ in tiles]
+            banks = [psum.tile([P, width], F32, name="out_bank", tag="bank") for tile in tiles]
             for g in range(FG):
                 for i, bank in zip(tiles, banks):
                     m = slice(i * P, (i + 1) * P)
@@ -296,10 +288,8 @@ def tile_bootstrap_signature_cosine_s12_kernel(
             out_passes(tiles, lo, width)
             out_store(tiles, lo, width, eng)
 
-
-        make_identity(nc, ident_f32[:])
-        warm_up_scalar()
         clear(dev_s_rest[:])
+        warm_up_scalar()
         clear(boot_s[0][:])
         zeros = dev_s_rest[:].rearrange("p k n -> p (k n)").bitcast(BF16)
         for n in (slice(0, BANK // 2), slice(BANK // 2, BANK)):
@@ -307,34 +297,36 @@ def tile_bootstrap_signature_cosine_s12_kernel(
         clear(dev_s_head[:])
         nc.vector.memset(base_raw[:].bitcast(I32), 0)
         clear(boot_s[1][:])
-        nc.vector.memset(rlen_rows[:], 0.0)
+        nc.vector.memset(ident_f32[:], 0.0)
 
         load_scales(dev_s_first, dev_scales[:, :, 0:PASS])
-        load_bytes(dev_w_raw[:, 0], dev_view[:, 0])
-        load_bytes(boot_w[:, 0], boot_view[:, 0])
+        load_bytes(dev_w_raw[0][:], dev_view[:, 0])
+        load_bytes(boot_w[0][:], boot_view[:, 0])
         load_scales(boot_s[0], boot_scales[:, :, 0:BANK])
         nc.sync.dma_start(
             out=base_raw[0:P:QUAD, :].rearrange("q (g c) -> q g c", g=FG),
             in_=base.rearrange("(g q c) -> q g c", g=FG, q=P // QUAD),
         )
-        load_bytes(boot_w[:, 1], boot_view[:, 1])
+        load_bytes(boot_w[1][:], boot_view[:, 1])
         load_scales(boot_s[1], boot_scales[:, :, BANK:M])
-        load_bytes(dev_w_raw[:, 1], dev_view[:, 1])
+        load_bytes(dev_w_raw[1][:], dev_view[:, 1])
         load_scales(dev_s_rest, dev_scales[:, :, PASS:F])
-        nc.sync.dma_start(out=sig_raw[:, 0], in_=sig_view[:, 0])
-        load_bytes(dev_w_raw[:, 2], dev_view[:, 2])
-        nc.sync.dma_start(out=sig_raw[:, 1], in_=sig_view[:, 1])
-        nc.sync.dma_start(out=expo_raw[0][:], in_=expo_view[:, 0:2])
-        nc.sync.dma_start(out=rlen_raw[:], in_=rlen.rearrange("(i p) -> i p", p=P))
-        nc.sync.dma_start(out=sig_raw[:, 2], in_=sig_view[:, 2])
-        nc.sync.dma_start(out=expo_raw[1][:], in_=expo_view[:, 2:4])
+        nc.sync.dma_start(out=expo_raw[0][:], in_=expo_view[0])
+        nc.sync.dma_start(out=expo_raw[1][:], in_=expo_view[1])
+        nc.sync.dma_start(out=sig_raw[0][:], in_=sig_view[:, 0])
+        load_bytes(dev_w_raw[2][:], dev_view[:, 2])
+        nc.sync.dma_start(out=sig_raw[1][:], in_=sig_view[:, 1])
+        nc.sync.dma_start(out=sig_raw[2][:], in_=sig_view[:, 2])
+        with nc.allow_non_contiguous_dma(reason="one value of rlen to a partition and output tile"):
+            nc.sync.dma_start(out=rlen_raw[:], in_=rlen.rearrange("(i p) -> p i", p=P))
 
-        warm_up_tensor(zero_c[:], zero_s[:], FP8X4)
-        warm_up_tensor(zero_c[:], zero_s[:], FP8X4)
-        for q in QUADRANTS:
-            order_first_dev_scales(q)
-        warm_up_tensor(dev_w_raw[:, 0, 0, :], dev_s_head[:, 0, :], FP4X4)
-        warm_up_tensor(boot_w[:, 0, 0, :], dev_s_head[:, 0, :], FP4X4)
+        make_identity(nc, ident_f32[:], nomemset=True)
+        warm_up_tensor(zero_c[:].bitcast(FP8X4))
+        warm_up_tensor(zero_c[:].bitcast(FP8X4))
+        for u in QUADRANTS:
+            order_first_dev_scales(u)
+        warm_up_tensor(dev_w_raw[0][:, 0, :].bitcast(FP4X4))
+        warm_up_tensor(boot_w[0][:, 0, :].bitcast(FP4X4))
         order_dev_words(0)
         order_base()
         turn_base(0, P)
@@ -343,48 +335,49 @@ def tile_bootstrap_signature_cosine_s12_kernel(
         turn_base(P, F // 4)
         cat_unit(1, 0)
         order_dev_words(1)
-        order_other_dev_scales()
+        order_dev(dev_s_tail[:], dev_s_rest[:], RUN // 4)
         cat_unit(0, 1)
         cat_weave(0, 0, BANK)
-        sig_weave(0)
-        order_dev_words(2)
+        expo_sort(0)
+        expo_sort(1)
         cat_quant(0, 0, BANK)
-        sig_quant(0)
+        for h in range(2):
+            for b in range(2):
+                expo_bank(h, b, nc.scalar)
+        sig_weave(0)
         cat_unit(1, 1)
+        order_dev_words(2)
+        sig_quant(0)
         sig_weave(1)
-        nc.scalar.copy(out=rlen_rows[0:M_TILES, :], in_=rlen_raw[:])
-        cat_weave(1, 0, BANK)
-        for b in range(2):
-            expo_bank(b, nc.scalar)
-        sig_weave(2)
         cat_unit(0, 2)
-        expo_quant(0, 2)
+        expo_quant(0)
         sig_quant(1)
-        cat_quant(1, 0, BANK)
-        for b in range(2, 4):
-            expo_bank(b, nc.scalar)
-        turn_rlen()
+        sig_weave(2)
+        expo_quant(1)
         sig_quant(2)
-        cat_weave_aside(2, "sig2")
+        cat_weave_aside(1, "sig2")
+        cat_weave_aside(2, "sig1")
 
-        mix_banks(0, FG * HALF_TILES, 0)
-        expo_quant(2, 2)
+        for t in range(PACK):
+            mix_bank(3 * t, 0, nc.vector)
+            mix_bank(3 * t + 1, 0, nc.scalar)
+            mix_bank(3 * t + 2, 0, nc.vector)
+            cat_bank(1, 2, t)
+        nc.scalar.copy(out=rlen_cols[:], in_=rlen_raw[:])
+
+        mix_bank(0, 1, nc.vector)
         mix_quant(0, 0)
-        cat_unit(1, 2)
         mix_quant(1, 0)
+        cat_quant(1, 0, BANK)
         mix_quant(2, 0)
         cat_quant(2, 0, BANK)
-
-        mix_banks(0, 6, 1)
-        out_passes([0], 0, BANK)
-        mix_quant(0, 1)
-        mix_banks(6, 2, 1)
-        mix_quant(1, 1)
-        out_store([0], 0, BANK, nc.scalar)
-        out_passes([1], 0, BANK)
-        mix_banks(8, 4, 1)
-        mix_quant(2, 1)
-        out_store([1], 0, BANK, nc.scalar)
+        for n in range(1, 10):
+            mix_bank(n, 1, nc.scalar)
+        for n in range(10, 12):
+            mix_bank(n, 1, nc.vector)
+        out_banks([0, 1], 0, BANK, nc.scalar)
+        for g in range(FG):
+            mix_quant(g, 1)
         for i in range(2, HALF_TILES):
             out_banks([i], 0, BANK, nc.scalar)
         for i in range(HALF_TILES, M_TILES):
@@ -395,6 +388,7 @@ def tile_bootstrap_signature_cosine_s12_kernel(
         for i in range(HALF_TILES, M_TILES - 2):
             for lo in range(0, R, BANK):
                 out_banks([i], lo, BANK, nc.scalar)
-        for i in range(M_TILES - 2, M_TILES):
-            for q in range(R // SMALL_BANK):
-                out_banks([i], q * SMALL_BANK, SMALL_BANK, in_turn[(q + 1) % 2])
+        small = [(i, lo, SMALL_BANK) for i in range(M_TILES - 2, M_TILES) for lo in range(0, R, SMALL_BANK)]
+        small = small[:-1] + [(M_TILES - 1, lo, P) for lo in range(R - SMALL_BANK, R, P)]
+        for n, (i, lo, width) in enumerate(small):
+            out_banks([i], lo, width, in_turn[(n + 1) % 2])

@@ -297,7 +297,6 @@ def tile_bootstrap_signature_cosine_s12_kernel(
         clear(dev_s_head[:])
         nc.vector.memset(base_raw[:].bitcast(I32), 0)
         clear(boot_s[1][:])
-        nc.vector.memset(ident_f32[:], 0.0)
 
         load_scales(dev_s_first, dev_scales[:, :, 0:PASS])
         load_bytes(dev_w_raw[0][:], dev_view[:, 0])
@@ -320,7 +319,6 @@ def tile_bootstrap_signature_cosine_s12_kernel(
         with nc.allow_non_contiguous_dma(reason="one value of rlen to a partition and output tile"):
             nc.sync.dma_start(out=rlen_raw[:], in_=rlen.rearrange("(i p) -> p i", p=P))
 
-        make_identity(nc, ident_f32[:], nomemset=True)
         warm_up_tensor(zero_c[:].bitcast(FP8X4))
         warm_up_tensor(zero_c[:].bitcast(FP8X4))
         for u in QUADRANTS:
@@ -333,6 +331,8 @@ def tile_bootstrap_signature_cosine_s12_kernel(
 
         cat_unit(0, 0)
         turn_base(P, F // 4)
+        nc.vector.memset(ident_f32[:], 0.0)
+        make_identity(nc, ident_f32[:], nomemset=True)
         cat_unit(1, 0)
         order_dev_words(1)
         order_dev(dev_s_tail[:], dev_s_rest[:], RUN // 4)
@@ -358,11 +358,10 @@ def tile_bootstrap_signature_cosine_s12_kernel(
         cat_weave_aside(1, "sig2")
         cat_weave_aside(2, "sig1")
 
-        for t in range(PACK):
-            mix_bank(3 * t, 0, nc.vector)
-            mix_bank(3 * t + 1, 0, nc.scalar)
-            mix_bank(3 * t + 2, 0, nc.vector)
-            cat_bank(1, 2, t)
+        mix_banks(0, 2 * HALF_TILES, 0)
+        for n in range(2 * HALF_TILES, FG * HALF_TILES):
+            mix_bank(n, 0, nc.vector)
+        cat_unit(1, 2)
         nc.scalar.copy(out=rlen_cols[:], in_=rlen_raw[:])
 
         mix_bank(0, 1, nc.vector)

@@ -387,7 +387,6 @@ def tile_bootstrap_signature_cosine_s12_kernel(
         for i in range(HALF_TILES, M_TILES - 2):
             for lo in range(0, R, BANK):
                 out_banks([i], lo, BANK, nc.scalar)
-        small = [(i, lo, SMALL_BANK) for i in range(M_TILES - 2, M_TILES) for lo in range(0, R, SMALL_BANK)]
-        small = small[:-1] + [(M_TILES - 1, lo, P) for lo in range(R - SMALL_BANK, R, P)]
-        for n, (i, lo, width) in enumerate(small):
-            out_banks([i], lo, width, in_turn[(n + 1) % 2])
+        for i in range(M_TILES - 2, M_TILES):
+            for q in range(R // SMALL_BANK):
+                out_banks([i], q * SMALL_BANK, SMALL_BANK, in_turn[(q + 1) % 2])

@@ -137,7 +137,7 @@ def tile_bootstrap_signature_cosine_s12_kernel(
             else:
                 nc.vector.tensor_copy(out=dst, in_=src)
 
-        def cat_bank(h, g, t):
+        def cat_bank(h, g, t, eng):
             bank = psum.tile([P, BANK], F32, name="cat_bank", tag="bank")
             col = t * P
             for k in range(KG):
@@ -151,13 +151,15 @@ def tile_bootstrap_signature_cosine_s12_kernel(
                     stop=(k == KG - 1),
                 )
             column = QUAD * (PACK * g + t)
-            nc.scalar.activation(
-                out=cat_rows[:, h, g, t, :], in_=bank[:], func=ACT.Relu, bias=base_cols[:, column : column + 1]
-            )
+            rows, bias = cat_rows[:, h, g, t, :], base_cols[:, column : column + 1]
+            if eng is nc.scalar:
+                nc.scalar.activation(out=rows, in_=bank[:], func=ACT.Relu, bias=bias)
+            else:
+                nc.vector.tensor_scalar(out=rows, in0=bank[:], scalar1=bias, scalar2=0.0, op0=ALU.add, op1=ALU.max)
 
         def cat_unit(h, g):
             for t in range(PACK):
-                cat_bank(h, g, t)
+                cat_bank(h, g, t, nc.scalar)
 
         def cat_weave(g, lo, width):
             h, c = divmod(lo, BANK)
@@ -184,6 +186,11 @@ def tile_bootstrap_signature_cosine_s12_kernel(
         def cat_quant(g, lo, width):
             n = slice(lo, lo + width)
             nc.vector.quantize_mx(out=cat_c[:, g, n].bitcast(FP8X4), scales=cat_s[:, g, n], in_=staged[("cat", g, lo)][:])
+
+        def cat_quant_pair(g, pair):
+            n = slice(pair * 2 * P, (pair + 1) * 2 * P)
+            woven = staged[("cat", g, 0)][:, n.start * PACK : n.stop * PACK]
+            nc.vector.quantize_mx(out=cat_c[:, g, n].bitcast(FP8X4), scales=cat_s[:, g, n], in_=woven)
 
         def cat_piece(first, count):
             lo, width = first * P, count * P
@@ -329,10 +336,11 @@ def tile_bootstrap_signature_cosine_s12_kernel(
         order_base()
         turn_base(0, P)
 
-        cat_unit(0, 0)
         turn_base(P, F // 4)
         nc.vector.memset(ident_f32[:], 0.0)
         make_identity(nc, ident_f32[:], nomemset=True)
+        for t in range(PACK):
+            cat_bank(0, 0, t, nc.vector if t == PACK - 1 else nc.scalar)
         cat_unit(1, 0)
         order_dev_words(1)
         order_dev(dev_s_tail[:], dev_s_rest[:], RUN // 4)
@@ -358,19 +366,25 @@ def tile_bootstrap_signature_cosine_s12_kernel(
         cat_weave_aside(1, "sig2")
         cat_weave_aside(2, "sig1")
 
+        for t in range(PACK // 2):
+            cat_bank(1, 2, t, nc.scalar)
         mix_banks(0, 2 * HALF_TILES, 0)
         for n in range(2 * HALF_TILES, FG * HALF_TILES):
             mix_bank(n, 0, nc.vector)
-        cat_unit(1, 2)
+        for t in range(PACK // 2, PACK):
+            cat_bank(1, 2, t, nc.scalar)
         nc.scalar.copy(out=rlen_cols[:], in_=rlen_raw[:])
 
-        mix_bank(0, 1, nc.vector)
+        for n in range(2):
+            mix_bank(n, 1, nc.vector)
         mix_quant(0, 0)
         mix_quant(1, 0)
-        cat_quant(1, 0, BANK)
+        cat_quant_pair(1, 0)
         mix_quant(2, 0)
-        cat_quant(2, 0, BANK)
-        for n in range(1, 10):
+        cat_quant_pair(2, 0)
+        cat_quant_pair(1, 1)
+        cat_quant_pair(2, 1)
+        for n in range(2, 10):
             mix_bank(n, 1, nc.scalar)
         for n in range(10, 12):
             mix_bank(n, 1, nc.vector)
@@ -381,9 +395,8 @@ def tile_bootstrap_signature_cosine_s12_kernel(
             out_banks([i], 0, BANK, nc.scalar)
         for i in range(HALF_TILES, M_TILES):
             cat_piece(i, 1)
-        out_banks([0, 1], BANK, BANK, nc.scalar)
-        for i in range(2, HALF_TILES):
-            out_banks([i], BANK, BANK, nc.scalar)
+        out_banks([0, 1, 2], BANK, BANK, nc.scalar)
+        out_banks([3], BANK, BANK, nc.scalar)
         for i in range(HALF_TILES, M_TILES - 2):
             for lo in range(0, R, BANK):
                 out_banks([i], lo, BANK, nc.scalar)

@@ -246,8 +246,8 @@ def tile_bootstrap_signature_cosine_s12_kernel(
                     start=True,
                     stop=True,
                 )
-            dst = mix_in[:, g, tile * PASS : (tile + 1) * PASS].rearrange("p (r t) -> p r t", t=PACK)
-            copy_out(eng, dst, bank[:].rearrange("p t r -> p r t"))
+            dst = mix_in[:, g, tile * PASS : (tile + 1) * PASS].rearrange("p (c i t) -> p c t i", i=NEAR, t=PACK)
+            copy_out(eng, dst, bank[:].rearrange("p t (c i) -> p c t i", i=NEAR))
 
         def mix_banks(first, count, h):
             for n in range(first, first + count):

from contextlib import ExitStack

import concourse.mybir as mybir
from concourse.masks import make_identity

M, K, F, R, J = 1024, 1024, 1536, 1024, 512
FLOPS = 2 * M * K * F + 2 * R * J * F + 2 * M * R * F

F32 = mybir.dt.float32
BF16 = mybir.dt.bfloat16
I32 = mybir.dt.int32
U32 = mybir.dt.uint32
U8 = mybir.dt.uint8
FP8X4 = mybir.dt.float8_e4m3fn_x4
FP4X4 = mybir.dt.float4_e2m1fn_x4
ACT = mybir.ActivationFunctionType
ALU = mybir.AluOpType

P = 128
PACK = 4
PASS = P * PACK
BANK = 512
KG = K // PASS
FG = F // PASS
RUN = 8
NEAR = 4
QUAD = 32
SCALE_ROWS = 4
ROWS = 4
QUADRANTS = (0, 2, 1, 3)
M_TILES = M // P
HALF_TILES = BANK // P
SMALL_BANK = 256
ALIGN = 64
WOVEN_BUFS = 8
RESULT_BUFS = 10


def tile_bootstrap_signature_cosine_s12_kernel(
    tc, boot_words, boot_scales, dev_words, dev_scales, base, expo, sig, rlen, out
):
    nc = tc.nc
    with ExitStack() as ctx:
        keep = ctx.enter_context(tc.tile_pool(name="keep", bufs=1))
        ring = ctx.enter_context(tc.tile_pool(name="ring", bufs=2))
        psum = ctx.enter_context(tc.psum_pool(name="psum", bufs=8))
        ctx.enter_context(tc.manual_schedule())

        def kept(name, shape, dtype):
            return keep.tile(shape, dtype, name=name, align_bytes=ALIGN)

        dev_w_raw = [kept("dev_w_raw%d" % g, [P, KG, 2 * PASS], U8) for g in range(FG)]
        dev_w = [kept("dev_w%d" % g, [P, KG, 2 * PASS], U8) for g in range(FG)]
        dev_s_first = kept("dev_s_first", [P, KG, PASS], U8)
        dev_s_head = kept("dev_s_head", [P, KG, PASS], U8)
        dev_s_rest = kept("dev_s_rest", [P, KG, F - PASS], U8)
        dev_s_tail = kept("dev_s_tail", [P, KG, F - PASS], U8)
        dev_s = [dev_s_head[:]] + [dev_s_tail[:, :, g * PASS : (g + 1) * PASS] for g in range(FG - 1)]
        zero_c = kept("zero_c", [P, BANK], U32)
        zero_s = kept("zero_s", [P, BANK], U8)
        boot_w = [kept("boot_w%d" % h, [P, KG, 2 * BANK], U8) for h in range(2)]
        boot_s = [kept("boot_s%d" % h, [P, KG, BANK], U8) for h in range(2)]
        base_raw = kept("base_raw", [P, F // 4], BF16)
        base_rows = kept("base_rows", [P, F // 4], BF16)
        base_cols = kept("base_cols", [P, F // 4], BF16)
        rlen_raw = kept("rlen_raw", [P, M_TILES], BF16)
        rlen_cols = kept("rlen_cols", [P, M_TILES], F32)
        ident_f32 = kept("ident_f32", [P, P], F32)
        warm = kept("warm", [P, 8], F32)
        sig_raw = [kept("sig_raw%d" % g, [P, PACK, PASS], BF16) for g in range(FG)]
        sig_c = kept("sig_c", [P, F], U32)
        sig_s = kept("sig_s", [P, F], U8)
        expo_raw = [kept("expo_raw%d" % h, [P, ROWS * J], BF16) for h in range(2)]
        expo_sorted = [kept("expo_sorted%d" % h, [P, ROWS * J], BF16) for h in range(2)]
        expo_t = [kept("expo_t%d" % h, [P, BANK * PACK], BF16) for h in range(2)]
        expo_c = kept("expo_c", [P, R], U32)
        expo_s = kept("expo_s", [P, R], U8)
        cat_rows = kept("cat_rows", [P, 2, FG, PACK, BANK], BF16)
        cat_c = kept("cat_c", [P, FG, M], U32)
        cat_s = kept("cat_s", [P, FG, M], U8)
        mix_in = kept("mix_in", [P, FG, R * PACK], BF16)
        mix_c = kept("mix_c", [P, FG, R], U32)
        mix_s = kept("mix_s", [P, FG, R], U8)

        in_turn = (nc.vector, nc.scalar)
        staged = {}
        sig_view = sig.rearrange("(p j) (g f) -> p g j f", j=PACK, f=PASS)
        expo_view = expo.rearrange("(h p i) j -> h p (i j)", p=P, i=ROWS)
        dev_view = dev_words.rearrange("k p (g n) -> p g k n", g=FG)
        boot_view = boot_words.rearrange("k p (h n) -> p h k n", h=2)

        def load_bytes(dst, src):
            nc.sync.dma_start(out=dst.bitcast(I32), in_=src.bitcast(I32))

        def load_scales(dst, src):
            for r in range(SCALE_ROWS):
                load_bytes(dst[r:P:QUAD], src.rearrange("k (q r) n -> r q k n", r=SCALE_ROWS)[r])

        def order_dev(dst, src, words):
            nc.vector.tensor_copy(
                out=dst.rearrange("p k n -> p (k n)").bitcast(I32).rearrange("p (c t q w) -> p c q t w", t=PACK, q=P // RUN, w=words),
                in_=src.rearrange("p k n -> p (k n)").bitcast(I32).rearrange("p (c q t w) -> p c q t w", t=PACK, q=P // RUN, w=words),
            )

        def order_first_dev_scales(u):
            rows = slice(QUAD * u, QUAD * u + SCALE_ROWS)
            order_dev(dev_s_head[rows], dev_s_first[rows], RUN // 4)

        def order_dev_words(g):
            order_dev(dev_w[g][:], dev_w_raw[g][:], RUN // 2)

        def clear(plane):
            nc.vector.memset(plane.rearrange("p k n -> p (k n)").bitcast(I32), 0)

        def order_base():
            nc.vector.tensor_copy(
                out=base_rows[:].rearrange("p (g t q s) -> p g t q s", g=FG, t=PACK, s=RUN),
                in_=base_raw[:].rearrange("p (g q t s) -> p g t q s", g=FG, t=PACK, s=RUN),
            )

        def turn_base(lo, hi):
            nc.vector.transpose(base_cols[:, lo:hi], base_rows[:, lo:hi])

        def warm_up_tensor(codes):
            bank = psum.tile([P, BANK], F32, name="warm_bank", tag="bank")
            nc.tensor.matmul_mx(
                out=bank[:], lhsT=codes[:, 0:P], lhsT_scale=zero_s[:, 0:P], rhs=codes, rhs_scale=zero_s[:], start=True, stop=True
            )

        def warm_up_scalar():
            nc.vector.memset(warm[:], 0.0)
            nc.scalar.activation(out=warm[:, 4:5], in_=warm[:, 0:1], func=ACT.Relu)

        def copy_out(eng, dst, src):
            if eng is nc.scalar:
                nc.scalar.copy(out=dst, in_=src)
            else:
                nc.vector.tensor_copy(out=dst, in_=src)

        def cat_bank(h, g, t, eng):
            bank = psum.tile([P, BANK], F32, name="cat_bank", tag="bank")
            col = t * P
            for k in range(KG):
                nc.tensor.matmul_mx(
                    out=bank[:],
                    lhsT=dev_w[g][:, k, 2 * col : 2 * (col + P)].bitcast(FP4X4),
                    lhsT_scale=dev_s[g][:, k, col : col + P],
                    rhs=boot_w[h][:, k, :].bitcast(FP4X4),
                    rhs_scale=boot_s[h][:, k, :],
                    start=(k == 0),
                    stop=(k == KG - 1),
                )
            column = QUAD * (PACK * g + t)
            rows, bias = cat_rows[:, h, g, t, :], base_cols[:, column : column + 1]
            if eng is nc.scalar:
                nc.scalar.activation(out=rows, in_=bank[:], func=ACT.Relu, bias=bias)
            else:
                nc.vector.tensor_scalar(out=rows, in0=bank[:], scalar1=bias, scalar2=0.0, op0=ALU.add, op1=ALU.max)

        def cat_unit(h, g):
            for t in range(PACK):
                cat_bank(h, g, t, nc.scalar)

        def cat_weave(g, lo, width):
            h, c = divmod(lo, BANK)
            woven = ring.tile([P, width * PACK], BF16, name="woven", tag="woven", bufs=WOVEN_BUFS, align_bytes=ALIGN)
            for m in range(0, width, P):
                nc.vector.tensor_copy(
                    out=woven[:, m * PACK : (m + P) * PACK].rearrange("p (c i t) -> p c t i", i=NEAR, t=PACK),
                    in_=cat_rows[:, h, g, :, c + m : c + m + P].rearrange("p t (c i) -> p c t i", i=NEAR),
                )
            staged[("cat", g, lo)] = woven

        def cat_weave_aside(g, tag):
            woven = ring.tile([P, BANK * PACK], BF16, name="woven_aside", tag=tag, bufs=1, align_bytes=ALIGN)
            nc.gpsimd.tensor_scalar(
                out=woven[:].rearrange("p (c t) -> p c t", t=PACK),
                in0=cat_rows[:, 0, g].rearrange("p t c -> p c t"),
                scalar1=1.0,
                scalar2=0.0,
                op0=ALU.mult,
                op1=ALU.add,
            )
            staged[("cat", g, 0)] = woven

        def cat_quant(g, lo, width):
            n = slice(lo, lo + width)
            nc.vector.quantize_mx(out=cat_c[:, g, n].bitcast(FP8X4), scales=cat_s[:, g, n], in_=staged[("cat", g, lo)][:])

        def cat_quant_pair(g, pair):
            n = slice(pair * 2 * P, (pair + 1) * 2 * P)
            woven = staged[("cat", g, 0)][:, n.start * PACK : n.stop * PACK]
            nc.vector.quantize_mx(out=cat_c[:, g, n].bitcast(FP8X4), scales=cat_s[:, g, n], in_=woven)

        def cat_piece(first, count):
            lo, width = first * P, count * P
            for g in range(FG):
                cat_weave(g, lo, width)
            for g in range(FG):
                cat_quant(g, lo, width)

        def sig_weave(g):
            woven = ring.tile([P, BANK * PACK], BF16, name="sig_woven", tag="sig%d" % g, bufs=1, align_bytes=ALIGN)
            dst = woven[:].rearrange("p (t q a i j) -> p t q a j i", t=PACK, a=RUN // NEAR, i=NEAR, j=PACK)
            src = sig_raw[g][:].rearrange("p j (q t a i) -> p t q a j i", t=PACK, a=RUN // NEAR, i=NEAR)
            for t in range(PACK):
                nc.vector.tensor_copy(out=dst[:, t], in_=src[:, t])
            staged[("sig", g)] = woven

        def sig_quant(g):
            n = slice(g * PASS, (g + 1) * PASS)
            nc.vector.quantize_mx(out=sig_c[:, n].bitcast(FP8X4), scales=sig_s[:, n], in_=staged[("sig", g)][:])

        def expo_sort(h):
            nc.vector.tensor_copy(
                out=expo_sorted[h][:].bitcast(F32).rearrange("p (i u w) -> p i w u", i=ROWS, u=2),
                in_=expo_raw[h][:].bitcast(F32).rearrange("p (i w u) -> p i w u", i=ROWS, u=2),
            )

        def expo_bank(h, b, eng):
            bank = psum.tile([P, 2, 2, P], F32, name="expo_bank", tag="bank")
            for i in range(2):
                for u in range(2):
                    first = (2 * (2 * b + i) + u) * P
                    nc.tensor.transpose(bank[:, i, u, :], expo_sorted[h][:].bitcast(F32)[:, first : first + P], ident_f32[:])
            dst = expo_t[h][:].bitcast(F32).rearrange("p (r b i u) -> p b r i u", b=2, i=2, u=2)
            copy_out(eng, dst[:, b], bank[:].rearrange("p i u r -> p r i u"))

        def expo_quant(h):
            n = slice(h * BANK, (h + 1) * BANK)
            nc.vector.quantize_mx(out=expo_c[:, n].bitcast(FP8X4), scales=expo_s[:, n], in_=expo_t[h][:])

        def mix_bank(n, h, eng):
            g, i = divmod(n, HALF_TILES)
            tile = h * HALF_TILES + i
            bank = psum.tile([P, PACK, P], F32, name="mix_bank", tag="bank")
            r = slice(tile * P, (tile + 1) * P)
            for t in range(PACK):
                c = slice(g * PASS + t * P, g * PASS + (t + 1) * P)
                nc.tensor.matmul_mx(
                    out=bank[:, t, :],
                    lhsT=sig_c[:, c].bitcast(FP8X4),
                    lhsT_scale=sig_s[:, c],
                    rhs=expo_c[:, r].bitcast(FP8X4),
                    rhs_scale=expo_s[:, r],
                    start=True,
                    stop=True,
                )
            dst = mix_in[:, g, tile * PASS : (tile + 1) * PASS].rearrange("p (c i t) -> p c t i", i=NEAR, t=PACK)
            copy_out(eng, dst, bank[:].rearrange("p t (c i) -> p c t i", i=NEAR))

        def mix_banks(first, count, h):
            for n in range(first, first + count):
                mix_bank(n, h, in_turn[n % 2])

        def mix_quant(g, h):
            n = slice(h * BANK, (h + 1) * BANK)
            nc.vector.quantize_mx(
                out=mix_c[:, g, n].bitcast(FP8X4),
                scales=mix_s[:, g, n],
                in_=mix_in[:, g, n.start * PACK : n.stop * PACK],
            )

        def out_passes(tiles, lo, width):
            n = slice(lo, lo + width)
            banks = [psum.tile([P, width], F32, name="out_bank", tag="bank") for tile in tiles]
            for g in range(FG):
                for i, bank in zip(tiles, banks):
                    m = slice(i * P, (i + 1) * P)
                    nc.tensor.matmul_mx(
                        out=bank[:],
                        lhsT=cat_c[:, g, m].bitcast(FP8X4),
                        lhsT_scale=cat_s[:, g, m],
                        rhs=mix_c[:, g, n].bitcast(FP8X4),
                        rhs_scale=mix_s[:, g, n],
                        start=(g == 0),
                        stop=(g == FG - 1),
                    )
            for i, bank in zip(tiles, banks):
                staged[("out", i, lo)] = bank

        def out_store(tiles, lo, width, eng):
            n = slice(lo, lo + width)
            for i in tiles:
                bank = staged[("out", i, lo)]
                result = ring.tile([P, width], F32, name="result", tag="result", bufs=RESULT_BUFS)
                factor = rlen_cols[:, i : i + 1]
                if eng is nc.scalar:
                    nc.scalar.activation(out=result[:], in_=bank[:], func=ACT.Copy, scale=factor)
                else:
                    nc.vector.tensor_scalar(out=result[:], in0=bank[:], scalar1=factor, scalar2=None, op0=ALU.mult)
                nc.sync.dma_start(out=out[i * P : (i + 1) * P, n], in_=result[:])

        def out_banks(tiles, lo, width, eng):
            out_passes(tiles, lo, width)
            out_store(tiles, lo, width, eng)

        clear(dev_s_rest[:])
        warm_up_scalar()
        clear(boot_s[0][:])
        zeros = dev_s_rest[:].rearrange("p k n -> p (k n)").bitcast(BF16)
        for n in (slice(0, BANK // 2), slice(BANK // 2, BANK)):
            nc.vector.quantize_mx(out=zero_c[:, n].bitcast(FP8X4), scales=zero_s[:, n], in_=zeros)
        clear(dev_s_head[:])
        nc.vector.memset(base_raw[:].bitcast(I32), 0)
        clear(boot_s[1][:])

        load_scales(dev_s_first, dev_scales[:, :, 0:PASS])
        load_bytes(dev_w_raw[0][:], dev_view[:, 0])
        load_bytes(boot_w[0][:], boot_view[:, 0])
        load_scales(boot_s[0], boot_scales[:, :, 0:BANK])
        nc.sync.dma_start(
            out=base_raw[0:P:QUAD, :].rearrange("q (g c) -> q g c", g=FG),
            in_=base.rearrange("(g q c) -> q g c", g=FG, q=P // QUAD),
        )
        load_bytes(boot_w[1][:], boot_view[:, 1])
        load_scales(boot_s[1], boot_scales[:, :, BANK:M])
        load_bytes(dev_w_raw[1][:], dev_view[:, 1])
        load_scales(dev_s_rest, dev_scales[:, :, PASS:F])
        nc.sync.dma_start(out=expo_raw[0][:], in_=expo_view[0])
        nc.sync.dma_start(out=expo_raw[1][:], in_=expo_view[1])
        nc.sync.dma_start(out=sig_raw[0][:], in_=sig_view[:, 0])
        load_bytes(dev_w_raw[2][:], dev_view[:, 2])
        nc.sync.dma_start(out=sig_raw[1][:], in_=sig_view[:, 1])
        nc.sync.dma_start(out=sig_raw[2][:], in_=sig_view[:, 2])
        with nc.allow_non_contiguous_dma(reason="one value of rlen to a partition and output tile"):
            nc.sync.dma_start(out=rlen_raw[:], in_=rlen.rearrange("(i p) -> p i", p=P))

        warm_up_tensor(zero_c[:].bitcast(FP8X4))
        warm_up_tensor(zero_c[:].bitcast(FP8X4))
        for u in QUADRANTS:
            order_first_dev_scales(u)
        warm_up_tensor(dev_w_raw[0][:, 0, :].bitcast(FP4X4))
        warm_up_tensor(boot_w[0][:, 0, :].bitcast(FP4X4))
        order_dev_words(0)
        order_base()
        turn_base(0, P)

        turn_base(P, F // 4)
        nc.vector.memset(ident_f32[:], 0.0)
        make_identity(nc, ident_f32[:], nomemset=True)
        for t in range(PACK):
            cat_bank(0, 0, t, nc.vector if t == PACK - 1 else nc.scalar)
        cat_unit(1, 0)
        order_dev_words(1)
        order_dev(dev_s_tail[:], dev_s_rest[:], RUN // 4)
        cat_unit(0, 1)
        cat_weave(0, 0, BANK)
        expo_sort(0)
        expo_sort(1)
        cat_quant(0, 0, BANK)
        for h in range(2):
            for b in range(2):
                expo_bank(h, b, nc.scalar)
        sig_weave(0)
        cat_unit(1, 1)
        order_dev_words(2)
        sig_quant(0)
        sig_weave(1)
        cat_unit(0, 2)
        expo_quant(0)
        sig_quant(1)
        sig_weave(2)
        expo_quant(1)
        sig_quant(2)
        cat_weave_aside(1, "sig2")
        cat_weave_aside(2, "sig1")

        for t in range(PACK // 2):
            cat_bank(1, 2, t, nc.scalar)
        mix_banks(0, 2 * HALF_TILES, 0)
        for n in range(2 * HALF_TILES, FG * HALF_TILES):
            mix_bank(n, 0, nc.vector)
        for t in range(PACK // 2, PACK):
            cat_bank(1, 2, t, nc.scalar)
        nc.scalar.copy(out=rlen_cols[:], in_=rlen_raw[:])

        for n in range(2):
            mix_bank(n, 1, nc.vector)
        mix_quant(0, 0)
        mix_quant(1, 0)
        cat_quant_pair(1, 0)
        mix_quant(2, 0)
        cat_quant_pair(2, 0)
        cat_quant_pair(1, 1)
        cat_quant_pair(2, 1)
        for n in range(2, 10):
            mix_bank(n, 1, nc.scalar)
        for n in range(10, 12):
            mix_bank(n, 1, nc.vector)
        out_banks([0, 1], 0, BANK, nc.scalar)
        for g in range(FG):
            mix_quant(g, 1)
        for i in range(2, HALF_TILES):
            out_banks([i], 0, BANK, nc.scalar)
        for i in range(HALF_TILES, M_TILES):
            cat_piece(i, 1)
        out_banks([0, 1, 2], BANK, BANK, nc.scalar)
        out_banks([3], BANK, BANK, nc.scalar)
        for i in range(HALF_TILES, M_TILES - 2):
            for lo in range(0, R, BANK):
                out_banks([i], lo, BANK, nc.scalar)
        for i in range(M_TILES - 2, M_TILES):
            for q in range(R // SMALL_BANK):
                out_banks([i], q * SMALL_BANK, SMALL_BANK, in_turn[(q + 1) % 2])
